import numpy as np, ml_dtypes
CORES = [1,5,17,21,33,37,49,53]
N = 8
import mx_ref
BF = ml_dtypes.bfloat16
def entries(a):
    return np.ascontiguousarray(a.T).reshape(-1)
def table(e):
    return np.ascontiguousarray(np.reshape(e, (-1, 16)).T).astype(np.int32)
def gentries(a):
    return np.ascontiguousarray(a.reshape(8, 16, -1).transpose(0, 2, 1)).reshape(8, -1)
def gtable(e):
    e = np.asarray(e); return np.ascontiguousarray(e.reshape(8, -1, 16).transpose(0, 2, 1)).reshape(128, -1).astype(np.int32)
def gcols(t, e):
    v = np.concatenate([t.reshape(8, 16, -1, 4), np.zeros((8, 16, 1, 4), BF)], axis=2)
    return np.ascontiguousarray(np.stack([v[g][:, e[g]] for g in range(8)])).reshape(128, -1)
def tile(rs):
    return np.stack(rs, axis=2).reshape(128, -1).astype(BF)
def pick(q, e):
    c = np.concatenate([q[0].reshape(128, -1, 4), np.zeros((128, 1, 4), np.uint8)], axis=1); s = np.concatenate([q[1], np.ones((16, 1), np.uint8)], axis=1)
    return (np.ascontiguousarray(c[:, e].reshape(128, -1)), np.ascontiguousarray(s[:, e]))
def join(*qs):
    return (np.concatenate([q[0] for q in qs], axis=1), np.concatenate([q[1] for q in qs], axis=1))
def put(q, e, v):
    c, s = q[0].reshape(128, -1, 4).copy(), q[1].copy(); c[:, e] = v[0].reshape(128, -1, 4); s[:, e] = v[1]
    return (c.reshape(128, -1), s)
def pk(c, s):
    return (np.ascontiguousarray(c), mx_ref.live(s))
def emit(q):
    return q[0], q[1]
def packed(v, rng):
    q = [mx_ref.quantize(np.ascontiguousarray(v[r])) for r in range(N)]
    return np.stack([a for a, b in q]), np.stack([mx_ref.plane(b, rng) for a, b in q])
def values_of_codes():
    e, c = np.zeros((128, 128, 4), np.float32), np.zeros((128, 2, 4), np.uint8)
    e[np.arange(128), np.arange(128), 0] = 1
    c[:127, :, 0] = np.arange(256).reshape(2, 128).T[:127]
    return mx_ref.matmul(mx_ref.quantize(e.reshape(128, 512).astype(BF)), (c.reshape(128, 8), np.full((16, 2), 127, np.uint8))).T.reshape(-1).astype(np.float64)
CODE_VALUE, SCALE_VALUE = values_of_codes(), 2.0 ** (np.arange(256) - 127.0)
def decode(q):
    return (CODE_VALUE[q[0]].reshape(16, 8, -1, 4) * SCALE_VALUE[q[1]][:, None, :, None] + 0.0).reshape(128, -1).astype(np.float32)
def f(rng, *shape):
    return mx_ref.flush((rng.standard_normal(shape, dtype=np.float32) * np.exp2(rng.integers(-2, 3, shape[:-1] + (1,)))).astype(BF))
def wide(rng, *shape, cols=0):
    v = rng.standard_normal(shape, dtype=np.float32) * np.exp2(rng.integers(-12, 13, shape)).astype(np.float32)
    if cols: v *= np.repeat(np.exp2(rng.integers(-cols, cols + 1, shape[:-2] + (1, shape[-1] // 4))) * (rng.random(shape[:-2] + (1, shape[-1] // 4)) > 0.0625), 4, axis=-1).astype(np.float32)
    return mx_ref.flush(v.astype(BF))
C, L, M, CAP, E = 384, 3, 128, 48, 896
def pairs_of(e, lev):
    r, s = np.arange(N * C) // C, e // C
    return np.where((e < 0) | (s == r), -1, ((np.arange(8)[:, None] * L + lev) * N + r) * N + s)
def big(v):
    v = v.astype(np.float32)
    v[np.abs(v) < np.float32(2.0 ** -16)] = 0
    return v.astype(BF)
def levels(rng):
    return np.concatenate([rng.permutation(np.arange(C) // M) for r in range(N)])
def drawn(rng, lev, far=()):
    e = np.full((2, 8, N * C), -1)
    for k in range(2):
        for g in range(8):
            free = np.ones(N * C, bool)
            deep = g in far
            for l in range(L - 1 if deep else 1, L):
                a = rng.permutation(np.flatnonzero((lev < (1 if deep else l)) & free))[:E]
                e[k, g, rng.permutation(np.flatnonzero(lev == l))[:E]] = a
                free[a] = False
    return e
def fit(rng, e, lev):
    k = pairs_of(e, lev).reshape(-1)
    o = rng.permutation(k.size)
    o = o[np.argsort(k[o], kind="stable")]
    k = k[o]
    v = e.reshape(-1).copy()
    v[o[(k >= 0) & (np.arange(k.size) - np.searchsorted(k, k) >= CAP)]] = -1
    return v.reshape(e.shape)
def inputs(rng, x, e, lev, w, v):
    wc, ws = packed(w, rng)
    vc, vs = packed(v, rng)
    d = {"x": x, "lv": np.stack([table(a) for a in lev.reshape(N, C)])}
    for k in range(2): d["pr%d" % k] = np.stack([gtable(e[k][:, C * r:C * r + C]) for r in range(N)])
    return {**d, "u": np.array(f(rng, N, 128, 512)), "wc": wc, "ws": ws, "vc": vc, "vs": vs}
def still(k=32):
    w = np.zeros((N, 128, 4, 128, 4), np.float32)
    i = np.arange(128)
    for b in range(4): w[:, i, b, i, b] = k
    return w.reshape(N, 128, 2048).astype(BF)
def setup_inputs(rng):
    lev = levels(rng)
    return inputs(rng, big(f(rng, N, 128, 4 * C)), fit(rng, drawn(rng, lev), lev), lev, f(rng, N, 128, 2048), f(rng, N, 128, 2048))
def setup_inputs_same(rng):
    lev = levels(rng)
    o, p = rng.permutation(8), rng.permutation(N)
    e = drawn(rng, lev, o[[3, 7]])
    e[1, o[:4]] = e[0, o[:4]]
    e[0, o[4]] = -1
    e[1, o[5]] = -1
    e[:, o[6]] = -1
    e[:, :, C * p[0]:C * p[0] + C] = -1
    e[e // C == p[1]] = -1
    return inputs(rng, big(f(rng, N, 128, 4 * C)), fit(rng, e, lev), lev, f(rng, N, 128, 2048), f(rng, N, 128, 2048))
def setup_inputs_full(rng):
    lev = levels(rng)
    v, e = lev.reshape(N, C), np.full((2, 8, N * C), -1)
    o, n = rng.permutation(N), N - 1
    m = min(n - 1, 2 * (M // CAP))
    some = rng.permutation(8)
    far, near = some[:2], some[2:4]
    for g in range(8):
        flip, deep = int(rng.integers(2)), g in far
        for k in range(2):
            free = np.ones((N, C), bool)
            for l in range(L - 1 if deep else 1, L):
                may = v == 1 if g in near and l == L - 1 else v < (1 if deep else l)
                pool = [rng.permutation(np.flatnonzero(may[s] & free[s])) for s in range(N)]
                for i in range(N):
                    r, p = o[i], 0
                    to = C * r + rng.permutation(np.flatnonzero(v[r] == l))
                    want = [(o[(i + 1 + a) % n], CAP) for a in range(m) if (a + k + flip) % 2 == 0] if i < n else []
                    rest = M - CAP * len(want)
                    want.append((r, rest if l == L - 1 else rest // 2))
                    for s, c in want:
                        a, pool[s] = pool[s][:c], pool[s][c:]
                        e[k, g, to[p:p + c]] = C * s + a
                        free[s, a] = False
                        p += c
    return inputs(rng, big(f(rng, N, 128, 4 * C)), e, lev, f(rng, N, 128, 2048), f(rng, N, 128, 2048))
def setup_inputs_cancel(rng):
    lev = levels(rng)
    e, x = np.full((2, 8, N * C), -1), np.zeros((8, 16, N * C, 4))
    large = rng.permutation(8) % 2
    for g in range(8):
        v = rng.integers(4, 8, (16, N * C, 4)) * rng.choice([-1.0, 1.0], (16, N * C, 4)) * 2.0 ** -16
        half = []
        for l in range(L):
            p = rng.permutation(np.flatnonzero(lev == l)).reshape(2, -1)
            v[:, p[1]] = -v[:, p[0]]
            if l % 2 == large[g]: v[:, p] = v[:, p] * 2.0 ** 28
            half.append(p[:, :E // 2])
        for l in range(1, L):
            e[0, g, half[l]] = half[l - 1]
            e[1, g, half[l]] = half[l - 1][::-1]
        x[g] = v
    x = np.ascontiguousarray(x.reshape(128, N, 4 * C).transpose(1, 0, 2)).astype(np.float32).astype(BF)
    return inputs(rng, x, fit(rng, e, lev), lev, still(), still())
def setup_inputs_crowd(rng):
    lev = levels(rng)
    e, x = np.full((2, 8, N * C), -1), np.zeros((8, 16, N * C, 4))
    by, h, some = lev.reshape(N, C), CAP // 2, rng.permutation(8)
    for g in range(8):
        v = rng.integers(1, 32, (16, N * C, 4)) * rng.choice([-1.0, 1.0], (16, N * C, 4)) * 2.0 ** -13
        half = [rng.permutation(np.flatnonzero(lev == l)).reshape(2, -1) for l in range(L)]
        v[::8, half[0][0], 0] = 28
        v[::8, half[0][1], 0] = -28
        x[g] = v
        if g in some[L:]:
            for l in range(1, L):
                e[0, g, half[l][:, :E // 2]] = half[l - 1][:, :E // 2]
                e[1, g, half[l][:, :E // 2]] = half[l - 1][::-1, :E // 2]
            continue
        p = rng.permutation(N)
        for k in range(2):
            free = np.ones((N, C), bool)
            for l in range(1, L):
                if g == some[0]:
                    to = C * p[0] + rng.permutation(np.flatnonzero(by[p[0]] == l))
                    for j in range(N - 1):
                        s, t = p[j + 1], to[h * j:h * j + h]
                        a = rng.permutation(np.flatnonzero((by[s] < l) & free[s]))[:t.size]
                        e[k, g, t] = C * s + a
                        free[s, a] = False
                elif g == some[l]:
                    a = C * p[0] + rng.permutation(np.flatnonzero(by[p[0]] < l))
                    for j in range(N - 1):
                        r, t = p[j + 1], a[h * j:h * j + h]
                        e[k, g, C * r + rng.permutation(np.flatnonzero(by[r] == l))[:t.size]] = t
    x = np.ascontiguousarray(x.reshape(128, N, 4 * C).transpose(1, 0, 2)).astype(np.float32).astype(BF)
    return inputs(rng, x, fit(rng, e, lev), lev, still(36), still())
def setup_inputs_spread(rng):
    d = setup_inputs(rng)
    d["x"] = big(wide(rng, N, 128, 4 * C, cols=6))
    return d
def check_inputs(d):
    b = []
    for k in ("x", "u"):
        a = np.abs(d[k].astype(np.float32))
        if not (np.isfinite(a).all() and ((a == 0) | (a >= 2.0 ** -30) & (a <= 2.0 ** 30)).all()): b.append("a value of " + k)
    lev = np.concatenate([entries(a) for a in d["lv"]])
    if not all((np.sum(lev.reshape(N, C) == l, axis=1) == M).all() for l in range(L)): b.append("a number of columns of a level")
    e = np.stack([np.concatenate([gentries(a) for a in d[k]], axis=1) for k in ("pr0", "pr1")]).astype(np.int64)
    ok = (e >= -1) & (e < N * C)
    if not ok.all(): b.append("an entry out of range")
    e = np.where(ok, e, -1)
    if ((e >= 0) & (lev[np.maximum(e, 0)] >= lev)).any(): b.append("a predecessor that isn't of a lower level")
    s = np.sort(e, axis=2)
    if ((s[:, :, 1:] == s[:, :, :-1]) & (s[:, :, 1:] >= 0)).any(): b.append("a number twice in a list of a group")
    if np.bincount(pairs_of(e, np.clip(lev, 0, L - 1)).reshape(-1) + 1)[1:].max(initial=0) > CAP: b.append("too many entries of two ranks in a group and a level")
    return b
def sweep(base, links, lev, steps, layer):
    got = np.zeros((128, 4 * N * C), BF)
    kept, order = [], []
    for l in steps:
        at = np.flatnonzero(lev == l)
        a, b = [gcols(got, e[:, at]).astype(np.float32) for e in links]
        t = (base.reshape(128, -1, 4)[:, at].reshape(128, -1) - (a + b) * np.float32(0.5)).astype(BF)
        q = mx_ref.quantize(np.ascontiguousarray(t))
        made = []
        for r in range(N):
            mine = pick(q, np.arange(M * r, M * r + M))
            made.append(tile([mx_ref.matmul(pick(layer[r], np.arange(128 * i, 128 * i + 128)), mine) * np.float32(0.03125) for i in range(4)]))
        z = mx_ref.quantize(np.ascontiguousarray(np.concatenate(made, axis=1)))
        got.reshape(128, -1, 4)[:, at] = decode(z).astype(BF).reshape(128, -1, 4)
        kept.append(z)
        order.append(at)
    return pick(join(*kept), np.argsort(np.concatenate(order))), got
def reference(x, lv, pr0, pr1, u, wc, ws, vc, vs):
    lev = np.concatenate([entries(lv[r]) for r in range(N)])
    pr = [np.concatenate([gentries(a[r]) for r in range(N)], axis=1) for a in (pr0, pr1)]
    su = []
    for e in pr:
        i = np.full((8, N * C + 1), -1)
        i[np.arange(8)[:, None], e] = np.arange(N * C)
        su.append(i[:, :N * C])
    first = decode(mx_ref.quantize(np.ascontiguousarray(np.concatenate([x[r] for r in range(N)], axis=1))))
    qy, dy = sweep(first, pr, lev, range(L), [pk(wc[r], ws[r]) for r in range(N)])
    qz, dz = sweep(dy.astype(np.float32), su, lev, range(L - 1, -1, -1), [pk(vc[r], vs[r]) for r in range(N)])
    y = np.zeros((N, 128, C), np.float32)
    oc, osc = np.zeros((N, 128, 4 * C), np.uint8), np.zeros((N, 16, C), np.uint8)
    for r in range(N):
        mine = pick(qz, np.arange(C * r, C * r + C))
        y[r] = mx_ref.matmul(mx_ref.quantize(u[r]), mine)
        oc[r], osc[r] = emit(mine)
    return {"y": y, "oc": oc, "osc": osc}

@@ -1,0 +1,660 @@
+from concourse.bass import DstId, RemoteDMATransfer
+from concourse.mybir import dt, AluOpType as Op, ActivationFunctionType as Act
+
+N, C, M, CAP, NP = 8, 384, 128, 48, 7
+SL = CAP * NP
+CHUNK = True
+F32, BF, I32, U16, Q4, U8 = "float32", "bfloat16", "int32", "uint16", "float8_e4m3fn_x4", "uint8"
+FY, FZ, FL2, FW = NP * M, NP * M + 2 * M, NP * M + 3 * M, NP * M + 3 * M + SL
+BZ, BL3, BL4, BW = 384, 512, 512 + SL, 512 + 2 * SL
+NE, NS = 2 * C, 2 * SL
+SEG, LSEG = 17, 25
+UM = 1 + N * C
+RK = 1024
+SU0 = NE + NS + SL
+WIDE = {1: M, 2: CAP, 3: CAP, 4: CAP}
+LAND = {1: ("wf", 0), 2: ("wf", FL2), 3: ("wb", BL3), 4: ("wb", BL4)}
+
+
+def _sb(n, d):
+    return ("sbuf", [128, n], d)
+
+
+SMALL = {}
+for _n in ("tot", "tt", "ts", "tb", "rt", "kc", "kt", "pos", "nt0", "nt", "a1", "a2", "a3", "a4", "a5"):
+    SMALL[_n] = (32 * len(SMALL), 32 if len(SMALL) < 7 else 24)
+
+SCRATCH = {
+    "sm": _sb(32 * len(SMALL), F32), "e": _sb(48, I32), "lvt": _sb(24, I32), "iot": _sb(C, F32),
+    "ew": _sb(UM, F32), "eexp": _sb(NE, F32), "es": _sb(512, F32), "vi": _sb(16, I32), "si": _sb(32, I32), "ci": _sb(32, I32),
+    "oh": _sb(NP * SEG, F32), "rs": _sb(NP * SEG, F32), "c1": _sb(NP * SEG, F32), "c2": _sb(NP * SEG, F32),
+    "prod": _sb(128, F32), "rp": _sb(128, F32), "pm": _sb(256, F32),
+    "loh": _sb(3 * LSEG, F32), "lrs": _sb(3 * LSEG, F32), "lc1": _sb(3 * LSEG, F32), "lc2": _sb(3 * LSEG, F32),
+    "ou": _sb(32, U16), "pp": _sb(NE, F32), "posu": _sb(24, U16), "pin": _sb(24 * NP, U16), "pc": _sb(4, I32), "pf": _sb(8, F32),
+    "nm": _sb(C, BF), "ma": _sb(C, BF), "mask": _sb(C, BF), "r16": _sb(C, BF),
+    "rw": _sb(NE + NS, F32), "m1": _sb(C, F32), "m2": _sb(C, F32),
+    "req1": _sb(24, F32), "req2": _sb(24, F32), "rin1": _sb(24, F32), "rin2": _sb(24, F32), "hr1": _sb(6, F32), "hr2": _sb(6, F32),
+    "c2u": _sb(22, U16), "g2": _sb(22, U16), "h1": _sb(22, U16), "h2": _sb(22, U16),
+    "pw": _sb(C, F32), "permu": _sb(24, U16), "pd": _sb(96, U16), "pn": _sb(32, U16),
+    "u1": _sb(48, U16), "u2": _sb(32, U16), "o2u": _sb(16, U16), "uw": _sb(UM + SL, F32), "uexp": _sb(NE, F32),
+    "gx": _sb(512, F32), "gt": _sb(512, F32), "f1": _sb(32, U16), "f2": _sb(32, U16), "b1": _sb(32, U16), "b0": _sb(32, U16),
+    "pl": _sb(512, F32), "w2": _sb(SU0 + NE, F32), "sud": _sb(NS, F32), "suu": _sb(22, U16),
+    "ones": _sb(128, BF), "ident": _sb(128, BF), "et": _sb(2048, BF), "zt": _sb(512, BF), "pe": _sb(2, F32),
+    "e1q": _sb(512, Q4), "e1s": _sb(512, U8), "eeq": _sb(512, Q4), "ees": _sb(512, U8), "eoq": _sb(512, Q4), "eos": _sb(512, U8),
+    "xt": _sb(4 * C, BF), "ut": _sb(512, BF), "sq": _sb(C, Q4), "ss": _sb(C, U8), "uq": _sb(128, Q4), "us": _sb(128, U8),
+    "wq": _sb(512, Q4), "wp": _sb(512, U8), "vq": _sb(512, Q4), "vp": _sb(512, U8), "yp": _sb(4 * 256, BF),
+    "wfq": _sb(FW, Q4), "wfs": _sb(FW, U8), "wbq": _sb(BW, Q4), "wbs": _sb(BW, U8),
+    "spq": _sb(C, Q4), "sps": _sb(C, U8), "ds": _sb(1024, BF), "dy": _sb(1024, BF),
+    "xs": _sb(7 * 512, BF), "xq": _sb(7 * 128, Q4), "xp": _sb(7 * 128, U8), "ti": _sb(5 * 512, BF), "zp": _sb(1024, BF),
+    "st": _sb(3 * 4 * SL, BF), "oq": _sb(C, Q4), "opl": _sb(C, U8), "yo": _sb(C, F32),
+    "PA": ("psum", [128, 2048], F32), "PB": ("psum", [128, 2048], F32),
+}
+for _k in range(1, 5):
+    SCRATCH["pk%d" % _k] = _sb(512, Q4)
+    SCRATCH["ps%d" % _k] = _sb(512, U8)
+    SCRATCH["sdq%d" % _k] = _sb(M if _k == 1 else SL, Q4)
+    SCRATCH["sds%d" % _k] = _sb(M if _k == 1 else SL, U8)
+    SCRATCH["hs%d" % _k] = _sb(M if _k == 1 else 2 * CAP, U8)
+SEMAPHORES = ["q_v", "q_s", "q_t", "q_g", "sent", "ld_l", "ld_e", "ld_x", "ld_w", "ld_v", "ld_u", "st_c", "st_s", "st_y",
+              "ar_pa", "ar_pb", "ar_pc", "ar_r1", "ar_r2", "ar_hr1", "ar_hr2"] + \
+    ["ar_c%d" % k for k in range(1, 5)] + ["ar_s%d" % k for k in range(1, 5)] + ["ar_h%d" % k for k in range(1, 5)]
+
+
+def peers_of(T, topo, r):
+    n = len(T.cores)
+    mine = topo.chip(T.cores[r])
+    far = [(r + i) % n for i in range(1, n) if topo.chip(T.cores[(r + i) % n]) != mine]
+    chips = []
+    for s in far:
+        if topo.chip(T.cores[s]) not in chips:
+            chips.append(topo.chip(T.cores[s]))
+    out = [s for ch in chips for s in sorted(far) if topo.chip(T.cores[s]) == ch]
+    return out + [s for s in range(n) if s != r and topo.chip(T.cores[s]) == mine]
+
+
+def helpers_of(T, topo, r):
+    core = T.cores[r]
+    return [c for c in topo.cores_of(core) if topo.die(c) == topo.die(core) and T.rank_of(c) is None][:3]
+
+
+def bits(es):
+    return sum(1 << e for e in es)
+
+
+def parts(es, n):
+    k = len(es) // n
+    return [es[k * i:k * i + k] for i in range(n)]
+
+
+def engine_sets(T, topo, r):
+    ps = peers_of(T, topo, r)
+    core = T.cores[r]
+    off = topo.engines(core, T.cores[ps[0]])
+    return off, [e for e in topo.engines(core, T.cores[ps[-1]]) if e not in off]
+
+
+def spread(T, topo, r, k=1):
+    off, rest = engine_sets(T, topo, r)
+    one, two, near = list(enumerate(parts(off, 4))), [(4 + i, es) for i, es in enumerate(parts(off, 2))], [(NP - 1, rest)]
+    return (one, two + near) if CHUNK and k > 1 else (one + near, two)
+
+
+def helper_engines(T, topo, r, k):
+    off, rest = engine_sets(T, topo, r)
+    return parts(rest, 2) + [rest if CHUNK and k > 1 else off]
+
+
+def arrivals(T, topo, r):
+    direct, planes, tables = [], 0, 0
+    for s in peers_of(T, topo, r):
+        i = peers_of(T, topo, s).index(r)
+        one, two = spread(T, topo, s)
+        n = [len(es) for j, es in one + two if j == i][0]
+        direct.append((i, n))
+        if i < NP - 1:
+            far = len(topo.engines(helpers_of(T, topo, s)[i // 2], T.cores[r])) // 2
+            planes += far
+            tables += far
+        else:
+            planes += n
+            tables += n // 4
+    return direct, planes, tables
+
+
+def dst(topo, c):
+    a = topo.addr(c)
+    return DstId(rid=a[0], pnc=a[1])
+
+
+def helper_program(g, core, T, topo, r, h):
+    ps = peers_of(T, topo, r)
+    sent = 0
+    for kind, k in (("s", 1), ("r", 2), ("s", 2), ("s", 3), ("r", 1), ("s", 4)):
+        if kind == "s":
+            (name, base), w = LAND[k], WIDE[k]
+            here, there, sem, step = "hs%d" % k, name + "s", "ar_s%d" % k, 0 if k == 1 else w
+            g.wait_ge(T.sem["ar_h%d" % k], len(helper_engines(T, topo, r, k)[h]))
+        else:
+            base, w = 0, 3
+            here, there, sem, step = "hr%d" % k, "rin%d" % k, "ar_r%d" % k, w
+            g.wait_ge(T.sem["ar_hr%d" % k], len(engine_sets(T, topo, r)[1]) // 4)
+        tr = []
+        for j in range(2):
+            d = ps[2 * h + j]
+            es = parts(topo.engines(core, T.cores[d]), 2)[j]
+            at = base + w * peers_of(T, topo, d).index(r)
+            tr.append(RemoteDMATransfer(dst_ids=[dst(topo, T.cores[d])], dma_engine_mask=bits(es), remote_sem=T.sem[sem],
+                                        src=T[here][:, step * j:step * j + w], dst=T[there][:, at:at + w]))
+            sent += len(es)
+        g.remote_dma_fused(tr, local_sem=T.sem.sent)
+    g.wait_ge(T.sem.sent, sent)
+
+
+def rank_program(g, core, T, topo):
+    r = T.rank_of(core)
+    if r is None:
+        for s in range(len(T.cores)):
+            hs = helpers_of(T, topo, s)
+            if core in hs:
+                helper_program(g, core, T, topo, s, hs.index(core))
+        return
+    ps = peers_of(T, topo, r)
+    hs = helpers_of(T, topo, r)
+    Q = {"v": g.vector, "s": g.scalar, "t": g.tensor, "g": g, "y": g.sync}
+    cnt = {"v": 0, "s": 0, "t": 0, "g": 0}
+    seen = {k: {} for k in Q}
+    log = {}
+    total = {}
+    sent = [0]
+
+    def A(name, a=0, b=None, step=1):
+        if name in SMALL:
+            at, n = SMALL[name]
+            return ("sm", at + a, at + (n if b is None else b), step)
+        return (name, a, SCRATCH[name][1][1] if b is None else b, step)
+
+    def ap(v):
+        return T[v[0]][:, v[1]:v[2]] if v[3] == 1 else T[v[0]][:, v[1]:v[2]:v[3]]
+
+    def meet(u, v):
+        if u[0][0] == "P":
+            return u[1] // 512 <= (v[2] - 1) // 512 and v[1] // 512 <= (u[2] - 1) // 512
+        if u[1] >= v[2] or v[1] >= u[2]:
+            return False
+        return not (u[3] == v[3] and u[3] > 1 and (u[1] - v[1]) % u[3])
+
+    def before(q, reads, writes):
+        w = {}
+        for v, wr in [(v, False) for v in reads] + [(v, True) for v in writes]:
+            for u, uw, uq, sem, val in log.get(v[0], []):
+                psum = v[0][0] == "P"
+                if psum and uq == q:
+                    continue
+                if (uw or wr or psum) and meet(u, v):
+                    w[sem] = max(w.get(sem, 0), val)
+        for sem, val in w.items():
+            if seen[q].get(sem, 0) < val:
+                Q[q].wait_ge(T.sem[sem], val)
+                seen[q][sem] = val
+
+    def note(q, reads, writes, sem, val):
+        for v, wr in [(v, False) for v in reads] + [(v, True) for v in writes]:
+            log.setdefault(v[0], []).append((v, wr, q, sem, val))
+        total[sem] = max(total.get(sem, 0), val)
+
+    def run(q, reads, writes, call):
+        before(q, reads, writes)
+        cnt[q] += 1
+        call().then_inc(T.sem["q_" + q], 1)
+        note(q, reads, writes, "q_" + q, cnt[q])
+
+    def col(x):
+        return ([x], ap(x)) if isinstance(x, tuple) else ([], x)
+
+    def src(v, off):
+        return ap(v) if off is None else ap(v).indirect(ap(off))
+
+    def cp(o, i, off=None):
+        run("v", [i] + ([off] if off else []), [o], lambda: g.vector.tensor_copy(ap(o), src(i, off)))
+
+    def scat(o, off, i):
+        run("v", [i, off], [o], lambda: g.vector.tensor_copy(ap(o).indirect(ap(off)), ap(i)))
+
+    def tt(o, a, b, op, off=None):
+        run("v", [a, b] + ([off] if off else []), [o], lambda: g.vector.tensor_tensor(ap(o), src(a, off), ap(b), op))
+
+    def ts(o, a, s1, op0, s2=None, op1=None):
+        r1, x1 = col(s1)
+        if op1 is None:
+            run("v", [a] + r1, [o], lambda: g.vector.tensor_scalar(ap(o), ap(a), x1, None, op0))
+        else:
+            run("v", [a] + r1, [o], lambda: g.vector.tensor_scalar(ap(o), ap(a), x1, s2, op0, op1))
+
+    def scan(o, reset, d, op1=Op.add):
+        run("v", [reset, d], [o], lambda: g.vector.tensor_tensor_scan(ap(o), ap(reset), ap(d), 0.0, Op.mult, op1))
+
+    def trn(o, i):
+        run("v", [i], [o], lambda: g.vector.transpose(ap(o), ap(i)))
+
+    def fill(o, x):
+        run("v", [], [o], lambda: g.vector.memset(ap(o), x))
+
+    def act(o, i, f=Act.Copy, off=None, bias=None, scale=None):
+        kw, rd = {}, [i] + ([off] if off else [])
+        for k, x in (("bias", bias), ("scale", scale)):
+            if x is not None:
+                rr, kw[k] = col(x)
+                rd = rd + rr
+        run("s", rd, [o], lambda: g.scalar.activation(ap(o), src(i, off), f, **kw))
+
+    def iota(o, pat, base, cm=0):
+        if SCRATCH[o[0]][2] == I32:
+            run("g", [], [o], lambda: g.iota(ap(o), pat, base, cm))
+        else:
+            run("g", [], [o], lambda: g.iota(ap(o), pat, base, cm, allow_small_or_imprecise_dtypes=True))
+
+    def quant(qn, sn, a, n, i):
+        o, s = A(qn, a, a + n), A(sn, a, a + n)
+        run("v", [i], [o, s], lambda: g.vector.quantize_mx(ap(o), ap(s), ap(i)))
+
+    def mm(o, wn, wsn, a, xn, xsn, b, n, start=True, stop=True):
+        w, ws, x, xs = A(wn, a, a + 128), A(wsn, a, a + 128), A(xn, b, b + n), A(xsn, b, b + n)
+        run("t", [w, ws, x, xs], [o], lambda: g.tensor.matmul_mx(ap(o), ap(w), ap(ws), ap(x), ap(xs), start, stop))
+
+    def pick(qo, so, a, qi, si, wlen, off):
+        n = 16 * (off[2] - off[1])
+        o, i = A(qo, a, a + n), A(qi, 0, wlen)
+        run("v", [i, off], [o], lambda: g.vector.tensor_copy(ap(o).bitcast(dt.uint32), ap(i).bitcast(dt.uint32).indirect(ap(off))))
+        act(A(so, a, a + n), A(si, 0, wlen), off=off)
+
+    def dmas(sem, items):
+        for q, o, i, rd, wr in items:
+            before(q, rd, wr)
+            Q[q].dma_start(o, i).then_inc(T.sem[sem], 16)
+        for q, o, i, rd, wr in items:
+            note(q, rd, wr, sem, 16 * len(items))
+
+    def u8(v):
+        return ap(v).bitcast(dt.uint8)
+
+    def call(items):
+        g.remote_dma_fused([RemoteDMATransfer(dst_ids=[dst(topo, c)], dma_engine_mask=bits(es), remote_sem=T.sem[sem], src=s, dst=d)
+                            for c, es, sem, s, d in items], local_sem=T.sem.sent)
+        sent[0] += sum(len(p[1]) for p in items)
+
+    def back(i):
+        return peers_of(T, topo, ps[i]).index(r)
+
+    direct, n_planes, n_tables = arrivals(T, topo, r)
+    n_direct = sum(n for i, n in direct)
+    rest = engine_sets(T, topo, r)[1]
+
+    def exchange(k, piece=None):
+        name, base = LAND[k]
+        w = WIDE[k]
+        step = 0 if k == 1 else w
+        qn, sn = "sdq%d" % k, "sds%d" % k
+        one, two = spread(T, topo, r, k)
+        he = helper_engines(T, topo, r, k)
+        hw = SCRATCH["hs%d" % k][1][1]
+
+        def codes(part):
+            call([(T.cores[ps[i]], es, "ar_c%d" % k, u8(A(qn, step * i, step * i + w)),
+                   u8(A(name + "q", base + w * back(i), base + w * back(i) + w))) for i, es in part])
+
+        def relay(which):
+            call([(hs[h], he[h], "ar_h%d" % k, ap(A(sn, 2 * step * h, 2 * step * h + hw)), ap(A("hs%d" % k))) for h in which])
+        a, b = {None: (0, None), 0: (0, 4 * w), 1: (4 * w, None)}[piece]
+        before("g", [A(qn, a, b), A(sn, a, b)], [])
+        relay({None: (0, 1, 2), 0: (0, 1), 1: (2,)}[piece])
+        if piece != 1:
+            codes(one)
+        if piece == 0:
+            return
+        codes(two)
+        i = NP - 1
+        call([(T.cores[ps[i]], rest, "ar_s%d" % k, ap(A(sn, step * i, step * i + w)),
+               ap(A(name + "s", base + w * back(i), base + w * back(i) + w)))])
+        note("x", [], [A(name + "q", base, base + NP * w)], "ar_c%d" % k, n_direct)
+        note("x", [], [A(name + "s", base, base + NP * w)], "ar_s%d" % k, n_planes)
+
+    def bank(p, b, n):
+        return A(p, 512 * b, 512 * b + n)
+
+    def scaled(q, o, i):
+        if q == "v":
+            ts(o, i, 0.03125, Op.mult)
+        else:
+            act(o, i, scale=0.03125)
+
+    def plain(q, o, i, off=None):
+        if q == "v":
+            cp(o, i, off)
+        else:
+            act(o, i, off=off)
+
+    def to_table(w, n):
+        tt(A("m1", 0, n), w, A("mask", 0, n), Op.mult)
+        scan(A("m2", 0, n), A("r16", 0, n), A("m1", 0, n))
+        return A("m2", 15, n, 16)
+
+    def across(n, k0):
+        trn(A("tt"), A("tot"))
+        tt(A("kt", 0, n), A("kc", k0, k0 + n), A("tot", 0, n), Op.subtract)
+        scan(A("ts"), A("rt"), A("tt"))
+        trn(A("tb"), A("ts"))
+
+    def spread_lists(win, level):
+        for k in range(2):
+            act(A("gx", 256 * k, 256 * k + 256), win, off=A("pd", 48 * k + 16 * level, 48 * k + 16 * level + 16))
+
+    def pair_lists(out):
+        trn(A("gt"), A("gx"))
+        cp(A(out, 0, 16), A("gt", 0, 512, 32))
+        cp(A(out, 16, 32), A("gt", 16, 512, 32))
+
+    def gathered(k, name, wlen, lists, dn, d0, dw, slot, pause=None):
+        pq, pp = "pk%d" % k, "ps%d" % k
+        for a, b in ((0, 8), (8, 16), (16, 32)):
+            pick(pq, pp, 16 * a, name + "q", name + "s", wlen, A(lists, a, b))
+        for h in range(2):
+            for b in range(4):
+                mm(bank("PA", b, M), "eeq", "ees", 128 * b, pq, pp, 128 * h, M, h == 0, False)
+        if pause:
+            pause()
+        for b in range(4):
+            mm(bank("PA", b, M), "eoq", "eos", 128 * b, pq, pp, 256, M, False, False)
+            mm(bank("PA", b, M), "eoq", "eos", 128 * b, pq, pp, 384, M, False, True)
+            tt(A("xs", 512 * slot + b, 512 * slot + 512, 4), bank("PA", b, M), A(dn, dw * b + d0, dw * b + d0 + M), Op.add)
+        quant("xq", "xp", 128 * slot, M, A("xs", 512 * slot, 512 * slot + 512))
+
+    def layer(wn, wsn, slot, out):
+        for b in range(4):
+            mm(bank("PB", b, M), wn, wsn, 128 * b, "xq", "xp", 128 * slot, M)
+        return [lambda b=b: scaled("vs"[b % 2], out(b), bank("PB", b, M)) for b in range(4)]
+
+    def send(k, evac, win, lists):
+        at = 4 * SL * (k - 2)
+        for piece, (a, z) in ((0, (0, 12)), (1, (12, 21))) if CHUNK else ((None, (0, 21)),):
+            for b in range(4):
+                if piece != 1:
+                    evac[b]()
+                plain("vs"[b % 2], A("st", at + 64 * a + b, at + 64 * z, 4), win(b), A(lists, a, z))
+            quant("sdq%d" % k, "sds%d" % k, 16 * a, 16 * (z - a), A("st", at + 64 * a, at + 64 * z))
+            exchange(k, piece)
+
+    def decode(qn, sn, a, n, out, engines="ssss"):
+        for b in range(4):
+            mm(bank("PA", b, n), "e1q", "e1s", 128 * b, qn, sn, a, n)
+        for b in range(4):
+            plain(engines[b], out(b), bank("PA", b, n))
+
+    def diagonal(scale):
+        for b in range(4):
+            act(A("et", 512 * b + b, 512 * b + 512, 4), A("ident"), scale=scale)
+
+    def tile(name, i):
+        return lambda b: A(name, 512 * i + b, 512 * i + 512, 4)
+
+    def level(l):
+        a = 2 - l
+        return A("es", 256 * a, 256 * a + 256), A("si", 16 * a, 16 * a + 16), A("ci", 16 * a, 16 * a + 16), A("pm", 128 * a + 7, 128 * a + 128, 8)
+
+    def sort_entries(l):
+        a = 2 - l
+        for k in range(2):
+            act(A("es", 256 * a + M * k, 256 * a + M * k + M), A("eexp"), Act.Identity, off=A("pn", 16 * a + 8 * k, 16 * a + 8 * k + 8),
+                bias=float(C * k + 1))
+
+    def slots(l):
+        es, si, ci, O = level(l)
+        a = 2 - l
+        cp(A("vi"), to_table(es, 256))
+        fill(A("oh", 0, None, SEG), 0.0)
+        ts(si, A("vi"), 10, Op.arith_shift_right)
+        ts(ci, A("vi"), RK - 1, Op.bitwise_and)
+        for i in range(NP):
+            ts(A("oh", SEG * i + 1, SEG * i + SEG), si, float(ps[i] + 1), Op.is_equal)
+        scan(A("c1"), A("rs"), A("oh"))
+        cp(A("tot", 0, NP), A("c1", SEG - 1, None, SEG))
+        across(NP, NP * a)
+        tt(A("oh", 0, None, SEG), A("tb", 0, NP), A("kt", 0, NP), Op.add)
+        scan(A("c2"), A("rs"), A("oh"))
+        for i in range(NP):
+            tt(A("prod", i, None, 8), A("oh", SEG * i + 1, SEG * i + SEG), A("c2", SEG * i + 1, SEG * i + SEG), Op.mult)
+        scan(A("pm", 128 * a, 128 * a + 128), A("rp"), A("prod"), Op.max)
+        cp(A("ou", 16 * a, 16 * a + 16), O)
+
+    def fill_slots(l):
+        scat(A("rw"), A("ou", 16 * (2 - l), 16 * (3 - l)), level(l)[0])
+
+    def tables(l):
+        a, b, at = "req%d" % l, "rin%d" % l, NE + SL * (2 - l)
+        cp(A(a, 0, 21), to_table(A("rw", at, at + SL), SL))
+        before("g", [A(a)], [])
+        es = parts(rest, 4)
+        call([(hs[h], es[h], "ar_hr%d" % l, ap(A(a, 6 * h, 6 * h + 6)), ap(A("hr%d" % l))) for h in range(3)] +
+             [(T.cores[ps[-1]], es[3], "ar_r%d" % l, ap(A(a, 18, 24)), ap(A(b, 18, 24)))])
+        note("x", [], [A(b)], "ar_r%d" % l, n_tables)
+
+    def senders(l):
+        es, si, ci, O = level(l)
+        a = 2 - l
+
+        def w(n):
+            return A(n, 0, 16)
+        tt(w("a2"), ci, w("nt"), Op.subtract)
+        ts(w("a3"), si, float(r + 1), Op.is_equal)
+        ts(w("a2"), w("a2"), float(SU0 - 1), Op.add)
+        tt(w("a2"), w("a2"), w("a3"), Op.mult)
+        tt(w("a2"), w("a2"), O, Op.add)
+        cp(A("o2u"), w("a2"))
+        scat(A("w2"), A("o2u"), A("pl", 256 * a, 256 * a + 256))
+        ts(A("h%d" % l, 0, 21), to_table(A("w2", NE + SL * a, NE + SL * a + SL), SL), float(-M * l), Op.add, 0.0, Op.max)
+
+    def successors(l):
+        ts(A("a1", 0, 21), A("rin%d" % l, 0, 21), float(SL - 1 - RK * (r + 1)), Op.add)
+        tt(A("a1", 0, 21), A("a1", 0, 21), A("nt", 0, 21), Op.max)
+        cp(A("suu", 0, 21), A("a1", 0, 21))
+        scat(A("w2", NE + NS), A("suu", 0, 21), A("sud", SL * (2 - l), SL * (3 - l)))
+
+    dmas("ld_l", [("ys"[i % 2], T.lvt[16 * i:16 * i + 16, :], T.lv[:], [], [A("lvt")]) for i in range(8)])
+    dmas("ld_e", [("y", T.e[:, 0:24], T.pr0[:], [], [A("e", 0, 24)]), ("y", T.e[:, 24:48], T.pr1[:], [], [A("e", 24, 48)])])
+    dmas("ld_x", [("y", T.xt[:], T.x[:], [], [A("xt")])])
+    dmas("ld_w", [("y", u8(A("wq")), T.wc[:], [], [A("wq")]), ("y", T.wp[:], T.ws[:], [], [A("wp")])])
+    dmas("ld_v", [("y", u8(A("vq")), T.vc[:], [], [A("vq")]), ("y", T.vp[:], T.vs[:], [], [A("vp")])])
+    dmas("ld_u", [("y", T.ut[:], T.u[:], [], [A("ut")])])
+
+    fill(A("ones"), 1.0)
+    iota(A("iot"), [[1, C]], 0)
+    iota(A("pc", 0, 1), [[0, 1]], 0, 1)
+    iota(A("kc", 14, 17), [[M, 3]], -1)
+    iota(A("nm"), [[0, C // 16], [1, 16]], 0)
+    run("g", [A("ones")], [A("ident")], lambda: g.affine_select(T.ident[:], T.ones[:], [[-1, 128]], Op.is_equal, 0.0, 0, 1))
+    iota(A("nt0"), [[16, 24]], 0)
+    fill(A("et"), 0.0)
+    for name, step in (("lrs", LSEG), ("rt", 16), ("rs", SEG), ("rp", 8)):
+        fill(A(name), 1.0)
+    fill(A("tot"), 0.0)
+    for l in (1, 2):
+        fill(A("req%d" % l, 21, 24), 0.0)
+    fill(A("loh", 0, None, LSEG), 0.0)
+    for name, step in (("lrs", LSEG), ("rt", 16), ("rs", SEG), ("rp", 8)):
+        fill(A(name, 0, None, step), 0.0)
+    ts(A("pc", 1, 2), A("pc", 0, 1), 15, Op.bitwise_and)
+    ts(A("pc", 2, 3), A("pc", 0, 1), 16, Op.bitwise_and)
+    ts(A("pf", 1, 2), A("pc", 1, 2), -1.0, Op.mult)
+
+    def ranks(some):
+        for s in some:
+            act(A("ew", 1 + C * s, 1 + C * s + C), A("iot"), Act.Identity, bias=float(RK * (s + 1)))
+    ranks(range(0, 3))
+    act(A("ma"), A("nm"), Act.Abs, bias=A("pf", 1, 2))
+    act(A("r16"), A("nm"), Act.Sign)
+    act(A("mask"), A("ma"), Act.Relu, bias=1.0, scale=-1.0)
+    diagonal(None)
+    ranks(range(3, N))
+
+    for l in range(3):
+        ts(A("loh", LSEG * l + 1, LSEG * l + LSEG), A("lvt"), float(l), Op.is_equal)
+    scan(A("lc1"), A("lrs"), A("loh"))
+    cp(A("pf", 0, 1), A("pc", 1, 2))
+    cp(A("tot", 0, 3), A("lc1", LSEG - 1, None, LSEG))
+    ts(A("pe", 0, 1), A("pc", 2, 3), 0.03125, Op.mult, -0.5, Op.add)
+    across(3, 14)
+    ts(A("pe", 1, 2), A("pc", 2, 3), -0.03125, Op.mult)
+    tt(A("loh", 0, None, LSEG), A("tb", 0, 3), A("kt", 0, 3), Op.add)
+    fill(A("ew", 0, 1), float(RK * (N + 1)))
+    scan(A("lc2"), A("lrs"), A("loh"))
+    ts(A("u1"), A("e"), 1.0, Op.add)
+    tt(A("lc1"), A("loh"), A("lc2"), Op.mult)
+    tt(A("pos"), A("lc1", 1, LSEG), A("lc1", LSEG + 1, 2 * LSEG), Op.add)
+    tt(A("pos"), A("pos"), A("lc1", 2 * LSEG + 1, 3 * LSEG), Op.add)
+    cp(A("posu"), A("pos"))
+    before("g", [A("posu")], [])
+    PSEM = ["ar_pa"] * 4 + ["ar_pb"] * 2 + ["ar_pc"]
+    for part in spread(T, topo, r):
+        call([(T.cores[ps[i]], es, PSEM[i], ap(A("posu")), ap(A("pin", 24 * back(i), 24 * back(i) + 24))) for i, es in part])
+    for i in range(NP):
+        sem = PSEM[direct[i][0]]
+        note("x", [], [A("pin", 24 * i, 24 * i + 24)], sem, sum(n for j, n in direct if PSEM[j] == sem))
+    iota(A("kc", 0, 14), [[CAP, 14]], NE - 1)
+    iota(A("rw", NE), [[0, NS]], 0)
+    iota(A("uw", 0, 1), [[0, 1]], FZ)
+    iota(A("uw", UM), [[1, SL]], FL2)
+    scat(A("pw"), A("posu"), A("iot"))
+    PERM = to_table(A("pw"), C)
+    cp(A("permu"), PERM)
+    act(A("eexp"), A("ew"), off=A("u1"))
+    quant("sq", "ss", 0, C, A("xt"))
+    quant("e1q", "e1s", 0, 512, A("et"))
+
+    pick("spq", "sps", 0, "sq", "ss", C, A("permu", 0, 8))
+    for l in (2, 1):
+        for k in range(2):
+            a = 16 * (2 - l) + 8 * k
+            ts(A("pn", a, a + 8), A("m2", M * l + 15, M * l + M, 16), float(C * k), Op.add)
+    decode("spq", "sps", 0, M, tile("xs", 6), "vsvs")
+    sort_entries(2)
+    quant("xq", "xp", 128 * 6, M, A("xs", 512 * 6, 512 * 7))
+    ts(A("nt"), A("nt0"), A("pf", 0, 1), Op.add)
+    ts(A("prod", 7, None, 8), A("nt0", 0, 16), A("pf", 0, 1), Op.add)
+    ev = layer("wq", "wp", 6, tile("ti", 0))
+    for k in range(2):
+        for h in range(2):
+            ts(A("pd", 48 * k + h, 48 * k + 48, 2), PERM, float(C * k), Op.add)
+    for f in ev:
+        f()
+    quant("sdq1", "sds1", 0, M, A("ti", 0, 512))
+    exchange(1)
+    iota(A("zt"), [[0, 512]], 0)
+    iota(A("pl"), [[-M, 2], [0, 2], [1, M]], 2 * M)
+
+    def place(i):
+        s, off = (r, A("posu")) if i == NP else (ps[i], A("pin", 24 * i, 24 * i + 24))
+        act(A("uw", 1 + C * s, 1 + C * s + C), A("iot"), Act.Identity, off=off, bias=float(M * i))
+    sort_entries(1)
+    diagonal(A("pe", 0, 1))
+    place(NP)
+    slots(2)
+    fill_slots(2)
+    tables(2)
+    iota(A("w2", NE, NE + NS), [[0, NS]], 0)
+    iota(A("w2", SU0), [[0, NE]], BZ)
+    iota(A("sud"), [[1, NS]], BL3)
+    for i in sorted(range(NP), key=lambda i: (direct[i][0] != NP - 1, direct[i][0])):
+        place(i)
+    pick("spq", "sps", M, "sq", "ss", C, A("permu", 8, 24))
+    quant("eeq", "ees", 0, 512, A("et"))
+    act(A("uexp"), A("uw", 0, UM), off=A("u1"))
+    spread_lists(A("uexp"), 1)
+    diagonal(A("pe", 1, 2))
+    decode("spq", "sps", M, 256, lambda b: A("ds", 256 * b, 256 * b + 256))
+    for k in range(2):
+        act(A("pp", C * k, C * k + C), A("iot"), off=A("posu"))
+    for b in range(4):
+        act(A("yp", 256 * b, 256 * b + M), tile("ti", 0)(b))
+    quant("wfq", "wfs", FY, M, A("ti", 0, 512))
+    quant("wfq", "wfs", FZ, M, A("zt"))
+    slots(1)
+    pair_lists("f1")
+    quant("eoq", "eos", 0, 512, A("et"))
+
+    def asked():
+        ts(A("c2u", 0, 21), A("rin2", 0, 21), float(-1 - RK * (r + 1)), Op.add, 0.0, Op.max)
+        tt(A("m1", 0, SL), A("pp"), A("mask", 0, SL), Op.mult, off=A("c2u", 0, 21))
+    gathered(1, "wf", FL2, "f1", "ds", 0, 256, 0, asked)
+    ev = layer("wq", "wp", 0, lambda b: A("yp", 256 * b + M, 256 * b + 256))
+    scan(A("m2", 0, SL), A("r16", 0, SL), A("m1", 0, SL))
+    ts(A("g2", 0, 21), A("m2", 15, SL, 16), float(2 * M - 1), Op.min)
+    send(2, ev, lambda b: A("yp", 256 * b, 256 * b + 256), "g2")
+
+    es, si, ci, O = level(2)
+    for k in range(2):
+        ts(A("a1", 8 * k, 8 * k + 8), A("ci", 8 * k, 8 * k + 8), float(C * (r - k)), Op.add)
+    ts(A("a4", 0, 16), si, float(r + 1), Op.is_equal)
+    ts(A("a3", 0, 16), O, float(NE), Op.is_ge, float(UM + SL), Op.mult)
+    ts(A("a2", 0, 16), O, float(UM - NE), Op.add)
+    tt(A("a1", 0, 16), A("a1", 0, 16), A("a4", 0, 16), Op.mult)
+    tt(A("a2", 0, 16), A("a2", 0, 16), A("a3", 0, 16), Op.min)
+    tt(A("a5", 0, 16), A("a1", 0, 16), A("a2", 0, 16), Op.max)
+    for h in range(2):
+        cp(A("u2", h, 32, 2), A("a5", 0, 16))
+    act(A("gx"), A("uw"), off=A("u2"))
+    for b in range(4):
+        act(tile("ti", 1)(b), A("yp", 256 * b + M, 256 * b + 256))
+    senders(2)
+    pair_lists("f2")
+    quant("wfq", "wfs", FY + M, M, A("ti", 512, 1024))
+    successors(2)
+
+    gathered(2, "wf", FW, "f2", "ds", 128, 256, 1)
+    for f in layer("wq", "wp", 1, tile("xs", 2)):
+        f()
+    quant("xq", "xp", 256, M, A("xs", 1024, 1536))
+    decode("xq", "xp", 256, M, tile("xs", 3), "vsvs")
+    quant("xq", "xp", 384, M, A("xs", 1536, 2048))
+    ev = layer("vq", "vp", 3, lambda b: A("zp", 128 * b, 128 * b + M))
+    send(3, ev, lambda b: A("zp", 128 * b, 128 * b + M), "h2")
+
+    SU = A("w2", SU0)
+    for b in range(4):
+        act(tile("ti", 2)(b), A("zp", 128 * b, 128 * b + M))
+    spread_lists(SU, 1)
+    decode("wfq", "wfs", FY, 256, lambda b: A("dy", 256 * b, 256 * b + 256))
+    fill_slots(1)
+    quant("wbq", "wbs", BZ, M, A("zt"))
+    quant("wbq", "wbs", 2 * M, M, A("ti", 1024, 1536))
+    pair_lists("b1")
+    tables(1)
+    senders(1)
+
+    gathered(3, "wb", BL4, "b1", "dy", M, 256, 4)
+    ev = layer("vq", "vp", 4, lambda b: A("zp", 512 + 128 * b, 512 + 128 * b + M))
+    send(4, ev, lambda b: A("zp", 512 + 128 * b, 512 + 128 * b + M), "h1")
+
+    successors(1)
+    spread_lists(SU, 0)
+    for b in range(4):
+        act(tile("ti", 3)(b), A("zp", 512 + 128 * b, 512 + 128 * b + M))
+    quant("uq", "us", 0, 128, A("ut"))
+    pair_lists("b0")
+    quant("wbq", "wbs", M, M, A("ti", 1536, 2048))
+
+    gathered(4, "wb", BW, "b0", "dy", 0, 256, 5)
+    for f in layer("vq", "vp", 5, tile("ti", 4)):
+        f()
+    quant("wbq", "wbs", 0, M, A("ti", 2048, 2560))
+    pick("oq", "opl", 0, "wbq", "wbs", C, A("posu"))
+    H = C // 2
+    for h in range(2):
+        mm(bank("PA", h, H), "uq", "us", 0, "oq", "opl", H * h, H)
+    dmas("st_c", [("y", T.oc[:], u8(A("oq")), [A("oq")], [])])
+    dmas("st_s", [("y", T.osc[4 * k:4 * k + 4, :], T.opl[32 * k:32 * k + 4, :], [A("opl")], []) for k in range(4)])
+    for h in range(2):
+        plain("vs"[h], A("yo", H * h, H * h + H), bank("PA", h, H))
+    dmas("st_y", [("s", T.y[:], T.yo[:], [A("yo")], [])])
+
+    g.wait_ge(T.sem.sent, sent[0])
+    for sem, val in total.items():
+        g.wait_ge(T.sem[sem], val)

@@ -23,16 +23,18 @@ def _sb(n, d):
 SMALL = {}
 for _n in ("tot", "tt", "ts", "tb", "rt", "kc", "kt", "pos", "nt0", "nt", "a1", "a2", "a3", "a4", "a5"):
     SMALL[_n] = (32 * len(SMALL), 32 if len(SMALL) < 7 else 24)
+for _n in ("tot1", "tt1", "ts1", "tb1", "kt1", "b1", "b2", "b3"):
+    SMALL["x" + _n] = (32 * len(SMALL), 32)
 
 SCRATCH = {
     "sm": _sb(32 * len(SMALL), F32), "e": _sb(48, I32), "lvt": _sb(24, I32), "iot": _sb(C, F32),
-    "ew": _sb(UM, F32), "eexp": _sb(NE, F32), "es": _sb(512, F32), "vi": _sb(16, I32), "si": _sb(32, I32), "ci": _sb(32, I32),
-    "oh": _sb(NP * SEG, F32), "rs": _sb(NP * SEG, F32), "c1": _sb(NP * SEG, F32), "c2": _sb(NP * SEG, F32),
-    "prod": _sb(128, F32), "rp": _sb(128, F32), "pm": _sb(256, F32),
+    "ew": _sb(UM, F32), "eexp": _sb(NE, F32), "es": _sb(512, F32), "vi": _sb(32, I32), "si": _sb(32, I32), "ci": _sb(32, I32),
+    "oh": _sb(2 * NP * SEG, F32), "rs": _sb(NP * SEG, F32), "c1": _sb(2 * NP * SEG, F32), "c2": _sb(2 * NP * SEG, F32),
+    "prod": _sb(256, F32), "rp": _sb(128, F32), "pm": _sb(256, F32),
     "loh": _sb(3 * LSEG, F32), "lrs": _sb(3 * LSEG, F32), "lc1": _sb(3 * LSEG, F32), "lc2": _sb(3 * LSEG, F32),
     "ou": _sb(32, U16), "pp": _sb(NE, F32), "posu": _sb(24, U16), "pin": _sb(24 * NP, U16), "pc": _sb(4, I32), "pf": _sb(8, F32),
     "nm": _sb(C, BF), "ma": _sb(C, BF), "mask": _sb(C, BF), "r16": _sb(C, BF),
-    "rw": _sb(NE + NS, F32), "m1": _sb(C, F32), "m2": _sb(C, F32),
+    "rw": _sb(NE + NS, F32), "m1": _sb(2 * C, F32), "m2": _sb(2 * C, F32),
     "req1": _sb(24, F32), "req2": _sb(24, F32), "rin1": _sb(24, F32), "rin2": _sb(24, F32), "hr1": _sb(6, F32), "hr2": _sb(6, F32),
     "c2u": _sb(22, U16), "g2": _sb(22, U16), "h1": _sb(22, U16), "h2": _sb(22, U16),
     "pw": _sb(C, F32), "permu": _sb(24, U16), "pd": _sb(96, U16), "pn": _sb(32, U16),
@@ -105,20 +107,14 @@ def helper_engines(T, topo, r, k):
 
 
 def arrivals(T, topo, r):
-    direct, planes, tables = [], 0, 0
+    direct, relayed = [], 0
     for s in peers_of(T, topo, r):
         i = peers_of(T, topo, s).index(r)
         one, two = spread(T, topo, s)
         n = [len(es) for j, es in one + two if j == i][0]
         direct.append((i, n))
-        if i < NP - 1:
-            far = len(topo.engines(helpers_of(T, topo, s)[i // 2], T.cores[r])) // 2
-            planes += far
-            tables += far
-        else:
-            planes += n
-            tables += n // 4
-    return direct, planes, tables
+        relayed += len(topo.engines(helpers_of(T, topo, s)[i // 2], T.cores[r])) // 2 if i < NP - 1 else n
+    return direct, relayed
 
 
 def dst(topo, c):
@@ -137,7 +133,7 @@ def helper_program(g, core, T, topo, r, h):
         else:
             base, w = 0, 3
             here, there, sem, step = "hr%d" % k, "rin%d" % k, "ar_r%d" % k, w
-            g.wait_ge(T.sem["ar_hr%d" % k], len(engine_sets(T, topo, r)[1]) // 4)
+            g.wait_ge(T.sem["ar_hr%d" % k], len(engine_sets(T, topo, r)[1]))
         tr = []
         for j in range(2):
             d = ps[2 * h + j]
@@ -166,6 +162,7 @@ def rank_program(g, core, T, topo):
     log = {}
     total = {}
     sent = [0]
+    held = [None]
 
     def A(name, a=0, b=None, step=1):
         if name in SMALL:
@@ -202,7 +199,39 @@ def rank_program(g, core, T, topo):
             log.setdefault(v[0], []).append((v, wr, q, sem, val))
         total[sem] = max(total.get(sem, 0), val)
 
+    def weave(*chains, keep=False):
+        out = []
+        for f in chains:
+            held[0] = []
+            f()
+            out.append(held[0])
+        held[0] = None
+        first, others = out[0], out[1:]
+        turn = 0
+        for i, (fs, rd, wr) in enumerate(first):
+            for f in fs:
+                f()
+            nxt = first[i + 1][1] + first[i + 1][2] if i + 1 < len(first) else []
+            others = [c for c in others if c]
+            if others and any(u[0] == v[0] and meet(u, v) for u in wr for v in nxt):
+                turn += 1
+                for f in others[turn % len(others)].pop(0)[0]:
+                    f()
+        if keep:
+            return sum(others, [])
+        while any(others):
+            for c in others:
+                for f in c.pop(0)[0] if c else ():
+                    f()
+
+    def hold(q, f, reads=(), writes=()):
+        if q == "v" or not held[0]:
+            held[0].append(([], list(reads), list(writes)))
+        held[0][-1][0].append(f)
+
     def run(q, reads, writes, call):
+        if held[0] is not None:
+            return hold(q, lambda: run(q, reads, writes, call), reads, writes)
         before(q, reads, writes)
         cnt[q] += 1
         call().then_inc(T.sem["q_" + q], 1)
@@ -285,7 +314,7 @@ def rank_program(g, core, T, topo):
     def back(i):
         return peers_of(T, topo, ps[i]).index(r)
 
-    direct, n_planes, n_tables = arrivals(T, topo, r)
+    direct, n_relayed = arrivals(T, topo, r)
     n_direct = sum(n for i, n in direct)
     rest = engine_sets(T, topo, r)[1]
 
@@ -316,7 +345,7 @@ def rank_program(g, core, T, topo):
         call([(T.cores[ps[i]], rest, "ar_s%d" % k, ap(A(sn, step * i, step * i + w)),
                ap(A(name + "s", base + w * back(i), base + w * back(i) + w)))])
         note("x", [], [A(name + "q", base, base + NP * w)], "ar_c%d" % k, n_direct)
-        note("x", [], [A(name + "s", base, base + NP * w)], "ar_s%d" % k, n_planes)
+        note("x", [], [A(name + "s", base, base + NP * w)], "ar_s%d" % k, n_relayed)
 
     def bank(p, b, n):
         return A(p, 512 * b, 512 * b + n)
@@ -333,16 +362,16 @@ def rank_program(g, core, T, topo):
         else:
             act(o, i, off=off)
 
-    def to_table(w, n):
-        tt(A("m1", 0, n), w, A("mask", 0, n), Op.mult)
-        scan(A("m2", 0, n), A("r16", 0, n), A("m1", 0, n))
-        return A("m2", 15, n, 16)
+    def to_table(w, n, a=0):
+        tt(A("m1", a, a + n), w, A("mask", 0, n), Op.mult)
+        scan(A("m2", a, a + n), A("r16", 0, n), A("m1", a, a + n))
+        return A("m2", a + 15, a + n, 16)
 
-    def across(n, k0):
-        trn(A("tt"), A("tot"))
-        tt(A("kt", 0, n), A("kc", k0, k0 + n), A("tot", 0, n), Op.subtract)
-        scan(A("ts"), A("rt"), A("tt"))
-        trn(A("tb"), A("ts"))
+    def across(n, k0, x="%s"):
+        trn(A(x % "tt"), A(x % "tot"))
+        tt(A(x % "kt", 0, n), A("kc", k0, k0 + n), A(x % "tot", 0, n), Op.subtract)
+        scan(A(x % "ts"), A("rt"), A(x % "tt"))
+        trn(A(x % "tb"), A(x % "ts"))
 
     def spread_lists(win, level):
         for k in range(2):
@@ -376,9 +405,9 @@ def rank_program(g, core, T, topo):
     def send(k, evac, win, lists):
         at = 4 * SL * (k - 2)
         for piece, (a, z) in ((0, (0, 12)), (1, (12, 21))) if CHUNK else ((None, (0, 21)),):
+            for b in range(4 if piece != 1 else 0):
+                evac[b]()
             for b in range(4):
-                if piece != 1:
-                    evac[b]()
                 plain("vs"[b % 2], A("st", at + 64 * a + b, at + 64 * z, 4), win(b), A(lists, a, z))
             quant("sdq%d" % k, "sds%d" % k, 16 * a, 16 * (z - a), A("st", at + 64 * a, at + 64 * z))
             exchange(k, piece)
@@ -409,20 +438,23 @@ def rank_program(g, core, T, topo):
     def slots(l):
         es, si, ci, O = level(l)
         a = 2 - l
-        cp(A("vi"), to_table(es, 256))
-        fill(A("oh", 0, None, SEG), 0.0)
-        ts(si, A("vi"), 10, Op.arith_shift_right)
-        ts(ci, A("vi"), RK - 1, Op.bitwise_and)
+        x, W = ("%s", "x%s1")[a], NP * SEG
+        o, vi = W * a, A("vi", 16 * a, 16 * a + 16)
+        fill(A("oh", o, o + W, SEG), 0.0)
+        cp(vi, to_table(es, 256, C * a))
+        ts(si, vi, 10, Op.arith_shift_right)
+        ts(ci, vi, RK - 1, Op.bitwise_and)
         for i in range(NP):
-            ts(A("oh", SEG * i + 1, SEG * i + SEG), si, float(ps[i] + 1), Op.is_equal)
-        scan(A("c1"), A("rs"), A("oh"))
-        cp(A("tot", 0, NP), A("c1", SEG - 1, None, SEG))
-        across(NP, NP * a)
-        tt(A("oh", 0, None, SEG), A("tb", 0, NP), A("kt", 0, NP), Op.add)
-        scan(A("c2"), A("rs"), A("oh"))
+            ts(A("oh", o + SEG * i + 1, o + SEG * i + SEG), si, float(ps[i] + 1), Op.is_equal)
+        scan(A("c1", o, o + W), A("rs"), A("oh", o, o + W))
+        cp(A(x % "tot", 0, NP), A("c1", o + SEG - 1, o + W, SEG))
+        across(NP, NP * a, x)
+        tt(A("oh", o, o + W, SEG), A(x % "tb", 0, NP), A(x % "kt", 0, NP), Op.add)
+        scan(A("c2", o, o + W), A("rs"), A("oh", o, o + W))
         for i in range(NP):
-            tt(A("prod", i, None, 8), A("oh", SEG * i + 1, SEG * i + SEG), A("c2", SEG * i + 1, SEG * i + SEG), Op.mult)
-        scan(A("pm", 128 * a, 128 * a + 128), A("rp"), A("prod"), Op.max)
+            b = o + SEG * i
+            tt(A("prod", 128 * a + i, 128 * a + 128, 8), A("oh", b + 1, b + SEG), A("c2", b + 1, b + SEG), Op.mult)
+        scan(A("pm", 128 * a, 128 * a + 128), A("rp"), A("prod", 128 * a, 128 * a + 128), Op.max)
         cp(A("ou", 16 * a, 16 * a + 16), O)
 
     def fill_slots(l):
@@ -431,11 +463,14 @@ def rank_program(g, core, T, topo):
     def tables(l):
         a, b, at = "req%d" % l, "rin%d" % l, NE + SL * (2 - l)
         cp(A(a, 0, 21), to_table(A("rw", at, at + SL), SL))
-        before("g", [A(a)], [])
-        es = parts(rest, 4)
-        call([(hs[h], es[h], "ar_hr%d" % l, ap(A(a, 6 * h, 6 * h + 6)), ap(A("hr%d" % l))) for h in range(3)] +
-             [(T.cores[ps[-1]], es[3], "ar_r%d" % l, ap(A(a, 18, 24)), ap(A(b, 18, 24)))])
-        note("x", [], [A(b)], "ar_r%d" % l, n_tables)
+
+        def go():
+            before("g", [A(a)], [])
+            for h in range(3):
+                call([(hs[h], rest, "ar_hr%d" % l, ap(A(a, 6 * h, 6 * h + 6)), ap(A("hr%d" % l)))])
+            call([(T.cores[ps[-1]], rest, "ar_r%d" % l, ap(A(a, 18, 21)), ap(A(b, 18, 21)))])
+            note("x", [], [A(b)], "ar_r%d" % l, n_relayed)
+        hold("g", go)
 
     def senders(l):
         es, si, ci, O = level(l)
@@ -443,19 +478,24 @@ def rank_program(g, core, T, topo):
 
         def w(n):
             return A(n, 0, 16)
-        tt(w("a2"), ci, w("nt"), Op.subtract)
-        ts(w("a3"), si, float(r + 1), Op.is_equal)
-        ts(w("a2"), w("a2"), float(SU0 - 1), Op.add)
-        tt(w("a2"), w("a2"), w("a3"), Op.mult)
-        tt(w("a2"), w("a2"), O, Op.add)
-        cp(A("o2u"), w("a2"))
+        tt(w("xb1"), ci, w("nt"), Op.subtract)
+        ts(w("xb2"), si, float(r + 1), Op.is_equal)
+        ts(w("xb1"), w("xb1"), float(SU0 - 1), Op.add)
+        tt(w("xb1"), w("xb1"), w("xb2"), Op.mult)
+        tt(w("xb1"), w("xb1"), O, Op.add)
+        cp(A("o2u"), w("xb1"))
         scat(A("w2"), A("o2u"), A("pl", 256 * a, 256 * a + 256))
-        ts(A("h%d" % l, 0, 21), to_table(A("w2", NE + SL * a, NE + SL * a + SL), SL), float(-M * l), Op.add, 0.0, Op.max)
+
+    def sent_from(l):
+        a = NE + SL * (2 - l)
+        return (lambda: tt(A("m1", C, C + SL), A("w2", a, a + SL), A("mask", 0, SL), Op.mult),
+                lambda: scan(A("m2", C, C + SL), A("r16", 0, SL), A("m1", C, C + SL)),
+                lambda: ts(A("h%d" % l, 0, 21), A("m2", C + 15, C + SL, 16), float(-M * l), Op.add, 0.0, Op.max))
 
     def successors(l):
-        ts(A("a1", 0, 21), A("rin%d" % l, 0, 21), float(SL - 1 - RK * (r + 1)), Op.add)
-        tt(A("a1", 0, 21), A("a1", 0, 21), A("nt", 0, 21), Op.max)
-        cp(A("suu", 0, 21), A("a1", 0, 21))
+        ts(A("xb3", 0, 21), A("rin%d" % l, 0, 21), float(SL - 1 - RK * (r + 1)), Op.add)
+        tt(A("xb3", 0, 21), A("xb3", 0, 21), A("nt", 0, 21), Op.max)
+        cp(A("suu", 0, 21), A("xb3", 0, 21))
         scat(A("w2", NE + NS), A("suu", 0, 21), A("sud", SL * (2 - l), SL * (3 - l)))
 
     dmas("ld_l", [("ys"[i % 2], T.lvt[16 * i:16 * i + 16, :], T.lv[:], [], [A("lvt")]) for i in range(8)])
@@ -476,8 +516,7 @@ def rank_program(g, core, T, topo):
     for name, step in (("lrs", LSEG), ("rt", 16), ("rs", SEG), ("rp", 8)):
         fill(A(name), 1.0)
     fill(A("tot"), 0.0)
-    for l in (1, 2):
-        fill(A("req%d" % l, 21, 24), 0.0)
+    fill(A("xtot1"), 0.0)
     fill(A("loh", 0, None, LSEG), 0.0)
     for name, step in (("lrs", LSEG), ("rt", 16), ("rs", SEG), ("rp", 8)):
         fill(A(name, 0, None, step), 0.0)
@@ -523,11 +562,13 @@ def rank_program(g, core, T, topo):
     iota(A("uw", 0, 1), [[0, 1]], FZ)
     iota(A("uw", UM), [[1, SL]], FL2)
     scat(A("pw"), A("posu"), A("iot"))
-    PERM = to_table(A("pw"), C)
-    cp(A("permu"), PERM)
-    act(A("eexp"), A("ew"), off=A("u1"))
     quant("sq", "ss", 0, C, A("xt"))
+    tt(A("m1", 0, C), A("pw"), A("mask"), Op.mult)
     quant("e1q", "e1s", 0, 512, A("et"))
+    scan(A("m2", 0, C), A("r16"), A("m1", 0, C))
+    PERM = A("m2", 15, C, 16)
+    act(A("eexp"), A("ew"), off=A("u1"))
+    cp(A("permu"), PERM)
 
     pick("spq", "sps", 0, "sq", "ss", C, A("permu", 0, 8))
     for l in (2, 1):
@@ -538,7 +579,8 @@ def rank_program(g, core, T, topo):
     sort_entries(2)
     quant("xq", "xp", 128 * 6, M, A("xs", 512 * 6, 512 * 7))
     ts(A("nt"), A("nt0"), A("pf", 0, 1), Op.add)
-    ts(A("prod", 7, None, 8), A("nt0", 0, 16), A("pf", 0, 1), Op.add)
+    for a in range(2):
+        ts(A("prod", 128 * a + 7, 128 * a + 128, 8), A("nt0", 0, 16), A("pf", 0, 1), Op.add)
     ev = layer("wq", "wp", 6, tile("ti", 0))
     for k in range(2):
         for h in range(2):
@@ -556,62 +598,57 @@ def rank_program(g, core, T, topo):
     sort_entries(1)
     diagonal(A("pe", 0, 1))
     place(NP)
-    slots(2)
-    fill_slots(2)
-    tables(2)
-    iota(A("w2", NE, NE + NS), [[0, NS]], 0)
-    iota(A("w2", SU0), [[0, NE]], BZ)
-    iota(A("sud"), [[1, NS]], BL3)
-    for i in sorted(range(NP), key=lambda i: (direct[i][0] != NP - 1, direct[i][0])):
-        place(i)
-    pick("spq", "sps", M, "sq", "ss", C, A("permu", 8, 24))
-    quant("eeq", "ees", 0, 512, A("et"))
-    act(A("uexp"), A("uw", 0, UM), off=A("u1"))
-    spread_lists(A("uexp"), 1)
-    diagonal(A("pe", 1, 2))
-    decode("spq", "sps", M, 256, lambda b: A("ds", 256 * b, 256 * b + 256))
     for k in range(2):
         act(A("pp", C * k, C * k + C), A("iot"), off=A("posu"))
     for b in range(4):
         act(A("yp", 256 * b, 256 * b + M), tile("ti", 0)(b))
-    quant("wfq", "wfs", FY, M, A("ti", 0, 512))
-    quant("wfq", "wfs", FZ, M, A("zt"))
-    slots(1)
-    pair_lists("f1")
-    quant("eoq", "eos", 0, 512, A("et"))
+    for i in sorted(range(NP), key=lambda i: (direct[i][0] != NP - 1, direct[i][0])):
+        place(i)
+    act(A("uexp"), A("uw", 0, UM), off=A("u1"))
+    spread_lists(A("uexp"), 1)
+    rest1 = weave(lambda: (slots(2), fill_slots(2), tables(2), quant("eeq", "ees", 0, 512, A("et")), diagonal(A("pe", 1, 2)),
+                           pick("spq", "sps", M, "sq", "ss", C, A("permu", 8, 24))), lambda: slots(1), keep=True)
+    iota(A("w2", NE, NE + NS), [[0, NS]], 0)
+    iota(A("w2", SU0), [[0, NE]], BZ)
+    iota(A("sud"), [[1, NS]], BL3)
+    decode("spq", "sps", M, 256, lambda b: A("ds", 256 * b, 256 * b + 256))
+    weave(lambda: held[0].extend(rest1), lambda: (quant("wfq", "wfs", FY, M, A("ti", 0, 512)), quant("wfq", "wfs", FZ, M, A("zt")),
+                                                  pair_lists("f1"), quant("eoq", "eos", 0, 512, A("et"))))
 
-    def asked():
-        ts(A("c2u", 0, 21), A("rin2", 0, 21), float(-1 - RK * (r + 1)), Op.add, 0.0, Op.max)
-        tt(A("m1", 0, SL), A("pp"), A("mask", 0, SL), Op.mult, off=A("c2u", 0, 21))
-    gathered(1, "wf", FL2, "f1", "ds", 0, 256, 0, asked)
+    gathered(1, "wf", FL2, "f1", "ds", 0, 256, 0)
     ev = layer("wq", "wp", 0, lambda b: A("yp", 256 * b + M, 256 * b + 256))
+    ts(A("c2u", 0, 21), A("rin2", 0, 21), float(-1 - RK * (r + 1)), Op.add, 0.0, Op.max)
+    tt(A("m1", 0, SL), A("pp"), A("mask", 0, SL), Op.mult, off=A("c2u", 0, 21))
     scan(A("m2", 0, SL), A("r16", 0, SL), A("m1", 0, SL))
     ts(A("g2", 0, 21), A("m2", 15, SL, 16), float(2 * M - 1), Op.min)
     send(2, ev, lambda b: A("yp", 256 * b, 256 * b + 256), "g2")
 
-    es, si, ci, O = level(2)
-    for k in range(2):
-        ts(A("a1", 8 * k, 8 * k + 8), A("ci", 8 * k, 8 * k + 8), float(C * (r - k)), Op.add)
-    ts(A("a4", 0, 16), si, float(r + 1), Op.is_equal)
-    ts(A("a3", 0, 16), O, float(NE), Op.is_ge, float(UM + SL), Op.mult)
-    ts(A("a2", 0, 16), O, float(UM - NE), Op.add)
-    tt(A("a1", 0, 16), A("a1", 0, 16), A("a4", 0, 16), Op.mult)
-    tt(A("a2", 0, 16), A("a2", 0, 16), A("a3", 0, 16), Op.min)
-    tt(A("a5", 0, 16), A("a1", 0, 16), A("a2", 0, 16), Op.max)
-    for h in range(2):
-        cp(A("u2", h, 32, 2), A("a5", 0, 16))
-    act(A("gx"), A("uw"), off=A("u2"))
-    for b in range(4):
-        act(tile("ti", 1)(b), A("yp", 256 * b + M, 256 * b + 256))
-    senders(2)
-    pair_lists("f2")
-    quant("wfq", "wfs", FY + M, M, A("ti", 512, 1024))
-    successors(2)
+    def places():
+        es, si, ci, O = level(2)
+        for k in range(2):
+            ts(A("a1", 8 * k, 8 * k + 8), A("ci", 8 * k, 8 * k + 8), float(C * (r - k)), Op.add)
+        ts(A("a4", 0, 16), si, float(r + 1), Op.is_equal)
+        ts(A("a3", 0, 16), O, float(NE), Op.is_ge, float(UM + SL), Op.mult)
+        ts(A("a2", 0, 16), O, float(UM - NE), Op.add)
+        tt(A("a1", 0, 16), A("a1", 0, 16), A("a4", 0, 16), Op.mult)
+        tt(A("a2", 0, 16), A("a2", 0, 16), A("a3", 0, 16), Op.min)
+        tt(A("a5", 0, 16), A("a1", 0, 16), A("a2", 0, 16), Op.max)
+        for h in range(2):
+            cp(A("u2", h, 32, 2), A("a5", 0, 16))
+        act(A("gx"), A("uw"), off=A("u2"))
+        for b in range(4):
+            act(tile("ti", 1)(b), A("yp", 256 * b + M, 256 * b + 256))
+    weave(places, lambda: senders(2))
+    weave(lambda: (pair_lists("f2"), quant("wfq", "wfs", FY + M, M, A("ti", 512, 1024))), lambda: successors(2))
 
-    gathered(2, "wf", FW, "f2", "ds", 128, 256, 1)
-    for f in layer("wq", "wp", 1, tile("xs", 2)):
+    steps = sent_from(2)
+    gathered(2, "wf", FW, "f2", "ds", 128, 256, 1, steps[0])
+    ev = layer("wq", "wp", 1, tile("xs", 2))
+    steps[1]()
+    for f in ev:
         f()
     quant("xq", "xp", 256, M, A("xs", 1024, 1536))
+    steps[2]()
     decode("xq", "xp", 256, M, tile("xs", 3), "vsvs")
     quant("xq", "xp", 384, M, A("xs", 1536, 2048))
     ev = layer("vq", "vp", 3, lambda b: A("zp", 128 * b, 128 * b + M))
@@ -622,15 +659,14 @@ def rank_program(g, core, T, topo):
         act(tile("ti", 2)(b), A("zp", 128 * b, 128 * b + M))
     spread_lists(SU, 1)
     decode("wfq", "wfs", FY, 256, lambda b: A("dy", 256 * b, 256 * b + 256))
-    fill_slots(1)
-    quant("wbq", "wbs", BZ, M, A("zt"))
-    quant("wbq", "wbs", 2 * M, M, A("ti", 1024, 1536))
-    pair_lists("b1")
-    tables(1)
-    senders(1)
+    weave(lambda: (fill_slots(1), tables(1)), lambda: senders(1),
+          lambda: (quant("wbq", "wbs", BZ, M, A("zt")), quant("wbq", "wbs", 2 * M, M, A("ti", 1024, 1536)), pair_lists("b1")))
 
-    gathered(3, "wb", BL4, "b1", "dy", M, 256, 4)
+    steps = sent_from(1)
+    steps[0]()
+    gathered(3, "wb", BL4, "b1", "dy", M, 256, 4, steps[1])
     ev = layer("vq", "vp", 4, lambda b: A("zp", 512 + 128 * b, 512 + 128 * b + M))
+    steps[2]()
     send(4, ev, lambda b: A("zp", 512 + 128 * b, 512 + 128 * b + M), "h1")
 
     successors(1)
@@ -645,9 +681,9 @@ def rank_program(g, core, T, topo):
     for f in layer("vq", "vp", 5, tile("ti", 4)):
         f()
     quant("wbq", "wbs", 0, M, A("ti", 2048, 2560))
-    pick("oq", "opl", 0, "wbq", "wbs", C, A("posu"))
     H = C // 2
     for h in range(2):
+        pick("oq", "opl", H * h, "wbq", "wbs", C, A("posu", 12 * h, 12 * h + 12))
         mm(bank("PA", h, H), "uq", "us", 0, "oq", "opl", H * h, H)
     dmas("st_c", [("y", T.oc[:], u8(A("oq")), [A("oq")], [])])
     dmas("st_s", [("y", T.osc[4 * k:4 * k + 4, :], T.opl[32 * k:32 * k + 4, :], [A("opl")], []) for k in range(4)])

@@ -9,8 +9,10 @@ FY, FZ, FL2, FW = NP * M, NP * M + 2 * M, NP * M + 3 * M, NP * M + 3 * M + SL
 BZ, BL3, BL4, BW = 384, 512, 512 + SL, 512 + 2 * SL
 NE, NS = 2 * C, 2 * SL
 SEG, LSEG = 17, 25
-UM = 1 + N * C
+UM = 2 + N * C
+EW = 528
 RK = 1024
+BIG = 16 * RK
 SU0 = NE + NS + SL
 WIDE = {1: M, 2: CAP, 3: CAP, 4: CAP}
 LAND = {1: ("wf", 0), 2: ("wf", FL2), 3: ("wb", BL3), 4: ("wb", BL4)}
@@ -23,25 +25,25 @@ def _sb(n, d):
 SMALL = {}
 for _n in ("tot", "tt", "ts", "tb", "rt", "kc", "kt", "pos", "nt0", "nt", "a1", "a2", "a3", "a4", "a5"):
     SMALL[_n] = (32 * len(SMALL), 32 if len(SMALL) < 7 else 24)
-for _n in ("tot1", "tt1", "ts1", "tb1", "kt1", "b1", "b2", "b3"):
+for _n in ("b1", "b2", "b3"):
     SMALL["x" + _n] = (32 * len(SMALL), 32)
 
 SCRATCH = {
     "sm": _sb(32 * len(SMALL), F32), "e": _sb(48, I32), "lvt": _sb(24, I32), "iot": _sb(C, F32),
-    "ew": _sb(UM, F32), "eexp": _sb(NE, F32), "es": _sb(512, F32), "vi": _sb(32, I32), "si": _sb(32, I32), "ci": _sb(32, I32),
-    "oh": _sb(2 * NP * SEG, F32), "rs": _sb(NP * SEG, F32), "c1": _sb(2 * NP * SEG, F32), "c2": _sb(2 * NP * SEG, F32),
-    "prod": _sb(256, F32), "rp": _sb(128, F32), "pm": _sb(256, F32),
+    "ew": _sb(UM - 1, F32), "eexp": _sb(NE, F32), "es": _sb(512, F32), "vi": _sb(34, I32), "si": _sb(34, I32), "ci": _sb(34, I32),
+    "oh": _sb(2 * NP * SEG, F32), "rs": _sb(2 * NP * SEG, F32), "c1": _sb(2 * NP * SEG, F32), "c2": _sb(2 * NP * SEG, F32),
+    "prod": _sb(264, F32), "rp": _sb(264, F32), "pm": _sb(264, F32),
     "loh": _sb(3 * LSEG, F32), "lrs": _sb(3 * LSEG, F32), "lc1": _sb(3 * LSEG, F32), "lc2": _sb(3 * LSEG, F32),
     "ou": _sb(32, U16), "pp": _sb(NE, F32), "posu": _sb(24, U16), "pin": _sb(24 * NP, U16), "pc": _sb(4, I32), "pf": _sb(8, F32),
-    "nm": _sb(C, BF), "ma": _sb(C, BF), "mask": _sb(C, BF), "r16": _sb(C, BF),
-    "rw": _sb(NE + NS, F32), "m1": _sb(2 * C, F32), "m2": _sb(2 * C, F32),
-    "req1": _sb(24, F32), "req2": _sb(24, F32), "rin1": _sb(24, F32), "rin2": _sb(24, F32), "hr1": _sb(6, F32), "hr2": _sb(6, F32),
+    "nm": _sb(C, BF), "ma": _sb(C, BF), "keep": _sb(C, BF),
+    "rw": _sb(NE + NS, F32), "m1": _sb(C, F32), "m2": _sb(2 * C, F32),
+    "req1": _sb(24, F32), "req2": _sb(24, F32), "rin1": _sb(24, F32), "rin2": _sb(24, F32), "hr1": _sb(6, F32),
     "c2u": _sb(22, U16), "g2": _sb(22, U16), "h1": _sb(22, U16), "h2": _sb(22, U16),
     "pw": _sb(C, F32), "permu": _sb(24, U16), "pd": _sb(96, U16), "pn": _sb(32, U16),
-    "u1": _sb(48, U16), "u2": _sb(32, U16), "o2u": _sb(16, U16), "uw": _sb(UM + SL, F32), "uexp": _sb(NE, F32),
+    "u1": _sb(48, U16), "u2": _sb(32, U16), "o2u": _sb(16, U16), "uw": _sb(UM + SL, F32),
     "gx": _sb(512, F32), "gt": _sb(512, F32), "f1": _sb(32, U16), "f2": _sb(32, U16), "b1": _sb(32, U16), "b0": _sb(32, U16),
     "pl": _sb(512, F32), "w2": _sb(SU0 + NE, F32), "sud": _sb(NS, F32), "suu": _sb(22, U16),
-    "ones": _sb(128, BF), "ident": _sb(128, BF), "et": _sb(2048, BF), "zt": _sb(512, BF), "pe": _sb(2, F32),
+    "ones": _sb(EW, BF), "et": _sb(3 * EW, BF), "zt": _sb(512, BF), "pe": _sb(2, F32),
     "e1q": _sb(512, Q4), "e1s": _sb(512, U8), "eeq": _sb(512, Q4), "ees": _sb(512, U8), "eoq": _sb(512, Q4), "eos": _sb(512, U8),
     "xt": _sb(4 * C, BF), "ut": _sb(512, BF), "sq": _sb(C, Q4), "ss": _sb(C, U8), "uq": _sb(128, Q4), "us": _sb(128, U8),
     "wq": _sb(512, Q4), "wp": _sb(512, U8), "vq": _sb(512, Q4), "vp": _sb(512, U8), "yp": _sb(4 * 256, BF),
@@ -58,7 +60,7 @@ for _k in range(1, 5):
     SCRATCH["sds%d" % _k] = _sb(M if _k == 1 else SL, U8)
     SCRATCH["hs%d" % _k] = _sb(M if _k == 1 else 2 * CAP, U8)
 SEMAPHORES = ["q_v", "q_s", "q_t", "q_g", "sent", "ld_l", "ld_e", "ld_x", "ld_w", "ld_v", "ld_u", "st_c", "st_s", "st_y",
-              "ar_pa", "ar_pb", "ar_pc", "ar_r1", "ar_r2", "ar_hr1", "ar_hr2"] + \
+              "ar_pa", "ar_pb", "ar_pc", "ar_r1", "ar_r2", "ar_hr1"] + \
     ["ar_c%d" % k for k in range(1, 5)] + ["ar_s%d" % k for k in range(1, 5)] + ["ar_h%d" % k for k in range(1, 5)]
 
 
@@ -125,7 +127,7 @@ def dst(topo, c):
 def helper_program(g, core, T, topo, r, h):
     ps = peers_of(T, topo, r)
     sent = 0
-    for kind, k in (("s", 1), ("r", 2), ("s", 2), ("s", 3), ("r", 1), ("s", 4)):
+    for kind, k in (("s", 1), ("s", 2), ("s", 3), ("r", 1), ("s", 4)):
         if kind == "s":
             (name, base), w = LAND[k], WIDE[k]
             here, there, sem, step = "hs%d" % k, name + "s", "ar_s%d" % k, 0 if k == 1 else w
@@ -199,7 +201,7 @@ def rank_program(g, core, T, topo):
             log.setdefault(v[0], []).append((v, wr, q, sem, val))
         total[sem] = max(total.get(sem, 0), val)
 
-    def weave(*chains, keep=False):
+    def weave(*chains):
         out = []
         for f in chains:
             held[0] = []
@@ -217,8 +219,6 @@ def rank_program(g, core, T, topo):
                 turn += 1
                 for f in others[turn % len(others)].pop(0)[0]:
                     f()
-        if keep:
-            return sum(others, [])
         while any(others):
             for c in others:
                 for f in c.pop(0)[0] if c else ():
@@ -259,8 +259,8 @@ def rank_program(g, core, T, topo):
         else:
             run("v", [a] + r1, [o], lambda: g.vector.tensor_scalar(ap(o), ap(a), x1, s2, op0, op1))
 
-    def scan(o, reset, d, op1=Op.add):
-        run("v", [reset, d], [o], lambda: g.vector.tensor_tensor_scan(ap(o), ap(reset), ap(d), 0.0, Op.mult, op1))
+    def scan(o, reset, d, op1=Op.add, op0=Op.mult):
+        run("v", [reset, d], [o], lambda: g.vector.tensor_tensor_scan(ap(o), ap(reset), ap(d), 0.0, op0, op1))
 
     def trn(o, i):
         run("v", [i], [o], lambda: g.vector.transpose(ap(o), ap(i)))
@@ -362,16 +362,17 @@ def rank_program(g, core, T, topo):
         else:
             act(o, i, off=off)
 
+    EXTRA = A("pf", 3, 4)
+
     def to_table(w, n, a=0):
-        tt(A("m1", a, a + n), w, A("mask", 0, n), Op.mult)
-        scan(A("m2", a, a + n), A("r16", 0, n), A("m1", a, a + n))
+        scan(A("m2", a, a + n), A("keep", 0, n), w, Op.max, Op.add)
         return A("m2", a + 15, a + n, 16)
 
-    def across(n, k0, x="%s"):
-        trn(A(x % "tt"), A(x % "tot"))
-        tt(A(x % "kt", 0, n), A("kc", k0, k0 + n), A(x % "tot", 0, n), Op.subtract)
-        scan(A(x % "ts"), A("rt"), A(x % "tt"))
-        trn(A(x % "tb"), A(x % "ts"))
+    def across(n, k0):
+        trn(A("tt"), A("tot"))
+        tt(A("kt", 0, n), A("kc", k0, k0 + n), A("tot", 0, n), Op.subtract)
+        scan(A("ts"), A("rt"), A("tt"))
+        trn(A("tb"), A("ts"))
 
     def spread_lists(win, level):
         for k in range(2):
@@ -397,16 +398,16 @@ def rank_program(g, core, T, topo):
             tt(A("xs", 512 * slot + b, 512 * slot + 512, 4), bank("PA", b, M), A(dn, dw * b + d0, dw * b + d0 + M), Op.add)
         quant("xq", "xp", 128 * slot, M, A("xs", 512 * slot, 512 * slot + 512))
 
-    def layer(wn, wsn, slot, out):
+    def layer(wn, wsn, slot, out, engines="vsvs"):
         for b in range(4):
             mm(bank("PB", b, M), wn, wsn, 128 * b, "xq", "xp", 128 * slot, M)
-        return [lambda b=b: scaled("vs"[b % 2], out(b), bank("PB", b, M)) for b in range(4)]
+        return [lambda b=b: scaled(engines[b], out(b), bank("PB", b, M)) for b in range(4)]
 
     def send(k, evac, win, lists):
         at = 4 * SL * (k - 2)
         for piece, (a, z) in ((0, (0, 12)), (1, (12, 21))) if CHUNK else ((None, (0, 21)),):
-            for b in range(4 if piece != 1 else 0):
-                evac[b]()
+            for f in evac if piece != 1 else ():
+                f()
             for b in range(4):
                 plain("vs"[b % 2], A("st", at + 64 * a + b, at + 64 * z, 4), win(b), A(lists, a, z))
             quant("sdq%d" % k, "sds%d" % k, 16 * a, 16 * (z - a), A("st", at + 64 * a, at + 64 * z))
@@ -418,16 +419,17 @@ def rank_program(g, core, T, topo):
         for b in range(4):
             plain(engines[b], out(b), bank("PA", b, n))
 
-    def diagonal(scale):
-        for b in range(4):
-            act(A("et", 512 * b + b, 512 * b + 512, 4), A("ident"), scale=scale)
+    def constant(qn, sn, i, some=range(4)):
+        for b in some:
+            quant(qn, sn, 128 * b, 128, A("et", EW * i + 3 - b, EW * i + 515 - b))
 
     def tile(name, i):
         return lambda b: A(name, 512 * i + b, 512 * i + 512, 4)
 
     def level(l):
         a = 2 - l
-        return A("es", 256 * a, 256 * a + 256), A("si", 16 * a, 16 * a + 16), A("ci", 16 * a, 16 * a + 16), A("pm", 128 * a + 7, 128 * a + 128, 8)
+        return (A("es", 256 * a, 256 * a + 256), A("si", SEG * a, SEG * a + 16), A("ci", SEG * a, SEG * a + 16),
+                A("pm", 8 * SEG * a + 7, 8 * SEG * a + 128, 8))
 
     def sort_entries(l):
         a = 2 - l
@@ -435,37 +437,55 @@ def rank_program(g, core, T, topo):
             act(A("es", 256 * a + M * k, 256 * a + M * k + M), A("eexp"), Act.Identity, off=A("pn", 16 * a + 8 * k, 16 * a + 8 * k + 8),
                 bias=float(C * k + 1))
 
-    def slots(l):
-        es, si, ci, O = level(l)
-        a = 2 - l
-        x, W = ("%s", "x%s1")[a], NP * SEG
-        o, vi = W * a, A("vi", 16 * a, 16 * a + 16)
-        fill(A("oh", o, o + W, SEG), 0.0)
-        cp(vi, to_table(es, 256, C * a))
-        ts(si, vi, 10, Op.arith_shift_right)
-        ts(ci, vi, RK - 1, Op.bitwise_and)
+    def slots():
+        W = 2 * SEG
+        two = [to_table(level(2 - a)[0], 256, C * a) for a in range(2)]
+        for a in range(2):
+            ts(A("vi", SEG * a, SEG * a + 16), two[a], EXTRA, Op.subtract)
+        quant("wfq", "wfs", FY, M, A("ti", 0, 512))
+        ts(A("si", 0, W - 1), A("vi", 0, W - 1), 10, Op.arith_shift_right)
+        ts(A("ci", 0, W - 1), A("vi", 0, W - 1), RK - 1, Op.bitwise_and)
         for i in range(NP):
-            ts(A("oh", o + SEG * i + 1, o + SEG * i + SEG), si, float(ps[i] + 1), Op.is_equal)
-        scan(A("c1", o, o + W), A("rs"), A("oh", o, o + W))
-        cp(A(x % "tot", 0, NP), A("c1", o + SEG - 1, o + W, SEG))
-        across(NP, NP * a, x)
-        tt(A("oh", o, o + W, SEG), A(x % "tb", 0, NP), A(x % "kt", 0, NP), Op.add)
-        scan(A("c2", o, o + W), A("rs"), A("oh", o, o + W))
+            ts(A("oh", W * i + 1, W * i + W), A("si", 0, W - 1), float(ps[i] + 1), Op.is_equal)
+        named(0)
+        scan(A("c1"), A("rs"), A("oh"))
+        named(1)
+        cp(A("tot", 0, 2 * NP), A("c1", SEG - 1, None, SEG))
+        named(2)
+        across(2 * NP, 0)
+        named(3)
+        tt(A("oh", 0, None, SEG), A("tb", 0, 2 * NP), A("kt", 0, 2 * NP), Op.add)
+        named(4)
+        scan(A("c2"), A("rs"), A("oh"))
         for i in range(NP):
-            b = o + SEG * i
-            tt(A("prod", 128 * a + i, 128 * a + 128, 8), A("oh", b + 1, b + SEG), A("c2", b + 1, b + SEG), Op.mult)
-        scan(A("pm", 128 * a, 128 * a + 128), A("rp"), A("prod", 128 * a, 128 * a + 128), Op.max)
-        cp(A("ou", 16 * a, 16 * a + 16), O)
+            tt(A("prod", i, None, 8), A("oh", W * i + 1, W * i + W), A("c2", W * i + 1, W * i + W), Op.mult)
+        scan(A("pm"), A("rp"), A("prod"), Op.max)
+        for a in range(2):
+            cp(A("ou", 16 * a, 16 * a + 16), level(2 - a)[3])
+
+    def named(step):
+        if step < 2:
+            a = 8 * step
+            ts(A("a1", a, a + 8), A("si", SEG + a, SEG + a + 8), float(C), Op.mult, float(-C * (step + 1)), Op.add)
+        elif step == 2:
+            tt(A("a2", 0, 16), A("a1", 0, 16), level(1)[2], Op.add)
+        else:
+            cp(A("u2", step - 3, 32, 2), A("a2", 0, 16))
 
     def fill_slots(l):
         scat(A("rw"), A("ou", 16 * (2 - l), 16 * (3 - l)), level(l)[0])
 
     def tables(l):
         a, b, at = "req%d" % l, "rin%d" % l, NE + SL * (2 - l)
-        cp(A(a, 0, 21), to_table(A("rw", at, at + SL), SL))
+        ts(A(a, 0, 21), to_table(A("rw", at, at + SL), SL), EXTRA, Op.subtract)
 
         def go():
             before("g", [A(a)], [])
+            if l == 2:
+                for part in spread(T, topo, r):
+                    call([(T.cores[ps[i]], es, "ar_r2", ap(A(a, 3 * i, 3 * i + 3)), ap(A(b, 3 * back(i), 3 * back(i) + 3))) for i, es in part])
+                note("x", [], [A(b)], "ar_r2", n_direct)
+                return
             for h in range(3):
                 call([(hs[h], rest, "ar_hr%d" % l, ap(A(a, 6 * h, 6 * h + 6)), ap(A("hr%d" % l)))])
             call([(T.cores[ps[-1]], rest, "ar_r%d" % l, ap(A(a, 18, 21)), ap(A(b, 18, 21)))])
@@ -488,9 +508,8 @@ def rank_program(g, core, T, topo):
 
     def sent_from(l):
         a = NE + SL * (2 - l)
-        return (lambda: tt(A("m1", C, C + SL), A("w2", a, a + SL), A("mask", 0, SL), Op.mult),
-                lambda: scan(A("m2", C, C + SL), A("r16", 0, SL), A("m1", C, C + SL)),
-                lambda: ts(A("h%d" % l, 0, 21), A("m2", C + 15, C + SL, 16), float(-M * l), Op.add, 0.0, Op.max))
+        return (lambda: to_table(A("w2", a, a + SL), SL, C),
+                lambda: ts(A("h%d" % l, 0, 21), A("m2", C + 15, C + SL, 16), A("pf", 3 + l, 4 + l), Op.subtract, 0.0, Op.max))
 
     def successors(l):
         ts(A("xb3", 0, 21), A("rin%d" % l, 0, 21), float(SL - 1 - RK * (r + 1)), Op.add)
@@ -510,45 +529,51 @@ def rank_program(g, core, T, topo):
     iota(A("pc", 0, 1), [[0, 1]], 0, 1)
     iota(A("kc", 14, 17), [[M, 3]], -1)
     iota(A("nm"), [[0, C // 16], [1, 16]], 0)
-    run("g", [A("ones")], [A("ident")], lambda: g.affine_select(T.ident[:], T.ones[:], [[-1, 128]], Op.is_equal, 0.0, 0, 1))
     iota(A("nt0"), [[16, 24]], 0)
-    fill(A("et"), 0.0)
+    run("g", [A("ones")], [A("et", 0, EW)], lambda: g.affine_select(ap(A("et", 0, EW)), T.ones[:], [[-1, EW]], Op.is_equal, 0.0, 3, 4))
     for name, step in (("lrs", LSEG), ("rt", 16), ("rs", SEG), ("rp", 8)):
         fill(A(name), 1.0)
     fill(A("tot"), 0.0)
-    fill(A("xtot1"), 0.0)
     fill(A("loh", 0, None, LSEG), 0.0)
+    fill(A("oh", 0, None, SEG), 0.0)
+    fill(A("vi"), 0)
+    fill(A("ew", 0, 1), float(RK * (N + 1)))
     for name, step in (("lrs", LSEG), ("rt", 16), ("rs", SEG), ("rp", 8)):
         fill(A(name, 0, None, step), 0.0)
     ts(A("pc", 1, 2), A("pc", 0, 1), 15, Op.bitwise_and)
     ts(A("pc", 2, 3), A("pc", 0, 1), 16, Op.bitwise_and)
-    ts(A("pf", 1, 2), A("pc", 1, 2), -1.0, Op.mult)
+    ts(A("pf", 1, 2), A("pc", 1, 2), -1.0, Op.mult, -0.5, Op.add)
+    cp(A("pf", 0, 1), A("pc", 1, 2))
+
+    def extra(l):
+        ts(A("pf", 3 + l, 4 + l), A("pc", 1, 2), float(-BIG), Op.mult, float(15 * BIG + M * l), Op.add)
 
     def ranks(some):
         for s in some:
             act(A("ew", 1 + C * s, 1 + C * s + C), A("iot"), Act.Identity, bias=float(RK * (s + 1)))
     ranks(range(0, 3))
-    act(A("ma"), A("nm"), Act.Abs, bias=A("pf", 1, 2))
-    act(A("r16"), A("nm"), Act.Sign)
-    act(A("mask"), A("ma"), Act.Relu, bias=1.0, scale=-1.0)
-    diagonal(None)
+    act(A("ma"), A("nm"), Act.Sign, bias=A("pf", 1, 2))
+    act(A("keep"), A("ma"), Act.Identity, bias=-15.5 * BIG, scale=16.5 * BIG)
     ranks(range(3, N))
 
     for l in range(3):
         ts(A("loh", LSEG * l + 1, LSEG * l + LSEG), A("lvt"), float(l), Op.is_equal)
     scan(A("lc1"), A("lrs"), A("loh"))
-    cp(A("pf", 0, 1), A("pc", 1, 2))
-    cp(A("tot", 0, 3), A("lc1", LSEG - 1, None, LSEG))
     ts(A("pe", 0, 1), A("pc", 2, 3), 0.03125, Op.mult, -0.5, Op.add)
-    across(3, 14)
+    cp(A("tot", 0, 3), A("lc1", LSEG - 1, None, LSEG))
     ts(A("pe", 1, 2), A("pc", 2, 3), -0.03125, Op.mult)
-    tt(A("loh", 0, None, LSEG), A("tb", 0, 3), A("kt", 0, 3), Op.add)
-    fill(A("ew", 0, 1), float(RK * (N + 1)))
-    scan(A("lc2"), A("lrs"), A("loh"))
+    across(3, 14)
     ts(A("u1"), A("e"), 1.0, Op.add)
+    tt(A("loh", 0, None, LSEG), A("tb", 0, 3), A("kt", 0, 3), Op.add)
+    ts(A("nt"), A("nt0"), A("pf", 0, 1), Op.add)
+    scan(A("lc2"), A("lrs"), A("loh"))
+    ts(A("prod", 7, 8 * SEG, 8), A("nt0", 0, SEG), A("pf", 0, 1), Op.add)
     tt(A("lc1"), A("loh"), A("lc2"), Op.mult)
+    ts(A("prod", 8 * SEG + 7, None, 8), A("nt0", 0, 16), A("pf", 0, 1), Op.add)
     tt(A("pos"), A("lc1", 1, LSEG), A("lc1", LSEG + 1, 2 * LSEG), Op.add)
+    extra(0)
     tt(A("pos"), A("pos"), A("lc1", 2 * LSEG + 1, 3 * LSEG), Op.add)
+    extra(1)
     cp(A("posu"), A("pos"))
     before("g", [A("posu")], [])
     PSEM = ["ar_pa"] * 4 + ["ar_pb"] * 2 + ["ar_pc"]
@@ -557,71 +582,82 @@ def rank_program(g, core, T, topo):
     for i in range(NP):
         sem = PSEM[direct[i][0]]
         note("x", [], [A("pin", 24 * i, 24 * i + 24)], sem, sum(n for j, n in direct if PSEM[j] == sem))
-    iota(A("kc", 0, 14), [[CAP, 14]], NE - 1)
-    iota(A("rw", NE), [[0, NS]], 0)
-    iota(A("uw", 0, 1), [[0, 1]], FZ)
-    iota(A("uw", UM), [[1, SL]], FL2)
+    iota(A("kc", 0, 14), [[CAP, NP], [SL, 2]], NE - 1)
+    extra(2)
     scat(A("pw"), A("posu"), A("iot"))
     quant("sq", "ss", 0, C, A("xt"))
-    tt(A("m1", 0, C), A("pw"), A("mask"), Op.mult)
-    quant("e1q", "e1s", 0, 512, A("et"))
-    scan(A("m2", 0, C), A("r16"), A("m1", 0, C))
+    first = to_table(A("pw", 0, M), M)
     PERM = A("m2", 15, C, 16)
-    act(A("eexp"), A("ew"), off=A("u1"))
-    cp(A("permu"), PERM)
+    act(A("eexp", 0, C), A("ew"), off=A("u1", 0, 24))
+    fill(A("uw", 0, UM, UM - 1), float(FZ))
+    ts(A("permu", 0, 8), first, EXTRA, Op.subtract)
+    constant("e1q", "e1s", 0, [0])
 
     pick("spq", "sps", 0, "sq", "ss", C, A("permu", 0, 8))
+    act(A("eexp", C, NE), A("ew"), off=A("u1", 24, 48))
+    constant("e1q", "e1s", 0, [1, 2, 3])
+    to_table(A("pw", M, C), C - M, M)
+    decode("spq", "sps", 0, M, tile("xs", 6), "vsvs")
     for l in (2, 1):
         for k in range(2):
             a = 16 * (2 - l) + 8 * k
-            ts(A("pn", a, a + 8), A("m2", M * l + 15, M * l + M, 16), float(C * k), Op.add)
-    decode("spq", "sps", 0, M, tile("xs", 6), "vsvs")
+            ts(A("pn", a, a + 8), A("m2", M * l + 15, M * l + M, 16), EXTRA, Op.subtract, float(C * k), Op.add)
+            if a == 8:
+                quant("xq", "xp", 128 * 6, M, A("xs", 512 * 6, 512 * 7))
     sort_entries(2)
-    quant("xq", "xp", 128 * 6, M, A("xs", 512 * 6, 512 * 7))
-    ts(A("nt"), A("nt0"), A("pf", 0, 1), Op.add)
-    for a in range(2):
-        ts(A("prod", 128 * a + 7, 128 * a + 128, 8), A("nt0", 0, 16), A("pf", 0, 1), Op.add)
-    ev = layer("wq", "wp", 6, tile("ti", 0))
+    ev = layer("wq", "wp", 6, tile("ti", 0), "vsvv")
+    ts(A("permu", 8, 24), A("m2", M + 15, C, 16), EXTRA, Op.subtract)
     for k in range(2):
         for h in range(2):
-            ts(A("pd", 48 * k + h, 48 * k + 48, 2), PERM, float(C * k), Op.add)
+            ts(A("pd", 48 * k + h, 48 * k + 48, 2), PERM, EXTRA, Op.subtract, float(C * k), Op.add)
     for f in ev:
         f()
+    sort_entries(1)
     quant("sdq1", "sds1", 0, M, A("ti", 0, 512))
     exchange(1)
+    iota(A("rw", NE), [[0, NS]], 0)
     iota(A("zt"), [[0, 512]], 0)
-    iota(A("pl"), [[-M, 2], [0, 2], [1, M]], 2 * M)
 
     def place(i):
         s, off = (r, A("posu")) if i == NP else (ps[i], A("pin", 24 * i, 24 * i + 24))
         act(A("uw", 1 + C * s, 1 + C * s + C), A("iot"), Act.Identity, off=off, bias=float(M * i))
-    sort_entries(1)
-    diagonal(A("pe", 0, 1))
     place(NP)
-    for k in range(2):
-        act(A("pp", C * k, C * k + C), A("iot"), off=A("posu"))
-    for b in range(4):
-        act(A("yp", 256 * b, 256 * b + M), tile("ti", 0)(b))
     for i in sorted(range(NP), key=lambda i: (direct[i][0] != NP - 1, direct[i][0])):
         place(i)
-    act(A("uexp"), A("uw", 0, UM), off=A("u1"))
-    spread_lists(A("uexp"), 1)
-    rest1 = weave(lambda: (slots(2), fill_slots(2), tables(2), quant("eeq", "ees", 0, 512, A("et")), diagonal(A("pe", 1, 2)),
-                           pick("spq", "sps", M, "sq", "ss", C, A("permu", 8, 24))), lambda: slots(1), keep=True)
+    slots()
+    act(A("gx"), A("uw", 0, UM), off=A("u2"))
+
+    def halves():
+        for i in range(2):
+            ts(A("et", EW * (i + 1), EW * (i + 2)), A("et", 0, EW), A("pe", i, i + 1), Op.mult)
+    weave(lambda: (fill_slots(2), tables(2)), halves)
+    iota(A("uw", UM), [[1, SL]], FL2)
+    iota(A("pl"), [[-M, 2], [0, 2], [1, M]], 2 * M)
     iota(A("w2", NE, NE + NS), [[0, NS]], 0)
     iota(A("w2", SU0), [[0, NE]], BZ)
-    iota(A("sud"), [[1, NS]], BL3)
+    pick("spq", "sps", M, "sq", "ss", C, A("permu", 8, 24))
+    quant("wfq", "wfs", FZ, M, A("zt"))
+    trn(A("gt"), A("gx"))
     decode("spq", "sps", M, 256, lambda b: A("ds", 256 * b, 256 * b + 256))
-    weave(lambda: held[0].extend(rest1), lambda: (quant("wfq", "wfs", FY, M, A("ti", 0, 512)), quant("wfq", "wfs", FZ, M, A("zt")),
-                                                  pair_lists("f1"), quant("eoq", "eos", 0, 512, A("et"))))
+    constant("eeq", "ees", 1)
+    cp(A("f1", 0, 16), A("gt", 0, 512, 32))
+    cp(A("f1", 16, 32), A("gt", 16, 512, 32))
+    constant("eoq", "eos", 2)
 
-    gathered(1, "wf", FL2, "f1", "ds", 0, 256, 0)
-    ev = layer("wq", "wp", 0, lambda b: A("yp", 256 * b + M, 256 * b + 256))
+    def own():
+        for k in range(2):
+            act(A("pp", C * k, C * k + C), A("uw", 1 + C * r, 1 + C * r + C), Act.Identity, bias=float(-M * NP))
+        for b in range(4):
+            plain("vs"[b % 2], A("yp", 256 * b, 256 * b + M), tile("ti", 0)(b))
+    gathered(1, "wf", FL2, "f1", "ds", 0, 256, 0, own)
+    ev = layer("wq", "wp", 0, lambda b: A("yp", 256 * b + M, 256 * b + 256), "vvvs")
     ts(A("c2u", 0, 21), A("rin2", 0, 21), float(-1 - RK * (r + 1)), Op.add, 0.0, Op.max)
-    tt(A("m1", 0, SL), A("pp"), A("mask", 0, SL), Op.mult, off=A("c2u", 0, 21))
-    scan(A("m2", 0, SL), A("r16", 0, SL), A("m1", 0, SL))
-    ts(A("g2", 0, 21), A("m2", 15, SL, 16), float(2 * M - 1), Op.min)
-    send(2, ev, lambda b: A("yp", 256 * b, 256 * b + 256), "g2")
+    act(A("m1", 0, SL), A("pp"), off=A("c2u", 0, 21))
+    for f in ev:
+        f()
+    ts(A("g2", 0, 21), to_table(A("m1", 0, SL), SL), EXTRA, Op.subtract, float(2 * M - 1), Op.min)
+    send(2, (), lambda b: A("yp", 256 * b, 256 * b + 256), "g2")
+    iota(A("sud"), [[1, NS]], BL3)
 
     def places():
         es, si, ci, O = level(2)
@@ -648,7 +684,6 @@ def rank_program(g, core, T, topo):
     for f in ev:
         f()
     quant("xq", "xp", 256, M, A("xs", 1024, 1536))
-    steps[2]()
     decode("xq", "xp", 256, M, tile("xs", 3), "vsvs")
     quant("xq", "xp", 384, M, A("xs", 1536, 2048))
     ev = layer("vq", "vp", 3, lambda b: A("zp", 128 * b, 128 * b + M))
@@ -663,10 +698,9 @@ def rank_program(g, core, T, topo):
           lambda: (quant("wbq", "wbs", BZ, M, A("zt")), quant("wbq", "wbs", 2 * M, M, A("ti", 1024, 1536)), pair_lists("b1")))
 
     steps = sent_from(1)
-    steps[0]()
-    gathered(3, "wb", BL4, "b1", "dy", M, 256, 4, steps[1])
+    gathered(3, "wb", BL4, "b1", "dy", M, 256, 4, steps[0])
     ev = layer("vq", "vp", 4, lambda b: A("zp", 512 + 128 * b, 512 + 128 * b + M))
-    steps[2]()
+    steps[1]()
     send(4, ev, lambda b: A("zp", 512 + 128 * b, 512 + 128 * b + M), "h1")
 
     successors(1)

@@ -1,21 +1,31 @@
 from concourse.bass import DstId, RemoteDMATransfer
-from concourse.mybir import dt, AluOpType as Op, ActivationFunctionType as Act
+from concourse.mybir import dt, AluOpType as Op, ActivationFunctionType as Act, AxisListType
 
 N, C, M, CAP, NP = 8, 384, 128, 48, 7
 SL = CAP * NP
-CHUNK = True
 F32, BF, I32, U16, Q4, U8 = "float32", "bfloat16", "int32", "uint16", "float8_e4m3fn_x4", "uint8"
-FY, FZ, FL2, FW = NP * M, NP * M + 2 * M, NP * M + 3 * M, NP * M + 3 * M + SL
+FY, FZ, FL2, FL1 = NP * M, NP * M + 2 * M, NP * M + 3 * M, NP * M + 3 * M + SL
+FW = FL1 + NP * M
+WHOLE = 4
 BZ, BL3, BL4, BW = 384, 512, 512 + SL, 512 + 2 * SL
 NE, NS = 2 * C, 2 * SL
 SEG, LSEG = 17, 25
 UM = 2 + N * C
 EW = 528
-RK = 1024
-BIG = 16 * RK
+RK = 800
+LOW = 8192
+BIG = 256 * LOW
+SH = 128 - 8 * BIG
+RND = 12582912.0
 SU0 = NE + NS + SL
-WIDE = {1: M, 2: CAP, 3: CAP, 4: CAP}
-LAND = {1: ("wf", 0), 2: ("wf", FL2), 3: ("wb", BL3), 4: ("wb", BL4)}
+VIA = (1, 2)
+LAND = {1: ("wf", 0, FY), 2: ("wf", FL2, FW), 3: ("wb", BL3, BL4), 4: ("wb", BL4, BW)}
+
+
+def lot(k, i):
+    if k == 1 or k == 2 and i < WHOLE:
+        return "sw%%s%d" % k, 0, M, FL1 * (k - 1)
+    return "sd%%s%d" % k, CAP * (i - WHOLE * (k == 2)), CAP, LAND[k][1]
 
 
 def _sb(n, d):
@@ -23,45 +33,46 @@ def _sb(n, d):
 
 
 SMALL = {}
-for _n in ("tot", "tt", "ts", "tb", "rt", "kc", "kt", "pos", "nt0", "nt", "a1", "a2", "a3", "a4", "a5"):
+for _n in ("tot", "tt", "ts", "tb", "rt", "kc", "kt", "pos", "nt0", "nt", "a1", "a2", "a3", "a4", "a5", "xb3"):
     SMALL[_n] = (32 * len(SMALL), 32 if len(SMALL) < 7 else 24)
-for _n in ("b1", "b2", "b3"):
-    SMALL["x" + _n] = (32 * len(SMALL), 32)
 
 SCRATCH = {
-    "sm": _sb(32 * len(SMALL), F32), "e": _sb(48, I32), "lvt": _sb(24, I32), "iot": _sb(C, F32),
-    "ew": _sb(UM - 1, F32), "eexp": _sb(NE, F32), "es": _sb(512, F32), "vi": _sb(34, I32), "si": _sb(34, I32), "ci": _sb(34, I32),
-    "oh": _sb(2 * NP * SEG, F32), "rs": _sb(2 * NP * SEG, F32), "c1": _sb(2 * NP * SEG, F32), "c2": _sb(2 * NP * SEG, F32),
-    "prod": _sb(264, F32), "rp": _sb(264, F32), "pm": _sb(264, F32),
+    "sm": _sb(32 * len(SMALL), F32), "e": _sb(48, I32), "lvt": _sb(24, I32), "iot": _sb(C, F32), "io2": _sb(C, F32),
+    "ew": _sb(UM - 1, F32), "eexp": _sb(NE, F32), "es": _sb(512, F32), "vi": _sb(34, F32), "si": _sb(34, F32), "ci": _sb(34, F32),
+    "val": _sb(512, F32), "on": _sb(34, F32), "pv": _sb(34, F32), "pu": _sb(34, F32), "lo": _sb(48, I32),
+    "oh": _sb(2 * NP * SEG, F32), "rs": _sb(2 * NP * SEG, BF), "c1": _sb(2 * NP * SEG, F32), "c2": _sb(2 * NP * SEG, F32),
+    "prod": _sb(264, F32), "rp": _sb(264, BF), "pm": _sb(264, F32),
     "loh": _sb(3 * LSEG, F32), "lrs": _sb(3 * LSEG, F32), "lc1": _sb(3 * LSEG, F32), "lc2": _sb(3 * LSEG, F32),
     "ou": _sb(32, U16), "pp": _sb(NE, F32), "posu": _sb(24, U16), "pin": _sb(24 * NP, U16), "pc": _sb(4, I32), "pf": _sb(8, F32),
-    "nm": _sb(C, BF), "ma": _sb(C, BF), "keep": _sb(C, BF),
-    "rw": _sb(NE + NS, F32), "m1": _sb(C, F32), "m2": _sb(2 * C, F32),
-    "req1": _sb(24, F32), "req2": _sb(24, F32), "rin1": _sb(24, F32), "rin2": _sb(24, F32), "hr1": _sb(6, F32),
-    "c2u": _sb(22, U16), "g2": _sb(22, U16), "h1": _sb(22, U16), "h2": _sb(22, U16),
+    "nm": _sb(C, BF), "ma": _sb(C, BF), "keep": _sb(C, BF), "m2": _sb(2 * C, F32),
+    "req1": _sb(24, I32), "req2": _sb(24, I32), "rin1": _sb(24, I32), "rin2": _sb(24, I32), "hi": _sb(24, I32), "hp": _sb(24, U16),
+    "c2u": _sb(22, U16), "g2": _sb(40, U16), "h1": _sb(22, U16), "h2": _sb(22, U16),
     "pw": _sb(C, F32), "permu": _sb(24, U16), "pd": _sb(96, U16), "pn": _sb(32, U16),
-    "u1": _sb(48, U16), "u2": _sb(32, U16), "o2u": _sb(16, U16), "uw": _sb(UM + SL, F32),
+    "u1": _sb(48, U16), "u2": _sb(32, U16), "uw": _sb(UM + SL, F32),
     "gx": _sb(512, F32), "gt": _sb(512, F32), "f1": _sb(32, U16), "f2": _sb(32, U16), "b1": _sb(32, U16), "b0": _sb(32, U16),
     "pl": _sb(512, F32), "w2": _sb(SU0 + NE, F32), "sud": _sb(NS, F32), "suu": _sb(22, U16),
     "ones": _sb(EW, BF), "et": _sb(3 * EW, BF), "zt": _sb(512, BF), "pe": _sb(2, F32),
     "e1q": _sb(512, Q4), "e1s": _sb(512, U8), "eeq": _sb(512, Q4), "ees": _sb(512, U8), "eoq": _sb(512, Q4), "eos": _sb(512, U8),
     "xt": _sb(4 * C, BF), "ut": _sb(512, BF), "sq": _sb(C, Q4), "ss": _sb(C, U8), "uq": _sb(128, Q4), "us": _sb(128, U8),
-    "wq": _sb(512, Q4), "wp": _sb(512, U8), "vq": _sb(512, Q4), "vp": _sb(512, U8), "yp": _sb(4 * 256, BF),
+    "wq": _sb(512, Q4), "wp": _sb(512, U8), "vq": _sb(512, Q4), "vp": _sb(512, U8),
     "wfq": _sb(FW, Q4), "wfs": _sb(FW, U8), "wbq": _sb(BW, Q4), "wbs": _sb(BW, U8),
     "spq": _sb(C, Q4), "sps": _sb(C, U8), "ds": _sb(1024, BF), "dy": _sb(1024, BF),
     "xs": _sb(7 * 512, BF), "xq": _sb(7 * 128, Q4), "xp": _sb(7 * 128, U8), "ti": _sb(5 * 512, BF), "zp": _sb(1024, BF),
-    "st": _sb(3 * 4 * SL, BF), "oq": _sb(C, Q4), "opl": _sb(C, U8), "yo": _sb(C, F32),
+    "st": _sb(3 * 4 * SL, BF), "oq": _sb(C, Q4), "opl": _sb(C, U8), "ys": _sb(C, F32), "yo": _sb(C, F32),
     "PA": ("psum", [128, 2048], F32), "PB": ("psum", [128, 2048], F32),
 }
 for _k in range(1, 5):
     SCRATCH["pk%d" % _k] = _sb(512, Q4)
     SCRATCH["ps%d" % _k] = _sb(512, U8)
-    SCRATCH["sdq%d" % _k] = _sb(M if _k == 1 else SL, Q4)
-    SCRATCH["sds%d" % _k] = _sb(M if _k == 1 else SL, U8)
-    SCRATCH["hs%d" % _k] = _sb(M if _k == 1 else 2 * CAP, U8)
+    for _n, _w in [("sw", M)] * (_k < 3) + [("sd", SL)] * (_k > 1):
+        SCRATCH["%sq%d" % (_n, _k)] = _sb(_w, Q4)
+        SCRATCH["%ss%d" % (_n, _k)] = _sb(_w, U8)
+    SCRATCH["hs%d" % _k] = _sb(M, U8)
+for _k in VIA:
+    SCRATCH["hc%d" % _k] = _sb(M, Q4)
 SEMAPHORES = ["q_v", "q_s", "q_t", "q_g", "sent", "ld_l", "ld_e", "ld_x", "ld_w", "ld_v", "ld_u", "st_c", "st_s", "st_y",
-              "ar_pa", "ar_pb", "ar_pc", "ar_r1", "ar_r2", "ar_hr1"] + \
-    ["ar_c%d" % k for k in range(1, 5)] + ["ar_s%d" % k for k in range(1, 5)] + ["ar_h%d" % k for k in range(1, 5)]
+              "ar_pa", "ar_pb", "ar_pc", "ar_pd", "ar_hp", "ar_r1", "ar_r2", "ar_t1", "ar_t2"] + \
+    ["ar_%s%d" % (_n, _k) for _k in range(1, 5) for _n in "csh"] + ["ar_g%d" % _k for _k in VIA]
 
 
 def peers_of(T, topo, r):
@@ -100,12 +111,33 @@ def engine_sets(T, topo, r):
 def spread(T, topo, r, k=1):
     off, rest = engine_sets(T, topo, r)
     one, two, near = list(enumerate(parts(off, 4))), [(4 + i, es) for i, es in enumerate(parts(off, 2))], [(NP - 1, rest)]
-    return (one, two + near) if CHUNK and k > 1 else (one + near, two)
+    return (one, two + near) if k > 1 else (one + near, two)
 
 
 def helper_engines(T, topo, r, k):
     off, rest = engine_sets(T, topo, r)
-    return parts(rest, 2) + [rest if CHUNK and k > 1 else off]
+    return parts(rest, 2) + [rest if k > 1 else off]
+
+
+def handed(T, topo, r, h):
+    ps, core = peers_of(T, topo, r), helpers_of(T, topo, r)[h]
+    return [(2 * h + j, es) for j, es in enumerate(parts(topo.engines(core, T.cores[ps[2 * h]]), 2))]
+
+
+def far_helper(T, topo, s, h):
+    d = [d for d in peers_of(T, topo, s)[2 * h:2 * h + 2] if topo.die(T.cores[d]) == topo.die(T.cores[s])][0]
+    return helpers_of(T, topo, d)[h]
+
+
+def on_chip(T, topo, r, h):
+    return list(zip((r, peers_of(T, topo, r)[-1]), parts(topo.engines(helpers_of(T, topo, r)[h], T.cores[r]), 2)))
+
+
+def code_plan(T, topo, r, k):
+    one, two = [[(i, None, es) for i, es in p] for p in spread(T, topo, r, k)]
+    if k in VIA:
+        one = [(None, h, es) for h, es in enumerate(parts(engine_sets(T, topo, r)[0], 2))] + one[WHOLE:]
+    return one, two
 
 
 def arrivals(T, topo, r):
@@ -113,9 +145,8 @@ def arrivals(T, topo, r):
     for s in peers_of(T, topo, r):
         i = peers_of(T, topo, s).index(r)
         one, two = spread(T, topo, s)
-        n = [len(es) for j, es in one + two if j == i][0]
-        direct.append((i, n))
-        relayed += len(topo.engines(helpers_of(T, topo, s)[i // 2], T.cores[r])) // 2 if i < NP - 1 else n
+        direct.append((i, [len(es) for j, es in one + two if j == i][0]))
+        relayed += ([len(es) for h in range(3) for j, es in handed(T, topo, s, h) if j == i] + [direct[-1][1]])[0]
     return direct, relayed
 
 
@@ -127,24 +158,33 @@ def dst(topo, c):
 def helper_program(g, core, T, topo, r, h):
     ps = peers_of(T, topo, r)
     sent = 0
-    for kind, k in (("s", 1), ("s", 2), ("s", 3), ("r", 1), ("s", 4)):
-        if kind == "s":
-            (name, base), w = LAND[k], WIDE[k]
-            here, there, sem, step = "hs%d" % k, name + "s", "ar_s%d" % k, 0 if k == 1 else w
-            g.wait_ge(T.sem["ar_h%d" % k], len(helper_engines(T, topo, r, k)[h]))
-        else:
-            base, w = 0, 3
-            here, there, sem, step = "hr%d" % k, "rin%d" % k, "ar_r%d" % k, w
-            g.wait_ge(T.sem["ar_hr%d" % k], len(engine_sets(T, topo, r)[1]))
+    if h < 2:
+        d = [d for d in ps[2 * h:2 * h + 2] if topo.die(T.cores[d]) != topo.die(core)][0]
+        es, at = topo.engines(core, T.cores[d]), 24 * peers_of(T, topo, d).index(r)
+        g.wait_ge(T.sem.ar_hp, len(helper_engines(T, topo, r, 1)[h]))
+        g.remote_dma_fused([RemoteDMATransfer(dst_ids=[dst(topo, T.cores[d])], dma_engine_mask=bits(es), remote_sem=T.sem.ar_pd,
+                                              src=T.hp[:], dst=T.pin[:, at:at + 24])], local_sem=T.sem.sent)
+        sent += len(es)
+    for k in range(1, 5):
+        w, base = lot(k, 2 * h)[2:]
+        g.wait_ge(T.sem["ar_h%d" % k], len(helper_engines(T, topo, r, k)[h]))
         tr = []
-        for j in range(2):
-            d = ps[2 * h + j]
-            es = parts(topo.engines(core, T.cores[d]), 2)[j]
-            at = base + w * peers_of(T, topo, d).index(r)
-            tr.append(RemoteDMATransfer(dst_ids=[dst(topo, T.cores[d])], dma_engine_mask=bits(es), remote_sem=T.sem[sem],
-                                        src=T[here][:, step * j:step * j + w], dst=T[there][:, at:at + w]))
+        for i, es in handed(T, topo, r, h):
+            a, at = 0 if w == M else w * (i % 2), base + w * peers_of(T, topo, ps[i]).index(r)
+            tr.append(RemoteDMATransfer(dst_ids=[dst(topo, T.cores[ps[i]])], dma_engine_mask=bits(es), remote_sem=T.sem["ar_s%d" % k],
+                                        src=T["hs%d" % k][:, a:a + w], dst=T[LAND[k][0] + "s"][:, at:at + w]))
             sent += len(es)
         g.remote_dma_fused(tr, local_sem=T.sem.sent)
+        if k in VIA and 2 * h < WHOLE:
+            s = [s for s in ps[:NP - 1] if far_helper(T, topo, s, h) == core][0]
+            g.wait_ge(T.sem["ar_g%d" % k], len(code_plan(T, topo, s, k)[0][h][2]))
+            tr = []
+            for d, es in on_chip(T, topo, r, h):
+                at = base + M * peers_of(T, topo, d).index(s)
+                tr.append(RemoteDMATransfer(dst_ids=[dst(topo, T.cores[d])], dma_engine_mask=bits(es), remote_sem=T.sem["ar_c%d" % k],
+                                            src=T["hc%d" % k][:].bitcast(dt.uint8), dst=T.wfq[:, at:at + M].bitcast(dt.uint8)))
+                sent += len(es)
+            g.remote_dma_fused(tr, local_sem=T.sem.sent)
     g.wait_ge(T.sem.sent, sent)
 
 
@@ -249,8 +289,8 @@ def rank_program(g, core, T, topo):
     def scat(o, off, i):
         run("v", [i, off], [o], lambda: g.vector.tensor_copy(ap(o).indirect(ap(off)), ap(i)))
 
-    def tt(o, a, b, op, off=None):
-        run("v", [a, b] + ([off] if off else []), [o], lambda: g.vector.tensor_tensor(ap(o), src(a, off), ap(b), op))
+    def tt(o, a, b, op):
+        run("v", [a, b], [o], lambda: g.vector.tensor_tensor(ap(o), ap(a), ap(b), op))
 
     def ts(o, a, s1, op0, s2=None, op1=None):
         r1, x1 = col(s1)
@@ -259,8 +299,11 @@ def rank_program(g, core, T, topo):
         else:
             run("v", [a] + r1, [o], lambda: g.vector.tensor_scalar(ap(o), ap(a), x1, s2, op0, op1))
 
-    def scan(o, reset, d, op1=Op.add, op0=Op.mult):
-        run("v", [reset, d], [o], lambda: g.vector.tensor_tensor_scan(ap(o), ap(reset), ap(d), 0.0, op0, op1))
+    def scan(o, reset, d, op1=Op.add, op0=Op.mult, first=0.0):
+        run("v", [reset, d], [o], lambda: g.vector.tensor_tensor_scan(ap(o), ap(reset), ap(d), first, op0, op1))
+
+    def summed(o, i):
+        run("v", [i], [o], lambda: g.vector.tensor_reduce(ap(o), ap(i), AxisListType.X, Op.add))
 
     def trn(o, i):
         run("v", [i], [o], lambda: g.vector.transpose(ap(o), ap(i)))
@@ -281,6 +324,10 @@ def rank_program(g, core, T, topo):
             run("g", [], [o], lambda: g.iota(ap(o), pat, base, cm))
         else:
             run("g", [], [o], lambda: g.iota(ap(o), pat, base, cm, allow_small_or_imprecise_dtypes=True))
+
+    def ones_where(o, pat, op, base, cm):
+        i = A("ones", 0, o[2] - o[1])
+        run("g", [i], [o], lambda: g.affine_select(ap(o), ap(i), pat, op, 0.0, base, cm))
 
     def quant(qn, sn, a, n, i):
         o, s = A(qn, a, a + n), A(sn, a, a + n)
@@ -315,37 +362,39 @@ def rank_program(g, core, T, topo):
         return peers_of(T, topo, ps[i]).index(r)
 
     direct, n_relayed = arrivals(T, topo, r)
-    n_direct = sum(n for i, n in direct)
-    rest = engine_sets(T, topo, r)[1]
+    off_chip, rest = engine_sets(T, topo, r)
 
     def exchange(k, piece=None):
-        name, base = LAND[k]
-        w = WIDE[k]
-        step = 0 if k == 1 else w
-        qn, sn = "sdq%d" % k, "sds%d" % k
-        one, two = spread(T, topo, r, k)
+        name, a0, z0 = LAND[k]
+        one, two = code_plan(T, topo, r, k)
         he = helper_engines(T, topo, r, k)
-        hw = SCRATCH["hs%d" % k][1][1]
+
+        def ends(i, kind):
+            n, a, w, base = lot(k, i)
+            return A(n % kind, a, a + w), A(name + kind, base + w * back(i), base + w * back(i) + w)
 
         def codes(part):
-            call([(T.cores[ps[i]], es, "ar_c%d" % k, u8(A(qn, step * i, step * i + w)),
-                   u8(A(name + "q", base + w * back(i), base + w * back(i) + w))) for i, es in part])
+            call([(T.cores[ps[i]], es, "ar_c%d" % k) + tuple(u8(v) for v in ends(i, "q")) if c is None else
+                  (far_helper(T, topo, r, c), es, "ar_g%d" % k, u8(ends(2 * c, "q")[0]), u8(A("hc%d" % k))) for i, c, es in part])
 
         def relay(which):
-            call([(hs[h], he[h], "ar_h%d" % k, ap(A(sn, 2 * step * h, 2 * step * h + hw)), ap(A("hs%d" % k))) for h in which])
-        a, b = {None: (0, None), 0: (0, 4 * w), 1: (4 * w, None)}[piece]
-        before("g", [A(qn, a, b), A(sn, a, b)], [])
+            items = []
+            for h in which:
+                n, a, w, base = lot(k, 2 * h)
+                w = w if w == M else 2 * w
+                items.append((hs[h], he[h], "ar_h%d" % k, ap(A(n % "s", a, a + w)), ap(A("hs%d" % k, 0, w))))
+            call(items)
+        before("g", [ends(i, kind)[0] for i in {None: range(NP), 0: range(4), 1: range(4, NP)}[piece] for kind in "qs"], [])
         relay({None: (0, 1, 2), 0: (0, 1), 1: (2,)}[piece])
         if piece != 1:
             codes(one)
         if piece == 0:
             return
         codes(two)
-        i = NP - 1
-        call([(T.cores[ps[i]], rest, "ar_s%d" % k, ap(A(sn, step * i, step * i + w)),
-               ap(A(name + "s", base + w * back(i), base + w * back(i) + w)))])
-        note("x", [], [A(name + "q", base, base + NP * w)], "ar_c%d" % k, n_direct)
-        note("x", [], [A(name + "s", base, base + NP * w)], "ar_s%d" % k, n_relayed)
+        call([(T.cores[ps[-1]], rest, "ar_s%d" % k) + tuple(ap(v) for v in ends(NP - 1, "s"))])
+        passed = len(on_chip(T, topo, r, 0)[0][1])
+        note("x", [], [A(name + "q", a0, z0)], "ar_c%d" % k, sum(passed if k in VIA and j < WHOLE else n for j, n in direct))
+        note("x", [], [A(name + "s", a0, z0)], "ar_s%d" % k, n_relayed)
 
     def bank(p, b, n):
         return A(p, 512 * b, 512 * b + n)
@@ -368,20 +417,17 @@ def rank_program(g, core, T, topo):
         scan(A("m2", a, a + n), A("keep", 0, n), w, Op.max, Op.add)
         return A("m2", a + 15, a + n, 16)
 
-    def across(n, k0):
-        trn(A("tt"), A("tot"))
-        tt(A("kt", 0, n), A("kc", k0, k0 + n), A("tot", 0, n), Op.subtract)
-        scan(A("ts"), A("rt"), A("tt"))
-        trn(A("tb"), A("ts"))
-
     def spread_lists(win, level):
         for k in range(2):
             act(A("gx", 256 * k, 256 * k + 256), win, off=A("pd", 48 * k + 16 * level, 48 * k + 16 * level + 16))
 
     def pair_lists(out):
         trn(A("gt"), A("gx"))
-        cp(A(out, 0, 16), A("gt", 0, 512, 32))
-        cp(A(out, 16, 32), A("gt", 16, 512, 32))
+        for h in range(2):
+            if out[0] == "f":
+                cp(A(out, 16 * h, 16 * h + 16), A("gt", 16 * h, 512, 32))
+            else:
+                ts(A(out, 16 * h, 16 * h + 16), A("gt", 16 * h, 512, 32), 1.0 / LOW, Op.mult, M - (SH + RK * (r + 1)) / LOW, Op.add)
 
     def gathered(k, name, wlen, lists, dn, d0, dw, slot, pause=None):
         pq, pp = "pk%d" % k, "ps%d" % k
@@ -404,10 +450,10 @@ def rank_program(g, core, T, topo):
         return [lambda b=b: scaled(engines[b], out(b), bank("PB", b, M)) for b in range(4)]
 
     def send(k, evac, win, lists):
-        at = 4 * SL * (k - 2)
-        for piece, (a, z) in ((0, (0, 12)), (1, (12, 21))) if CHUNK else ((None, (0, 21)),):
-            for f in evac if piece != 1 else ():
-                f()
+        at = 4 * SL * (k - 3)
+        for f in evac:
+            f()
+        for piece, (a, z) in enumerate(((0, 12), (12, 21))):
             for b in range(4):
                 plain("vs"[b % 2], A("st", at + 64 * a + b, at + 64 * z, 4), win(b), A(lists, a, z))
             quant("sdq%d" % k, "sds%d" % k, 16 * a, 16 * (z - a), A("st", at + 64 * a, at + 64 * z))
@@ -419,9 +465,8 @@ def rank_program(g, core, T, topo):
         for b in range(4):
             plain(engines[b], out(b), bank("PA", b, n))
 
-    def constant(qn, sn, i, some=range(4)):
-        for b in some:
-            quant(qn, sn, 128 * b, 128, A("et", EW * i + 3 - b, EW * i + 515 - b))
+    def constant(qn, i, b):
+        quant(qn + "q", qn + "s", 128 * b, 128, A("et", EW * i + 3 - b, EW * i + 515 - b))
 
     def tile(name, i):
         return lambda b: A(name, 512 * i + b, 512 * i + 512, 4)
@@ -431,91 +476,120 @@ def rank_program(g, core, T, topo):
         return (A("es", 256 * a, 256 * a + 256), A("si", SEG * a, SEG * a + 16), A("ci", SEG * a, SEG * a + 16),
                 A("pm", 8 * SEG * a + 7, 8 * SEG * a + 128, 8))
 
-    def sort_entries(l):
-        a = 2 - l
+    def numbered(l):
         for k in range(2):
-            act(A("es", 256 * a + M * k, 256 * a + M * k + M), A("eexp"), Act.Identity, off=A("pn", 16 * a + 8 * k, 16 * a + 8 * k + 8),
-                bias=float(C * k + 1))
+            a = 16 * (2 - l) + 8 * k
+            ts(A("pn", a, a + 8), A("m2", M * l + 15, M * l + M, 16), EXTRA, Op.subtract, float(C * k - RK), Op.add)
+
+    def sort_entries(l, k):
+        a = 2 - l
+        act(A("es", 256 * a + M * k, 256 * a + M * k + M), A("eexp"), Act.Identity, off=A("pn", 16 * a + 8 * k, 16 * a + 8 * k + 8),
+            bias=float(C * k + 1))
+
+    def listed(l):
+        a = 2 - l
+        t = to_table(level(l)[0], 256, C * a)
+        return lambda: ts(A("vi", SEG * a, SEG * a + 16), t, EXTRA, Op.subtract, float(-C), Op.add)
+
+    def twice(k, h):
+        ts(A("pd", 48 * k + h, 48 * k + 48, 2), A("permu"), float(C * k), Op.add)
 
     def slots():
         W = 2 * SEG
-        two = [to_table(level(2 - a)[0], 256, C * a) for a in range(2)]
-        for a in range(2):
-            ts(A("vi", SEG * a, SEG * a + 16), two[a], EXTRA, Op.subtract)
+
+        def w(n):
+            return A(n, 0, W - 1)
+        one = listed(1)
         quant("wfq", "wfs", FY, M, A("ti", 0, 512))
-        ts(A("si", 0, W - 1), A("vi", 0, W - 1), 10, Op.arith_shift_right)
-        ts(A("ci", 0, W - 1), A("vi", 0, W - 1), RK - 1, Op.bitwise_and)
+        one()
+        ones_where(A("rp"), [[0, W - 1], [1, 8]], Op.is_gt, 0, 0)
+        iota(A("pl", 0, 256), [[0, 2], [LOW, M]], LOW * M)
+        iota(A("w2", NE, NE + SL), [[0, SL]], SH)
+        iota(A("zt"), [[0, 512]], 0)
+        iota(A("uw", UM), [[1, SL]], FL2)
+        constant("eo", 2, 0)
+        ts(w("si"), w("vi"), 1.0 / RK, Op.mult, RND, Op.add)
+        constant("eo", 2, 1)
         for i in range(NP):
-            ts(A("oh", W * i + 1, W * i + W), A("si", 0, W - 1), float(ps[i] + 1), Op.is_equal)
+            ts(A("oh", W * i + 1, W * i + W), w("si"), RND + ps[i] + 1, Op.is_equal)
+        ts(w("pv"), w("si"), RND, Op.subtract, float(-RK), Op.mult)
+        ts(w("on"), w("si"), RND + r + 1, Op.is_equal)
         named(0)
         scan(A("c1"), A("rs"), A("oh"))
-        named(1)
+        tt(w("ci"), w("vi"), w("pv"), Op.add)
+        twice(0, 0)
         cp(A("tot", 0, 2 * NP), A("c1", SEG - 1, None, SEG))
+        named(1)
+        ts(w("pv"), w("ci"), float(SU0 + C - 1), Op.add)
+        trn(A("tt"), A("tot"))
+        tt(A("kt", 0, 2 * NP), A("kc", 0, 2 * NP), A("tot", 0, 2 * NP), Op.subtract)
         named(2)
-        across(2 * NP, 0)
+        scan(A("ts"), A("rt"), A("tt"))
+        tt(w("pv"), w("pv"), w("on"), Op.mult)
         named(3)
-        tt(A("oh", 0, None, SEG), A("tb", 0, 2 * NP), A("kt", 0, 2 * NP), Op.add)
+        trn(A("tb"), A("ts"))
         named(4)
+        act(A("gx"), A("uw", 0, UM), off=A("u2"))
+        tt(A("prod", 7, None, 8), w("pv"), w("pu"), Op.max)
+        tt(A("oh", 0, None, SEG), A("tb", 0, 2 * NP), A("kt", 0, 2 * NP), Op.add)
+        ts(A("et", EW, 2 * EW), A("et", 0, EW), A("pe", 0, 1), Op.mult)
         scan(A("c2"), A("rs"), A("oh"))
+        constant("ee", 1, 3)
         for i in range(NP):
             tt(A("prod", i, None, 8), A("oh", W * i + 1, W * i + W), A("c2", W * i + 1, W * i + W), Op.mult)
+        constant("ee", 1, 0)
         scan(A("pm"), A("rp"), A("prod"), Op.max)
-        for a in range(2):
-            cp(A("ou", 16 * a, 16 * a + 16), level(2 - a)[3])
+        placed(2)
+        cp(A("ou", 0, 16), level(2)[3])
+        constant("ee", 1, 1)
+
+    def placed(l):
+        a = 256 * (2 - l)
+        scan(A("val", a, a + 256), A("pl", a, a + 256), level(l)[0], Op.add, Op.max)
 
     def named(step):
-        if step < 2:
-            a = 8 * step
-            ts(A("a1", a, a + 8), A("si", SEG + a, SEG + a + 8), float(C), Op.mult, float(-C * (step + 1)), Op.add)
-        elif step == 2:
+        if step == 0:
+            ts(A("a1", 0, 16), level(1)[1], RND, Op.subtract, float(C), Op.mult)
+        elif step == 1:
             tt(A("a2", 0, 16), A("a1", 0, 16), level(1)[2], Op.add)
+        elif step == 2:
+            ts(A("a2", 8, 16), A("a2", 8, 16), float(-C), Op.add)
         else:
             cp(A("u2", step - 3, 32, 2), A("a2", 0, 16))
 
     def fill_slots(l):
-        scat(A("rw"), A("ou", 16 * (2 - l), 16 * (3 - l)), level(l)[0])
+        scat(A("w2"), A("ou", 16 * (2 - l), 16 * (3 - l)), A("val", 256 * (2 - l), 256 * (3 - l)))
 
-    def tables(l):
+    def tables(l, meanwhile):
         a, b, at = "req%d" % l, "rin%d" % l, NE + SL * (2 - l)
-        ts(A(a, 0, 21), to_table(A("rw", at, at + SL), SL), EXTRA, Op.subtract)
-
-        def go():
-            before("g", [A(a)], [])
-            if l == 2:
-                for part in spread(T, topo, r):
-                    call([(T.cores[ps[i]], es, "ar_r2", ap(A(a, 3 * i, 3 * i + 3)), ap(A(b, 3 * back(i), 3 * back(i) + 3))) for i, es in part])
-                note("x", [], [A(b)], "ar_r2", n_direct)
-                return
-            for h in range(3):
-                call([(hs[h], rest, "ar_hr%d" % l, ap(A(a, 6 * h, 6 * h + 6)), ap(A("hr%d" % l)))])
-            call([(T.cores[ps[-1]], rest, "ar_r%d" % l, ap(A(a, 18, 21)), ap(A(b, 18, 21)))])
-            note("x", [], [A(b)], "ar_r%d" % l, n_relayed)
-        hold("g", go)
-
-    def senders(l):
-        es, si, ci, O = level(l)
-        a = 2 - l
-
-        def w(n):
-            return A(n, 0, 16)
-        tt(w("xb1"), ci, w("nt"), Op.subtract)
-        ts(w("xb2"), si, float(r + 1), Op.is_equal)
-        ts(w("xb1"), w("xb1"), float(SU0 - 1), Op.add)
-        tt(w("xb1"), w("xb1"), w("xb2"), Op.mult)
-        tt(w("xb1"), w("xb1"), O, Op.add)
-        cp(A("o2u"), w("xb1"))
-        scat(A("w2"), A("o2u"), A("pl", 256 * a, 256 * a + 256))
+        t = to_table(A("w2", at, at + SL), SL)
+        meanwhile()
+        ts(A(a, 0, 21), t, EXTRA, Op.subtract)
+        before("g", [A(a)], [])
+        soon = list(enumerate(parts(off_chip, 2))) + [(NP - 1, rest)]
+        late = [(2 + i, es) for i, es in enumerate(parts(off_chip, 4))]
+        for part, sem in ((soon, "ar_r%d" % l), (late, "ar_t%d" % l)):
+            call([(T.cores[ps[i]], es, sem, ap(A(a, 3 * i, 3 * i + 3)), ap(A(b, 3 * back(i), 3 * back(i) + 3))) for i, es in part])
+            for i in range(NP):
+                if direct[i][0] in dict(part):
+                    note("x", [], [A(b, 3 * i, 3 * i + 3)], sem, sum(len(es) for j, es in part))
 
     def sent_from(l):
-        a = NE + SL * (2 - l)
-        return (lambda: to_table(A("w2", a, a + SL), SL, C),
-                lambda: ts(A("h%d" % l, 0, 21), A("m2", C + 15, C + SL, 16), A("pf", 3 + l, 4 + l), Op.subtract, 0.0, Op.max))
+        ts(A("hi", 0, 21), A("req%d" % l, 0, 21), 13, Op.arith_shift_right)
+        ts(A("h%d" % l, 0, 21), A("hi", 0, 21), float(M - M * l), Op.add, 0.0, Op.max)
 
-    def successors(l):
-        ts(A("xb3", 0, 21), A("rin%d" % l, 0, 21), float(SL - 1 - RK * (r + 1)), Op.add)
+    def asked(l, a, z):
+        ts(A("lo", 24 * (2 - l) + a, 24 * (2 - l) + z), A("rin%d" % l, a, z), LOW - 1, Op.bitwise_and)
+        return A("lo", 24 * (2 - l), 24 * (2 - l) + 21)
+
+    def successors(l, low):
+        ts(A("xb3", 0, 21), low, float(SL - 1 - RK * (r + 1)), Op.add)
         tt(A("xb3", 0, 21), A("xb3", 0, 21), A("nt", 0, 21), Op.max)
         cp(A("suu", 0, 21), A("xb3", 0, 21))
         scat(A("w2", NE + NS), A("suu", 0, 21), A("sud", SL * (2 - l), SL * (3 - l)))
+
+    def coded(place):
+        return LOW * (place - M) + SH + RK * (r + 1) + C
 
     dmas("ld_l", [("ys"[i % 2], T.lvt[16 * i:16 * i + 16, :], T.lv[:], [], [A("lvt")]) for i in range(8)])
     dmas("ld_e", [("y", T.e[:, 0:24], T.pr0[:], [], [A("e", 0, 24)]), ("y", T.e[:, 24:48], T.pr1[:], [], [A("e", 24, 48)])])
@@ -525,163 +599,176 @@ def rank_program(g, core, T, topo):
     dmas("ld_u", [("y", T.ut[:], T.u[:], [], [A("ut")])])
 
     fill(A("ones"), 1.0)
-    iota(A("iot"), [[1, C]], 0)
     iota(A("pc", 0, 1), [[0, 1]], 0, 1)
+    ones_where(A("et", 0, EW), [[-1, EW]], Op.is_equal, 3, 4)
     iota(A("kc", 14, 17), [[M, 3]], -1)
-    iota(A("nm"), [[0, C // 16], [1, 16]], 0)
     iota(A("nt0"), [[16, 24]], 0)
-    run("g", [A("ones")], [A("et", 0, EW)], lambda: g.affine_select(ap(A("et", 0, EW)), T.ones[:], [[-1, EW]], Op.is_equal, 0.0, 3, 4))
-    for name, step in (("lrs", LSEG), ("rt", 16), ("rs", SEG), ("rp", 8)):
-        fill(A(name), 1.0)
+    iota(A("nm"), [[0, C // 16], [1, 16]], 0)
+    iota(A("io2"), [[FL1, 3], [1, M]], 0)
+    fill(A("lrs"), 1.0)
+    scan(A("iot"), A("ones", 0, C), A("ones", 0, C), first=-1.0)
+    for k in range(2):
+        act(A("w2", SU0 + C * k, SU0 + C * k + C), A("ones", 0, C), scale=float(coded(BZ)))
+    fill(A("rt"), 1.0)
     fill(A("tot"), 0.0)
     fill(A("loh", 0, None, LSEG), 0.0)
-    fill(A("oh", 0, None, SEG), 0.0)
-    fill(A("vi"), 0)
-    fill(A("ew", 0, 1), float(RK * (N + 1)))
-    for name, step in (("lrs", LSEG), ("rt", 16), ("rs", SEG), ("rp", 8)):
+    fill(A("ew", 0, 1), float(RK * (N + 1) + SH))
+    for name, step in (("lrs", LSEG), ("rt", 16)):
         fill(A(name, 0, None, step), 0.0)
     ts(A("pc", 1, 2), A("pc", 0, 1), 15, Op.bitwise_and)
     ts(A("pc", 2, 3), A("pc", 0, 1), 16, Op.bitwise_and)
     ts(A("pf", 1, 2), A("pc", 1, 2), -1.0, Op.mult, -0.5, Op.add)
     cp(A("pf", 0, 1), A("pc", 1, 2))
-
-    def extra(l):
-        ts(A("pf", 3 + l, 4 + l), A("pc", 1, 2), float(-BIG), Op.mult, float(15 * BIG + M * l), Op.add)
-
-    def ranks(some):
-        for s in some:
-            act(A("ew", 1 + C * s, 1 + C * s + C), A("iot"), Act.Identity, bias=float(RK * (s + 1)))
-    ranks(range(0, 3))
-    act(A("ma"), A("nm"), Act.Sign, bias=A("pf", 1, 2))
-    act(A("keep"), A("ma"), Act.Identity, bias=-15.5 * BIG, scale=16.5 * BIG)
-    ranks(range(3, N))
+    ts(EXTRA, A("pc", 1, 2), float(-BIG), Op.mult, float(15 * BIG + SH), Op.add)
+    ts(A("pe", 0, 1), A("pc", 2, 3), 0.03125, Op.mult, -0.5, Op.add)
+    ts(A("pe", 1, 2), A("pc", 2, 3), -0.03125, Op.mult)
+    fill(A("vi"), 0.0)
+    fill(A("oh", 0, None, SEG), 0.0)
+    for s in range(N):
+        act(A("ew", 1 + C * s, 1 + C * s + C), A("iot"), Act.Identity, bias=float(RK * (s + 1) + SH))
+        if s == 5:
+            act(A("ma"), A("nm"), Act.Sign, bias=A("pf", 1, 2))
+            act(A("keep"), A("ma"), Act.Identity, bias=-15.5 * BIG, scale=16.5 * BIG)
 
     for l in range(3):
         ts(A("loh", LSEG * l + 1, LSEG * l + LSEG), A("lvt"), float(l), Op.is_equal)
-    scan(A("lc1"), A("lrs"), A("loh"))
-    ts(A("pe", 0, 1), A("pc", 2, 3), 0.03125, Op.mult, -0.5, Op.add)
-    cp(A("tot", 0, 3), A("lc1", LSEG - 1, None, LSEG))
-    ts(A("pe", 1, 2), A("pc", 2, 3), -0.03125, Op.mult)
-    across(3, 14)
+    constant("e1", 0, 0)
+    for l in range(3):
+        summed(A("tot", l, l + 1), A("loh", LSEG * l + 1, LSEG * l + LSEG))
+    constant("e1", 0, 1)
+    trn(A("tt"), A("tot"))
+    tt(A("kt", 0, 3), A("kc", 14, 17), A("tot", 0, 3), Op.subtract)
+    scan(A("ts"), A("rt"), A("tt"))
+    constant("e1", 0, 2)
+    trn(A("tb"), A("ts"))
     ts(A("u1"), A("e"), 1.0, Op.add)
-    tt(A("loh", 0, None, LSEG), A("tb", 0, 3), A("kt", 0, 3), Op.add)
     ts(A("nt"), A("nt0"), A("pf", 0, 1), Op.add)
+    tt(A("loh", 0, None, LSEG), A("tb", 0, 3), A("kt", 0, 3), Op.add)
+    constant("e1", 0, 3)
     scan(A("lc2"), A("lrs"), A("loh"))
-    ts(A("prod", 7, 8 * SEG, 8), A("nt0", 0, SEG), A("pf", 0, 1), Op.add)
+    ts(A("pu", 0, SEG), A("nt0", 0, SEG), A("pf", 0, 1), Op.add)
     tt(A("lc1"), A("loh"), A("lc2"), Op.mult)
-    ts(A("prod", 8 * SEG + 7, None, 8), A("nt0", 0, 16), A("pf", 0, 1), Op.add)
+    cp(A("pu", SEG, 2 * SEG - 1), A("nt", 0, 16))
     tt(A("pos"), A("lc1", 1, LSEG), A("lc1", LSEG + 1, 2 * LSEG), Op.add)
-    extra(0)
+    ts(A("pf", 4, 5), EXTRA, -1.0, Op.add)
     tt(A("pos"), A("pos"), A("lc1", 2 * LSEG + 1, 3 * LSEG), Op.add)
-    extra(1)
+    ts(A("pf", 5, 6), EXTRA, -2.0, Op.add)
     cp(A("posu"), A("pos"))
     before("g", [A("posu")], [])
-    PSEM = ["ar_pa"] * 4 + ["ar_pb"] * 2 + ["ar_pc"]
-    for part in spread(T, topo, r):
-        call([(T.cores[ps[i]], es, PSEM[i], ap(A("posu")), ap(A("pin", 24 * back(i), 24 * back(i) + 24))) for i, es in part])
+    halves = parts(off_chip, 2)
+    same = [i for i in range(4) if topo.die(T.cores[ps[i]]) == topo.die(core)]
+    plan = [[(same[0], halves[0], "ar_pa"), (same[1], halves[1], "ar_pa")],
+            [(4, halves[0], "ar_pb"), (5, halves[1], "ar_pb"), (NP - 1, rest, "ar_pc")]]
+    for j, part in enumerate(plan):
+        call([(T.cores[ps[i]], es, sem, ap(A("posu")), ap(A("pin", 24 * back(i), 24 * back(i) + 24))) for i, es, sem in part] +
+             [(hs[h], helper_engines(T, topo, r, 1)[h], "ar_hp", ap(A("posu")), ap(A("hp"))) for h in range(2 - 2 * j)])
+    PSEM = [("ar_pa" if topo.die(T.cores[ps[i]]) == topo.die(core) else "ar_pd") if j < 4 else "ar_pb" if j < 6 else "ar_pc"
+            for i, (j, n) in enumerate(direct)]
     for i in range(NP):
-        sem = PSEM[direct[i][0]]
-        note("x", [], [A("pin", 24 * i, 24 * i + 24)], sem, sum(n for j, n in direct if PSEM[j] == sem))
+        note("x", [], [A("pin", 24 * i, 24 * i + 24)], PSEM[i], len(off_chip) * (2 if PSEM[i] == "ar_pd" else 1))
     iota(A("kc", 0, 14), [[CAP, NP], [SL, 2]], NE - 1)
-    extra(2)
-    scat(A("pw"), A("posu"), A("iot"))
+    ones_where(A("rs"), [[0, 2 * NP], [1, SEG]], Op.is_gt, 0, 0)
+    fill(A("uw", 0, UM, UM - 1), float(FZ))
+    scat(A("pw"), A("posu"), A("ew", 1, 1 + C))
+    act(A("eexp", 0, C), A("ew"), off=A("u1", 0, 24))
+    act(A("eexp", C, NE), A("ew"), off=A("u1", 24, 48))
     quant("sq", "ss", 0, C, A("xt"))
     first = to_table(A("pw", 0, M), M)
-    PERM = A("m2", 15, C, 16)
-    act(A("eexp", 0, C), A("ew"), off=A("u1", 0, 24))
-    fill(A("uw", 0, UM, UM - 1), float(FZ))
-    ts(A("permu", 0, 8), first, EXTRA, Op.subtract)
-    constant("e1q", "e1s", 0, [0])
-
-    pick("spq", "sps", 0, "sq", "ss", C, A("permu", 0, 8))
-    act(A("eexp", C, NE), A("ew"), off=A("u1", 24, 48))
-    constant("e1q", "e1s", 0, [1, 2, 3])
     to_table(A("pw", M, C), C - M, M)
+    ts(A("permu", 0, 8), first, EXTRA, Op.subtract, float(-RK), Op.add)
+
+    numbered(2)
+    pick("spq", "sps", 0, "sq", "ss", C, A("permu", 0, 8))
+    sort_entries(2, 0)
+    numbered(1)
+    ts(A("permu", 8, 24), A("m2", M + 15, C, 16), EXTRA, Op.subtract, float(-RK), Op.add)
+    ts(A("pf", 6, 7), EXTRA, -3.0, Op.add)
     decode("spq", "sps", 0, M, tile("xs", 6), "vsvs")
-    for l in (2, 1):
-        for k in range(2):
-            a = 16 * (2 - l) + 8 * k
-            ts(A("pn", a, a + 8), A("m2", M * l + 15, M * l + M, 16), EXTRA, Op.subtract, float(C * k), Op.add)
-            if a == 8:
-                quant("xq", "xp", 128 * 6, M, A("xs", 512 * 6, 512 * 7))
-    sort_entries(2)
-    ev = layer("wq", "wp", 6, tile("ti", 0), "vsvv")
-    ts(A("permu", 8, 24), A("m2", M + 15, C, 16), EXTRA, Op.subtract)
-    for k in range(2):
-        for h in range(2):
-            ts(A("pd", 48 * k + h, 48 * k + 48, 2), PERM, EXTRA, Op.subtract, float(C * k), Op.add)
+    sort_entries(2, 1)
+    sort_entries(1, 0)
+    quant("xq", "xp", 128 * 6, M, A("xs", 512 * 6, 512 * 7))
+    ev = layer("wq", "wp", 6, tile("ti", 0))
+    ts(A("et", 2 * EW, 3 * EW), A("et", 0, EW), A("pe", 1, 2), Op.mult)
     for f in ev:
         f()
-    sort_entries(1)
-    quant("sdq1", "sds1", 0, M, A("ti", 0, 512))
+    sort_entries(1, 1)
+    two = listed(2)
+    quant("swq1", "sws1", 0, M, A("ti", 0, 512))
     exchange(1)
-    iota(A("rw", NE), [[0, NS]], 0)
-    iota(A("zt"), [[0, 512]], 0)
+    two()
 
     def place(i):
         s, off = (r, A("posu")) if i == NP else (ps[i], A("pin", 24 * i, 24 * i + 24))
-        act(A("uw", 1 + C * s, 1 + C * s + C), A("iot"), Act.Identity, off=off, bias=float(M * i))
+        act(A("uw", 1 + C * s, 1 + C * s + C), A("iot" if i == NP else "io2"), Act.Identity, off=off, bias=float(M * i))
     place(NP)
-    for i in sorted(range(NP), key=lambda i: (direct[i][0] != NP - 1, direct[i][0])):
+    for i in sorted(range(NP), key=lambda i: ("cabd".index(PSEM[i][-1]), i)):
         place(i)
     slots()
-    act(A("gx"), A("uw", 0, UM), off=A("u2"))
-
-    def halves():
-        for i in range(2):
-            ts(A("et", EW * (i + 1), EW * (i + 2)), A("et", 0, EW), A("pe", i, i + 1), Op.mult)
-    weave(lambda: (fill_slots(2), tables(2)), halves)
-    iota(A("uw", UM), [[1, SL]], FL2)
-    iota(A("pl"), [[-M, 2], [0, 2], [1, M]], 2 * M)
-    iota(A("w2", NE, NE + NS), [[0, NS]], 0)
-    iota(A("w2", SU0), [[0, NE]], BZ)
-    pick("spq", "sps", M, "sq", "ss", C, A("permu", 8, 24))
-    quant("wfq", "wfs", FZ, M, A("zt"))
+    fill_slots(2)
+    constant("ee", 1, 2)
+    tables(2, lambda: pick("spq", "sps", M, "sq", "ss", C, A("permu", 8, 16)))
+    iota(A("sud", 0, SL), [[LOW, SL]], coded(BL3))
+    iota(A("pl", 256, 512), [[0, 2], [LOW, M]], 0)
+    decode("spq", "sps", M, M, lambda b: A("ds", 256 * b, 256 * b + M))
     trn(A("gt"), A("gx"))
-    decode("spq", "sps", M, 256, lambda b: A("ds", 256 * b, 256 * b + 256))
-    constant("eeq", "ees", 1)
+    quant("wfq", "wfs", FZ, M, A("zt"))
     cp(A("f1", 0, 16), A("gt", 0, 512, 32))
     cp(A("f1", 16, 32), A("gt", 16, 512, 32))
-    constant("eoq", "eos", 2)
+    twice(0, 1)
 
     def own():
+        constant("eo", 2, 2)
+        constant("eo", 2, 3)
         for k in range(2):
-            act(A("pp", C * k, C * k + C), A("uw", 1 + C * r, 1 + C * r + C), Act.Identity, bias=float(-M * NP))
-        for b in range(4):
-            plain("vs"[b % 2], A("yp", 256 * b, 256 * b + M), tile("ti", 0)(b))
+            act(A("pp", C * k, C * k + C), A("uw", 1 + C * r, 1 + C * r + C), Act.Identity, bias=float(SH - 4 * M * NP), scale=4.0)
     gathered(1, "wf", FL2, "f1", "ds", 0, 256, 0, own)
-    ev = layer("wq", "wp", 0, lambda b: A("yp", 256 * b + M, 256 * b + 256), "vvvs")
-    ts(A("c2u", 0, 21), A("rin2", 0, 21), float(-1 - RK * (r + 1)), Op.add, 0.0, Op.max)
-    act(A("m1", 0, SL), A("pp"), off=A("c2u", 0, 21))
+    ev = layer("wq", "wp", 0, tile("ti", 1), "vsvv")
+    low = asked(2, 12, 21)
+    ts(A("a2", 0, 16), level(2)[3], float(UM - NE), Op.add)
+    ts(A("c2u", 12, 21), A("lo", 12, 21), float(-1 - RK * (r + 1)), Op.add, 0.0, Op.max)
+    act(A("pw", 0, 144), A("pp"), off=A("c2u", 12, 21))
     for f in ev:
         f()
-    ts(A("g2", 0, 21), to_table(A("m1", 0, SL), SL), EXTRA, Op.subtract, float(2 * M - 1), Op.min)
-    send(2, (), lambda b: A("yp", 256 * b, 256 * b + 256), "g2")
-    iota(A("sud"), [[1, NS]], BL3)
+    t = to_table(A("pw", 0, 144), 144)
+    quant("swq2", "sws2", 0, M, A("ti", 512, 1024))
+    exchange(2, 0)
+    for b in (1, 0, 3, 2):
+        ts(A("g2", 10 * b, 10 * b + 9), t, A("pf", 3 + b, 4 + b), Op.subtract, float(8 * M - 4 + b), Op.min)
+    for b in range(4):
+        plain("vs"[b % 2], A("st", 8 * SL + b, 8 * SL + 576, 4), A("ti", 0, 1024), A("g2", 10 * b, 10 * b + 9))
+    ts(A("a3", 0, 16), level(2)[3], float(NE), Op.is_ge)
+    quant("sdq2", "sds2", 0, 144, A("st", 8 * SL, 8 * SL + 576))
+    exchange(2, 1)
+    iota(A("w2", NE + SL, NE + NS), [[0, SL]], SH)
+    iota(A("sud", SL, NS), [[LOW, SL]], coded(BL4))
 
     def places():
         es, si, ci, O = level(2)
-        for k in range(2):
-            ts(A("a1", 8 * k, 8 * k + 8), A("ci", 8 * k, 8 * k + 8), float(C * (r - k)), Op.add)
-        ts(A("a4", 0, 16), si, float(r + 1), Op.is_equal)
-        ts(A("a3", 0, 16), O, float(NE), Op.is_ge, float(UM + SL), Op.mult)
-        ts(A("a2", 0, 16), O, float(UM - NE), Op.add)
-        tt(A("a1", 0, 16), A("a1", 0, 16), A("a4", 0, 16), Op.mult)
-        tt(A("a2", 0, 16), A("a2", 0, 16), A("a3", 0, 16), Op.min)
-        tt(A("a5", 0, 16), A("a1", 0, 16), A("a2", 0, 16), Op.max)
+        whole = [A("oh", 2 * SEG * i + 1, 2 * SEG * i + SEG) for i in range(NP) if direct[i][0] < WHOLE]
+        a1, a2, a3, a4, a5 = [A("a%d" % i, 0, 16) for i in range(1, 6)]
+        ts(a1, si, RND, Op.subtract, float(C), Op.mult)
+        tt(a4, whole[0], whole[1], Op.add)
+        tt(a5, whole[2], whole[3], Op.add)
+        tt(a1, a1, ci, Op.add)
+        tt(a4, a4, A("on", 0, 16), Op.add)
+        ts(A("a1", 8, 16), A("a1", 8, 16), float(-C), Op.add)
+        tt(a4, a4, a5, Op.add)
+        tt(a2, a2, a3, Op.mult)
+        tt(a1, a1, a2, Op.subtract)
+        tt(a1, a1, a4, Op.mult)
+        tt(a5, a1, a2, Op.add)
         for h in range(2):
-            cp(A("u2", h, 32, 2), A("a5", 0, 16))
+            cp(A("u2", h, 32, 2), a5)
         act(A("gx"), A("uw"), off=A("u2"))
-        for b in range(4):
-            act(tile("ti", 1)(b), A("yp", 256 * b + M, 256 * b + 256))
-    weave(places, lambda: senders(2))
-    weave(lambda: (pair_lists("f2"), quant("wfq", "wfs", FY + M, M, A("ti", 512, 1024))), lambda: successors(2))
+    weave(places, lambda: (twice(1, 0), twice(1, 1), sent_from(2), cp(A("ou", 16, 32), level(1)[3])))
+    asked(2, 0, 12)
+    pick("spq", "sps", 2 * M, "sq", "ss", C, A("permu", 16, 24))
+    decode("spq", "sps", 2 * M, M, lambda b: A("ds", 256 * b + M, 256 * b + 256))
+    weave(lambda: successors(2, low), lambda: (quant("wfq", "wfs", FY + M, M, A("ti", 512, 1024)), placed(1)))
+    pair_lists("f2")
 
-    steps = sent_from(2)
-    gathered(2, "wf", FW, "f2", "ds", 128, 256, 1, steps[0])
-    ev = layer("wq", "wp", 1, tile("xs", 2))
-    steps[1]()
-    for f in ev:
+    gathered(2, "wf", FW, "f2", "ds", 128, 256, 1)
+    for f in layer("wq", "wp", 1, tile("xs", 2)):
         f()
     quant("xq", "xp", 256, M, A("xs", 1024, 1536))
     decode("xq", "xp", 256, M, tile("xs", 3), "vsvs")
@@ -694,35 +781,38 @@ def rank_program(g, core, T, topo):
         act(tile("ti", 2)(b), A("zp", 128 * b, 128 * b + M))
     spread_lists(SU, 1)
     decode("wfq", "wfs", FY, 256, lambda b: A("dy", 256 * b, 256 * b + 256))
-    weave(lambda: (fill_slots(1), tables(1)), lambda: senders(1),
-          lambda: (quant("wbq", "wbs", BZ, M, A("zt")), quant("wbq", "wbs", 2 * M, M, A("ti", 1024, 1536)), pair_lists("b1")))
+    quant("wbq", "wbs", BZ, M, A("zt"))
+    quant("wbq", "wbs", 2 * M, M, A("ti", 1024, 1536))
+    pair_lists("b1")
+    fill_slots(1)
+    quant("uq", "us", 0, 128, A("ut"))
+    tables(1, lambda: None)
+    sent_from(1)
 
-    steps = sent_from(1)
-    gathered(3, "wb", BL4, "b1", "dy", M, 256, 4, steps[0])
+    gathered(3, "wb", BL4, "b1", "dy", M, 256, 4)
     ev = layer("vq", "vp", 4, lambda b: A("zp", 512 + 128 * b, 512 + 128 * b + M))
-    steps[1]()
     send(4, ev, lambda b: A("zp", 512 + 128 * b, 512 + 128 * b + M), "h1")
 
-    successors(1)
+    successors(1, asked(1, 0, 21))
     spread_lists(SU, 0)
     for b in range(4):
         act(tile("ti", 3)(b), A("zp", 512 + 128 * b, 512 + 128 * b + M))
-    quant("uq", "us", 0, 128, A("ut"))
     pair_lists("b0")
     quant("wbq", "wbs", M, M, A("ti", 1536, 2048))
+    mm(bank("PB", 0, 256), "uq", "us", 0, "wbq", "wbs", M, 256)
+    act(A("ys", M, C), bank("PB", 0, 256))
 
     gathered(4, "wb", BW, "b0", "dy", 0, 256, 5)
     for f in layer("vq", "vp", 5, tile("ti", 4)):
         f()
     quant("wbq", "wbs", 0, M, A("ti", 2048, 2560))
-    H = C // 2
-    for h in range(2):
-        pick("oq", "opl", H * h, "wbq", "wbs", C, A("posu", 12 * h, 12 * h + 12))
-        mm(bank("PA", h, H), "uq", "us", 0, "oq", "opl", H * h, H)
+    mm(bank("PA", 0, M), "uq", "us", 0, "wbq", "wbs", 0, M)
+    pick("oq", "opl", 0, "wbq", "wbs", C, A("posu"))
+    act(A("ys", 0, M), bank("PA", 0, M))
     dmas("st_c", [("y", T.oc[:], u8(A("oq")), [A("oq")], [])])
     dmas("st_s", [("y", T.osc[4 * k:4 * k + 4, :], T.opl[32 * k:32 * k + 4, :], [A("opl")], []) for k in range(4)])
     for h in range(2):
-        plain("vs"[h], A("yo", H * h, H * h + H), bank("PA", h, H))
+        plain("vs"[h], A("yo", 192 * h, 192 * h + 192), A("ys"), A("posu", 12 * h, 12 * h + 12))
     dmas("st_y", [("s", T.y[:], T.yo[:], [A("yo")], [])])
 
     g.wait_ge(T.sem.sent, sent[0])

@@ -16,10 +16,13 @@ RK = 800
 LOW = 8192
 BIG = 256 * LOW
 SH = 128 - 8 * BIG
-RND = 12582912.0
 SU0 = NE + NS + SL
-VIA = (1, 2)
+IOT = 240
 LAND = {1: ("wf", 0, FY), 2: ("wf", FL2, FW), 3: ("wb", BL3, BL4), 4: ("wb", BL4, BW)}
+CYC, WAKE, CALL, FIRST, GATHER, SCATTER = 0.00096, 0.18, 0.2, 1.4, 1.65, 4.0
+WAY = {"ar_pa": 2.0, "ar_pb": 2.6, "ar_pc": 2.0, "ar_pd": 4.6, "ar_r": 1.8, "ar_t": 5.0,
+       1: (4.0, 4.6), 2: (3.6, 4.6), 3: (3.6, 4.2), 4: (3.6, 4.2)}
+ORDER = []
 
 
 def lot(k, i):
@@ -28,37 +31,43 @@ def lot(k, i):
     return "sd%%s%d" % k, CAP * (i - WHOLE * (k == 2)), CAP, LAND[k][1]
 
 
+def wide(k, h):
+    if lot(k, 2 * h)[2] == M:
+        return 0, M
+    return (0 if h < 2 or k == 2 else SL - 4 * CAP), 4 * CAP
+
+
 def _sb(n, d):
     return ("sbuf", [128, n], d)
 
 
 SMALL = {}
-for _n in ("tot", "tt", "ts", "tb", "rt", "kc", "kt", "pos", "nt0", "nt", "a1", "a2", "a3", "a4", "a5", "xb3"):
-    SMALL[_n] = (32 * len(SMALL), 32 if len(SMALL) < 7 else 24)
+for _n in ("tot", "tt", "ts", "tb", "rt", "kc", "kt", "t2", "s2", "nt", "a1", "a2", "a3", "a4", "x1", "x2",
+           "vi", "vn", "pv", "n1", "on", "pu"):
+    SMALL[_n] = (40 * len(SMALL), 32 if len(SMALL) < 9 else 24 if len(SMALL) < 16 else 33)
 
 SCRATCH = {
-    "sm": _sb(32 * len(SMALL), F32), "e": _sb(48, I32), "lvt": _sb(24, I32), "iot": _sb(C, F32), "io2": _sb(C, F32),
-    "ew": _sb(UM - 1, F32), "eexp": _sb(NE, F32), "es": _sb(512, F32), "vi": _sb(34, F32), "si": _sb(34, F32), "ci": _sb(34, F32),
-    "val": _sb(512, F32), "on": _sb(34, F32), "pv": _sb(34, F32), "pu": _sb(34, F32), "lo": _sb(48, I32),
-    "oh": _sb(2 * NP * SEG, F32), "rs": _sb(2 * NP * SEG, BF), "c1": _sb(2 * NP * SEG, F32), "c2": _sb(2 * NP * SEG, F32),
+    "sm": _sb(40 * len(SMALL), F32), "e": _sb(48, I32), "lvt": _sb(24, I32), "ct": _sb(IOT + C, F32), "io2": _sb(C, F32),
+    "ew": _sb(UM - 1, F32), "eexp": _sb(NE, F32), "es": _sb(512, F32), "si": _sb(33, I32), "val": _sb(512, F32), "lo": _sb(48, I32),
+    "oh": _sb(32 * SEG, F32), "rs": _sb(2 * NP * SEG, BF), "c2": _sb(2 * NP * SEG, F32),
     "prod": _sb(264, F32), "rp": _sb(264, BF), "pm": _sb(264, F32),
-    "loh": _sb(3 * LSEG, F32), "lrs": _sb(3 * LSEG, F32), "lc1": _sb(3 * LSEG, F32), "lc2": _sb(3 * LSEG, F32),
+    "loh": _sb(3 * LSEG, F32), "lrs": _sb(152, BF), "lc1": _sb(3 * LSEG, F32), "lc2": _sb(3 * LSEG, F32), "lc3": _sb(144, F32),
     "ou": _sb(32, U16), "pp": _sb(NE, F32), "posu": _sb(24, U16), "pin": _sb(24 * NP, U16), "pc": _sb(4, I32), "pf": _sb(8, F32),
-    "nm": _sb(C, BF), "ma": _sb(C, BF), "keep": _sb(C, BF), "m2": _sb(2 * C, F32),
-    "req1": _sb(24, I32), "req2": _sb(24, I32), "rin1": _sb(24, I32), "rin2": _sb(24, I32), "hi": _sb(24, I32), "hp": _sb(24, U16),
+    "nm": _sb(SL, BF), "ma": _sb(SL, BF), "keep": _sb(SL, BF), "m2": _sb(1712, F32),
+    "req1": _sb(24, I32), "req2": _sb(24, I32), "rin1": _sb(24, I32), "rin2": _sb(24, I32), "hi": _sb(48, I32), "hp": _sb(24, U16),
     "c2u": _sb(22, U16), "g2": _sb(40, U16), "h1": _sb(22, U16), "h2": _sb(22, U16),
-    "pw": _sb(C, F32), "permu": _sb(24, U16), "pd": _sb(96, U16), "pn": _sb(32, U16),
-    "u1": _sb(48, U16), "u2": _sb(32, U16), "uw": _sb(UM + SL, F32),
-    "gx": _sb(512, F32), "gt": _sb(512, F32), "f1": _sb(32, U16), "f2": _sb(32, U16), "b1": _sb(32, U16), "b0": _sb(32, U16),
-    "pl": _sb(512, F32), "w2": _sb(SU0 + NE, F32), "sud": _sb(NS, F32), "suu": _sb(22, U16),
-    "ones": _sb(EW, BF), "et": _sb(3 * EW, BF), "zt": _sb(512, BF), "pe": _sb(2, F32),
+    "pw": _sb(C + 144, F32), "permu": _sb(24, U16), "pd": _sb(96, U16), "pn": _sb(32, U16),
+    "u1": _sb(48, U16), "u2": _sb(64, U16), "uw": _sb(UM + SL, F32),
+    "gx": _sb(1024, F32), "gt": _sb(1024, F32), "f1": _sb(32, U16), "f2": _sb(32, U16), "b1": _sb(32, U16), "b0": _sb(32, U16),
+    "pl": _sb(512, F32), "w2": _sb(SU0 + NE, F32), "sud": _sb(NS, F32), "suu": _sb(48, U16),
+    "ones": _sb(C, BF), "et": _sb(3 * EW, BF), "zt": _sb(512, BF),
     "e1q": _sb(512, Q4), "e1s": _sb(512, U8), "eeq": _sb(512, Q4), "ees": _sb(512, U8), "eoq": _sb(512, Q4), "eos": _sb(512, U8),
     "xt": _sb(4 * C, BF), "ut": _sb(512, BF), "sq": _sb(C, Q4), "ss": _sb(C, U8), "uq": _sb(128, Q4), "us": _sb(128, U8),
     "wq": _sb(512, Q4), "wp": _sb(512, U8), "vq": _sb(512, Q4), "vp": _sb(512, U8),
     "wfq": _sb(FW, Q4), "wfs": _sb(FW, U8), "wbq": _sb(BW, Q4), "wbs": _sb(BW, U8),
     "spq": _sb(C, Q4), "sps": _sb(C, U8), "ds": _sb(1024, BF), "dy": _sb(1024, BF),
     "xs": _sb(7 * 512, BF), "xq": _sb(7 * 128, Q4), "xp": _sb(7 * 128, U8), "ti": _sb(5 * 512, BF), "zp": _sb(1024, BF),
-    "st": _sb(3 * 4 * SL, BF), "oq": _sb(C, Q4), "opl": _sb(C, U8), "ys": _sb(C, F32), "yo": _sb(C, F32),
+    "st": _sb(8 * SL + 16 * CAP, BF), "oq": _sb(C, Q4), "opl": _sb(C, U8), "ys": _sb(C, F32), "yo": _sb(C, F32),
     "PA": ("psum", [128, 2048], F32), "PB": ("psum", [128, 2048], F32),
 }
 for _k in range(1, 5):
@@ -67,12 +76,12 @@ for _k in range(1, 5):
     for _n, _w in [("sw", M)] * (_k < 3) + [("sd", SL)] * (_k > 1):
         SCRATCH["%sq%d" % (_n, _k)] = _sb(_w, Q4)
         SCRATCH["%ss%d" % (_n, _k)] = _sb(_w, U8)
-    SCRATCH["hs%d" % _k] = _sb(M, U8)
-for _k in VIA:
+    SCRATCH["hs%d" % _k] = _sb(4 * CAP, U8)
+for _k in (1, 2):
     SCRATCH["hc%d" % _k] = _sb(M, Q4)
-SEMAPHORES = ["q_v", "q_s", "q_t", "q_g", "sent", "ld_l", "ld_e", "ld_x", "ld_w", "ld_v", "ld_u", "st_c", "st_s", "st_y",
-              "ar_pa", "ar_pb", "ar_pc", "ar_pd", "ar_hp", "ar_r1", "ar_r2", "ar_t1", "ar_t2"] + \
-    ["ar_%s%d" % (_n, _k) for _k in range(1, 5) for _n in "csh"] + ["ar_g%d" % _k for _k in VIA]
+SEMAPHORES = ["q_v", "q_s", "q_t", "q_g", "sent", "ld_l", "ld_s", "ld_e", "ld_x", "ld_w", "ld_v", "ld_u", "st_c", "st_s", "st_y",
+              "ar_pa", "ar_pb", "ar_pc", "ar_pd", "ar_hp", "ar_r1", "ar_r2", "ar_t1", "ar_t2", "ar_g1", "ar_g2"] + \
+    ["ar_%s%d" % (_n, _k) for _k in range(1, 5) for _n in "csh"]
 
 
 def peers_of(T, topo, r):
@@ -108,46 +117,9 @@ def engine_sets(T, topo, r):
     return off, [e for e in topo.engines(core, T.cores[ps[-1]]) if e not in off]
 
 
-def spread(T, topo, r, k=1):
-    off, rest = engine_sets(T, topo, r)
-    one, two, near = list(enumerate(parts(off, 4))), [(4 + i, es) for i, es in enumerate(parts(off, 2))], [(NP - 1, rest)]
-    return (one, two + near) if k > 1 else (one + near, two)
-
-
-def helper_engines(T, topo, r, k):
-    off, rest = engine_sets(T, topo, r)
-    return parts(rest, 2) + [rest if k > 1 else off]
-
-
-def handed(T, topo, r, h):
-    ps, core = peers_of(T, topo, r), helpers_of(T, topo, r)[h]
-    return [(2 * h + j, es) for j, es in enumerate(parts(topo.engines(core, T.cores[ps[2 * h]]), 2))]
-
-
 def far_helper(T, topo, s, h):
     d = [d for d in peers_of(T, topo, s)[2 * h:2 * h + 2] if topo.die(T.cores[d]) == topo.die(T.cores[s])][0]
     return helpers_of(T, topo, d)[h]
-
-
-def on_chip(T, topo, r, h):
-    return list(zip((r, peers_of(T, topo, r)[-1]), parts(topo.engines(helpers_of(T, topo, r)[h], T.cores[r]), 2)))
-
-
-def code_plan(T, topo, r, k):
-    one, two = [[(i, None, es) for i, es in p] for p in spread(T, topo, r, k)]
-    if k in VIA:
-        one = [(None, h, es) for h, es in enumerate(parts(engine_sets(T, topo, r)[0], 2))] + one[WHOLE:]
-    return one, two
-
-
-def arrivals(T, topo, r):
-    direct, relayed = [], 0
-    for s in peers_of(T, topo, r):
-        i = peers_of(T, topo, s).index(r)
-        one, two = spread(T, topo, s)
-        direct.append((i, [len(es) for j, es in one + two if j == i][0]))
-        relayed += ([len(es) for h in range(3) for j, es in handed(T, topo, s, h) if j == i] + [direct[-1][1]])[0]
-    return direct, relayed
 
 
 def dst(topo, c):
@@ -155,37 +127,98 @@ def dst(topo, c):
     return DstId(rid=a[0], pnc=a[1])
 
 
+def meet(u, v):
+    if u[0][0] == "P":
+        return u[1] // 512 <= (v[2] - 1) // 512 and v[1] // 512 <= (u[2] - 1) // 512
+    if u[1] >= v[2] or v[1] >= u[2]:
+        return False
+    return not (u[3] == v[3] and u[3] > 1 and (u[1] - v[1]) % u[3])
+
+
+def needs(ops):
+    out, log = [], {}
+    for j, (q, rd, wr, f, dur, lag, after) in enumerate(ops):
+        p = dict(after)
+        views = [(v, False) for v in rd] + [(v, True) for v in wr]
+        for v, w in views:
+            for u, uw, i in log.get(v[0], []):
+                psum = v[0][0] == "P"
+                if (uw or w or psum) and meet(u, v):
+                    p[i] = max(p.get(i, 0), ops[i][4] + ops[i][5] + (0 if psum and ops[i][0] == q else WAKE))
+        for v, w in views:
+            log.setdefault(v[0], []).append((v, w, j))
+        out.append(p)
+    return out
+
+
+def placed(ops, pre, turn):
+    start, busy = [0.0] * len(ops), {}
+    for j in turn:
+        t, dur = max([0.0] + [start[i] + x for i, x in pre[j].items()]), ops[j][4]
+        if ops[j][0]:
+            line = busy.setdefault(ops[j][0], [])
+            at = 0
+            for a, z in line:
+                if t + dur <= a + 1e-9:
+                    break
+                t, at = max(t, z), at + 1
+            line.insert(at, (t, t + dur))
+        start[j] = t
+    return start
+
+
+def arrange(ops, pre):
+    n = len(ops)
+    post = [{n: o[5]} for o in ops] + [{}]
+    for j in range(n):
+        for i, t in pre[j].items():
+            post[i][j] = t + ops[j][4] - ops[i][4]
+    way = [o[4] + o[5] for o in ops]
+    for j in range(n - 1, -1, -1):
+        for i, t in pre[j].items():
+            way[i] = max(way[i], t + way[j])
+    turn, best = sorted(range(n), key=lambda j: (-way[j], j)), None
+    for rounds in range(4):
+        start = placed(ops, pre, turn)
+        end = max(start[j] + ops[j][4] + ops[j][5] for j in range(n))
+        if best is None or end < best[0] - 1e-6:
+            best = (end, sorted(range(n), key=lambda j: (start[j], j)))
+        late = placed(ops + [(None, 0, 0, 0, 0.0)], post, [n] + sorted(range(n), key=lambda j: (-start[j] - ops[j][4], -j)))
+        turn = sorted(range(n), key=lambda j: (-late[j] - ops[j][4], j))
+    return best[1]
+
+
 def helper_program(g, core, T, topo, r, h):
     ps = peers_of(T, topo, r)
-    sent = 0
+    off, rest = engine_sets(T, topo, r)
+    sent = [0]
+
+    def call(items):
+        g.remote_dma_fused([RemoteDMATransfer(dst_ids=[dst(topo, T.cores[d])], dma_engine_mask=bits(es), remote_sem=T.sem[sem], src=a, dst=b)
+                            for d, es, sem, a, b in items], local_sem=T.sem.sent)
+        sent[0] += sum(len(p[1]) for p in items)
+
+    def plane(k, i, es):
+        n, a, w, base = lot(k, i)
+        a, at = a - wide(k, h)[0], base + w * peers_of(T, topo, ps[i]).index(r)
+        return ps[i], es, "ar_s%d" % k, T["hs%d" % k][:, a:a + w], T[LAND[k][0] + "s"][:, at:at + w]
     if h < 2:
         d = [d for d in ps[2 * h:2 * h + 2] if topo.die(T.cores[d]) != topo.die(core)][0]
-        es, at = topo.engines(core, T.cores[d]), 24 * peers_of(T, topo, d).index(r)
-        g.wait_ge(T.sem.ar_hp, len(helper_engines(T, topo, r, 1)[h]))
-        g.remote_dma_fused([RemoteDMATransfer(dst_ids=[dst(topo, T.cores[d])], dma_engine_mask=bits(es), remote_sem=T.sem.ar_pd,
-                                              src=T.hp[:], dst=T.pin[:, at:at + 24])], local_sem=T.sem.sent)
-        sent += len(es)
+        at = 24 * peers_of(T, topo, d).index(r)
+        g.wait_ge(T.sem.ar_hp, len(rest) // 2)
+        call([(d, off, "ar_pd", T.hp[:], T.pin[:, at:at + 24])])
     for k in range(1, 5):
-        w, base = lot(k, 2 * h)[2:]
-        g.wait_ge(T.sem["ar_h%d" % k], len(helper_engines(T, topo, r, k)[h]))
-        tr = []
-        for i, es in handed(T, topo, r, h):
-            a, at = 0 if w == M else w * (i % 2), base + w * peers_of(T, topo, ps[i]).index(r)
-            tr.append(RemoteDMATransfer(dst_ids=[dst(topo, T.cores[ps[i]])], dma_engine_mask=bits(es), remote_sem=T.sem["ar_s%d" % k],
-                                        src=T["hs%d" % k][:, a:a + w], dst=T[LAND[k][0] + "s"][:, at:at + w]))
-            sent += len(es)
-        g.remote_dma_fused(tr, local_sem=T.sem.sent)
-        if k in VIA and 2 * h < WHOLE:
+        g.wait_ge(T.sem["ar_h%d" % k], len(rest) // (1 if h == 2 else 2))
+        call([plane(k, 2 * h + j, es) for j, es in enumerate(parts(off, 2))] + ([plane(k, NP - 1, rest)] if h == 2 else []))
+        if k < 3 and h < 2:
             s = [s for s in ps[:NP - 1] if far_helper(T, topo, s, h) == core][0]
-            g.wait_ge(T.sem["ar_g%d" % k], len(code_plan(T, topo, s, k)[0][h][2]))
-            tr = []
-            for d, es in on_chip(T, topo, r, h):
-                at = base + M * peers_of(T, topo, d).index(s)
-                tr.append(RemoteDMATransfer(dst_ids=[dst(topo, T.cores[d])], dma_engine_mask=bits(es), remote_sem=T.sem["ar_c%d" % k],
-                                            src=T["hc%d" % k][:].bitcast(dt.uint8), dst=T.wfq[:, at:at + M].bitcast(dt.uint8)))
-                sent += len(es)
-            g.remote_dma_fused(tr, local_sem=T.sem.sent)
-    g.wait_ge(T.sem.sent, sent)
+            g.wait_ge(T.sem["ar_g%d" % k], len(off) // 2)
+            items = []
+            for d, es in zip((r, ps[-1]), parts(off + rest, 2)):
+                at = lot(k, 0)[3] + M * peers_of(T, topo, d).index(s)
+                items.append((d, es, "ar_c%d" % k, T["hc%d" % k][:].bitcast(dt.uint8), T.wfq[:, at:at + M].bitcast(dt.uint8)))
+            call(items)
+    g.wait_ge(T.sem.sent, sent[0])
 
 
 def rank_program(g, core, T, topo):
@@ -204,23 +237,22 @@ def rank_program(g, core, T, topo):
     log = {}
     total = {}
     sent = [0]
-    held = [None]
+    ops = []
+    calls = []
 
     def A(name, a=0, b=None, step=1):
         if name in SMALL:
             at, n = SMALL[name]
             return ("sm", at + a, at + (n if b is None else b), step)
+        if name == "iot":
+            return ("ct", IOT + a, IOT + (C if b is None else b), step)
         return (name, a, SCRATCH[name][1][1] if b is None else b, step)
 
     def ap(v):
         return T[v[0]][:, v[1]:v[2]] if v[3] == 1 else T[v[0]][:, v[1]:v[2]:v[3]]
 
-    def meet(u, v):
-        if u[0][0] == "P":
-            return u[1] // 512 <= (v[2] - 1) // 512 and v[1] // 512 <= (u[2] - 1) // 512
-        if u[1] >= v[2] or v[1] >= u[2]:
-            return False
-        return not (u[3] == v[3] and u[3] > 1 and (u[1] - v[1]) % u[3])
+    def size(v):
+        return len(range(v[1], v[2], v[3]))
 
     def before(q, reads, writes):
         w = {}
@@ -241,41 +273,20 @@ def rank_program(g, core, T, topo):
             log.setdefault(v[0], []).append((v, wr, q, sem, val))
         total[sem] = max(total.get(sem, 0), val)
 
-    def weave(*chains):
-        out = []
-        for f in chains:
-            held[0] = []
-            f()
-            out.append(held[0])
-        held[0] = None
-        first, others = out[0], out[1:]
-        turn = 0
-        for i, (fs, rd, wr) in enumerate(first):
-            for f in fs:
-                f()
-            nxt = first[i + 1][1] + first[i + 1][2] if i + 1 < len(first) else []
-            others = [c for c in others if c]
-            if others and any(u[0] == v[0] and meet(u, v) for u in wr for v in nxt):
-                turn += 1
-                for f in others[turn % len(others)].pop(0)[0]:
-                    f()
-        while any(others):
-            for c in others:
-                for f in c.pop(0)[0] if c else ():
-                    f()
+    def put(q, reads, writes, issue, dur, lag=0.0, after=()):
+        ops.append((q, list(reads), list(writes), issue, dur, lag, dict(after)))
+        return len(ops) - 1
 
-    def hold(q, f, reads=(), writes=()):
-        if q == "v" or not held[0]:
-            held[0].append(([], list(reads), list(writes)))
-        held[0][-1][0].append(f)
+    def run(q, reads, writes, call, cycles, more=0.0, after=()):
+        def issue():
+            before(q, reads, writes)
+            cnt[q] += 1
+            call().then_inc(T.sem["q_" + q], 1)
+            note(q, reads, writes, "q_" + q, cnt[q])
+        return put(q, reads, writes, issue, more + CYC * max(64, cycles), after=after)
 
-    def run(q, reads, writes, call):
-        if held[0] is not None:
-            return hold(q, lambda: run(q, reads, writes, call), reads, writes)
-        before(q, reads, writes)
-        cnt[q] += 1
-        call().then_inc(T.sem["q_" + q], 1)
-        note(q, reads, writes, "q_" + q, cnt[q])
+    def cycles(o, *ins):
+        return size(o) * (0.5 if all(SCRATCH[v[0]][2] in (BF, U16) for v in (o,) + ins) else 1)
 
     def col(x):
         return ([x], ap(x)) if isinstance(x, tuple) else ([], x)
@@ -284,32 +295,35 @@ def rank_program(g, core, T, topo):
         return ap(v) if off is None else ap(v).indirect(ap(off))
 
     def cp(o, i, off=None):
-        run("v", [i] + ([off] if off else []), [o], lambda: g.vector.tensor_copy(ap(o), src(i, off)))
+        if off:
+            return run("v", [i, off], [o], lambda: g.vector.tensor_copy(ap(o), src(i, off)), GATHER * size(o), 0.055)
+        return run("v", [i], [o], lambda: g.vector.tensor_copy(ap(o), ap(i)), cycles(o, i))
 
     def scat(o, off, i):
-        run("v", [i, off], [o], lambda: g.vector.tensor_copy(ap(o).indirect(ap(off)), ap(i)))
+        run("v", [i, off], [o], lambda: g.vector.tensor_copy(ap(o).indirect(ap(off)), ap(i)), SCATTER * size(i), 0.055)
 
     def tt(o, a, b, op):
-        run("v", [a, b], [o], lambda: g.vector.tensor_tensor(ap(o), ap(a), ap(b), op))
+        run("v", [a, b], [o], lambda: g.vector.tensor_tensor(ap(o), ap(a), ap(b), op), size(o) * (1 if a[0][0] == "P" else 2))
 
     def ts(o, a, s1, op0, s2=None, op1=None):
-        r1, x1 = col(s1)
+        (r1, x1), (r2, x2) = col(s1), col(s2)
         if op1 is None:
-            run("v", [a] + r1, [o], lambda: g.vector.tensor_scalar(ap(o), ap(a), x1, None, op0))
+            run("v", [a] + r1, [o], lambda: g.vector.tensor_scalar(ap(o), ap(a), x1, None, op0), cycles(o, a))
         else:
-            run("v", [a] + r1, [o], lambda: g.vector.tensor_scalar(ap(o), ap(a), x1, s2, op0, op1))
+            run("v", [a] + r1 + r2, [o], lambda: g.vector.tensor_scalar(ap(o), ap(a), x1, x2, op0, op1), cycles(o, a))
 
     def scan(o, reset, d, op1=Op.add, op0=Op.mult, first=0.0):
-        run("v", [reset, d], [o], lambda: g.vector.tensor_tensor_scan(ap(o), ap(reset), ap(d), first, op0, op1))
+        r1, x1 = col(first)
+        return run("v", [reset, d] + r1, [o], lambda: g.vector.tensor_tensor_scan(ap(o), ap(reset), ap(d), x1, op0, op1), size(o))
 
     def summed(o, i):
-        run("v", [i], [o], lambda: g.vector.tensor_reduce(ap(o), ap(i), AxisListType.X, Op.add))
+        run("v", [i], [o], lambda: g.vector.tensor_reduce(ap(o), ap(i), AxisListType.X, Op.add), size(i))
 
     def trn(o, i):
-        run("v", [i], [o], lambda: g.vector.transpose(ap(o), ap(i)))
+        run("v", [i], [o], lambda: g.vector.transpose(ap(o), ap(i)), size(o))
 
     def fill(o, x):
-        run("v", [], [o], lambda: g.vector.memset(ap(o), x))
+        run("v", [], [o], lambda: g.vector.memset(ap(o), x), cycles(o))
 
     def act(o, i, f=Act.Copy, off=None, bias=None, scale=None):
         kw, rd = {}, [i] + ([off] if off else [])
@@ -317,93 +331,97 @@ def rank_program(g, core, T, topo):
             if x is not None:
                 rr, kw[k] = col(x)
                 rd = rd + rr
-        run("s", rd, [o], lambda: g.scalar.activation(ap(o), src(i, off), f, **kw))
+        run("s", rd, [o], lambda: g.scalar.activation(ap(o), src(i, off), f, **kw), size(o) * (GATHER if off else 1), 0.07 if off else 0.0)
 
     def iota(o, pat, base, cm=0):
-        if SCRATCH[o[0]][2] == I32:
-            run("g", [], [o], lambda: g.iota(ap(o), pat, base, cm))
-        else:
-            run("g", [], [o], lambda: g.iota(ap(o), pat, base, cm, allow_small_or_imprecise_dtypes=True))
-
-    def ones_where(o, pat, op, base, cm):
-        i = A("ones", 0, o[2] - o[1])
-        run("g", [i], [o], lambda: g.affine_select(ap(o), ap(i), pat, op, 0.0, base, cm))
+        kw = {} if SCRATCH[o[0]][2] == I32 else {"allow_small_or_imprecise_dtypes": True}
+        run("g", [], [o], lambda: g.iota(ap(o), pat, base, cm, **kw), 2 * size(o), 0.14, [(c, CALL) for c in calls[-1:]])
 
     def quant(qn, sn, a, n, i):
         o, s = A(qn, a, a + n), A(sn, a, a + n)
-        run("v", [i], [o, s], lambda: g.vector.quantize_mx(ap(o), ap(s), ap(i)))
+        run("v", [i], [o, s], lambda: g.vector.quantize_mx(ap(o), ap(s), ap(i)), 1.06 * n, 0.013)
 
     def mm(o, wn, wsn, a, xn, xsn, b, n, start=True, stop=True):
         w, ws, x, xs = A(wn, a, a + 128), A(wsn, a, a + 128), A(xn, b, b + n), A(xsn, b, b + n)
-        run("t", [w, ws, x, xs], [o], lambda: g.tensor.matmul_mx(ap(o), ap(w), ap(ws), ap(x), ap(xs), start, stop))
+        run("t", [w, ws, x, xs], [o], lambda: g.tensor.matmul_mx(ap(o), ap(w), ap(ws), ap(x), ap(xs), start, stop), 0.7 * (n + 16),
+            after=[(j, ops[j][4]) for j in range(len(ops)) if ops[j][0] == "t"][-1:])
 
     def pick(qo, so, a, qi, si, wlen, off):
         n = 16 * (off[2] - off[1])
         o, i = A(qo, a, a + n), A(qi, 0, wlen)
-        run("v", [i, off], [o], lambda: g.vector.tensor_copy(ap(o).bitcast(dt.uint32), ap(i).bitcast(dt.uint32).indirect(ap(off))))
+        run("v", [i, off], [o], lambda: g.vector.tensor_copy(ap(o).bitcast(dt.uint32), ap(i).bitcast(dt.uint32).indirect(ap(off))),
+            GATHER * n, 0.055)
         act(A(so, a, a + n), A(si, 0, wlen), off=off)
 
-    def dmas(sem, items):
-        for q, o, i, rd, wr in items:
-            before(q, rd, wr)
-            Q[q].dma_start(o, i).then_inc(T.sem[sem], 16)
-        for q, o, i, rd, wr in items:
-            note(q, rd, wr, sem, 16 * len(items))
+    def dmas(sem, items, lag, after=(), now=False):
+        def issue():
+            for q, o, i, rd, wr in items:
+                before(q, rd, wr)
+                Q[q].dma_start(o, i).then_inc(T.sem[sem], 16)
+            for q, o, i, rd, wr in items:
+                note(q, rd, wr, sem, 16 * len(items))
+        if now:
+            issue()
+        put(None if now else items[0][0], sum([p[3] for p in items], []), sum([p[4] for p in items], []),
+            (lambda: None) if now else issue, 0.0 if now else 0.05 * len(items), lag, after)
 
     def u8(v):
         return ap(v).bitcast(dt.uint8)
 
-    def call(items):
-        g.remote_dma_fused([RemoteDMATransfer(dst_ids=[dst(topo, c)], dma_engine_mask=bits(es), remote_sem=T.sem[sem], src=s, dst=d)
-                            for c, es, sem, s, d in items], local_sem=T.sem.sent)
-        sent[0] += sum(len(p[1]) for p in items)
+    def call(items, reads):
+        def issue():
+            before("g", reads, [])
+            g.remote_dma_fused([RemoteDMATransfer(dst_ids=[dst(topo, c)], dma_engine_mask=bits(es), remote_sem=T.sem[sem], src=s, dst=d)
+                                for c, es, sem, s, d in items], local_sem=T.sem.sent)
+            sent[0] += sum(len(p[1]) for p in items)
+        calls.append(put("g", reads, [], issue, CALL if calls else CALL + FIRST, after=[(c, ops[c][4]) for c in calls[-1:]]))
+
+    def lands(views, sem, val, *ways):
+        put(None, [], views, lambda: note("x", [], views, sem, val), 0.0, after=[(c, ops[c][4] + t) for c, t in zip(calls[::-1], ways)])
 
     def back(i):
         return peers_of(T, topo, ps[i]).index(r)
 
-    direct, n_relayed = arrivals(T, topo, r)
     off_chip, rest = engine_sets(T, topo, r)
 
     def exchange(k, piece=None):
         name, a0, z0 = LAND[k]
-        one, two = code_plan(T, topo, r, k)
-        he = helper_engines(T, topo, r, k)
 
         def ends(i, kind):
             n, a, w, base = lot(k, i)
             return A(n % kind, a, a + w), A(name + kind, base + w * back(i), base + w * back(i) + w)
 
-        def codes(part):
-            call([(T.cores[ps[i]], es, "ar_c%d" % k) + tuple(u8(v) for v in ends(i, "q")) if c is None else
-                  (far_helper(T, topo, r, c), es, "ar_g%d" % k, u8(ends(2 * c, "q")[0]), u8(A("hc%d" % k))) for i, c, es in part])
+        def far(h, es):
+            return far_helper(T, topo, r, h), es, "ar_g%d" % k, u8(ends(2 * h, "q")[0]), u8(A("hc%d" % k))
 
-        def relay(which):
-            items = []
-            for h in which:
-                n, a, w, base = lot(k, 2 * h)
-                w = w if w == M else 2 * w
-                items.append((hs[h], he[h], "ar_h%d" % k, ap(A(n % "s", a, a + w)), ap(A("hs%d" % k, 0, w))))
-            call(items)
-        before("g", [ends(i, kind)[0] for i in {None: range(NP), 0: range(4), 1: range(4, NP)}[piece] for kind in "qs"], [])
-        relay({None: (0, 1, 2), 0: (0, 1), 1: (2,)}[piece])
-        if piece != 1:
-            codes(one)
+        def plane(h):
+            a, w = wide(k, h)
+            return A(lot(k, 2 * h)[0] % "s", a, a + w)
+
+        def relay(h, es):
+            return hs[h], es, "ar_h%d" % k, ap(plane(h)), ap(A("hs%d" % k, 0, wide(k, h)[1]))
+
+        def codes(i, es):
+            return (T.cores[ps[i]], es, "ar_c%d" % k) + tuple(u8(v) for v in ends(i, "q"))
+        rd = [ends(i, "q")[0] for i in {None: range(NP), 0: range(4), 1: range(4, NP)}[piece]] + \
+            [plane(h) for h in {None: range(3), 0: range(2), 1: [2]}[piece]]
+        o2, r2, n, m = parts(off_chip, 2), parts(rest, 2), len(off_chip), len(rest)
+        if k < 3 and piece != 1:
+            call([relay(0, r2[0]), relay(1, r2[1])] + ([relay(2, off_chip)] if k == 1 else []), rd)
+            call([far(0, o2[0]), far(1, o2[1])] + ([codes(6, rest)] if k == 1 else []), rd)
+        elif piece == 0:
+            call([codes(i, es) for i, es in enumerate(parts(off_chip, 4))] + [relay(0, r2[0]), relay(1, r2[1])], rd)
         if piece == 0:
             return
-        codes(two)
-        call([(T.cores[ps[-1]], rest, "ar_s%d" % k) + tuple(ap(v) for v in ends(NP - 1, "s"))])
-        passed = len(on_chip(T, topo, r, 0)[0][1])
-        note("x", [], [A(name + "q", a0, z0)], "ar_c%d" % k, sum(passed if k in VIA and j < WHOLE else n for j, n in direct))
-        note("x", [], [A(name + "s", a0, z0)], "ar_s%d" % k, n_relayed)
+        call([codes(4, o2[0]), codes(5, o2[1])] + ([relay(2, rest)] if k > 1 else []), rd)
+        ways = ((0.0,) if k > 1 else ()) + WAY[k]
+        if k > 1:
+            call([codes(6, rest)], rd)
+        lands([A(name + "q", a0, z0)], "ar_c%d" % k, (2 * (n + m) if k < 3 else n) + n + m, *ways)
+        lands([A(name + "s", a0, z0)], "ar_s%d" % k, 3 * n + m, *ways)
 
     def bank(p, b, n):
         return A(p, 512 * b, 512 * b + n)
-
-    def scaled(q, o, i):
-        if q == "v":
-            ts(o, i, 0.03125, Op.mult)
-        else:
-            act(o, i, scale=0.03125)
 
     def plain(q, o, i, off=None):
         if q == "v":
@@ -411,48 +429,56 @@ def rank_program(g, core, T, topo):
         else:
             act(o, i, off=off)
 
+    OWN = A("pf", 0, 1)
     EXTRA = A("pf", 3, 4)
 
-    def to_table(w, n, a=0):
+    def to_table(w, n, a):
         scan(A("m2", a, a + n), A("keep", 0, n), w, Op.max, Op.add)
         return A("m2", a + 15, a + n, 16)
 
-    def spread_lists(win, level):
-        for k in range(2):
-            act(A("gx", 256 * k, 256 * k + 256), win, off=A("pd", 48 * k + 16 * level, 48 * k + 16 * level + 16))
-
-    def pair_lists(out):
-        trn(A("gt"), A("gx"))
+    def pair_lists(out, at):
+        trn(A("gt", at, at + 512), A("gx", at, at + 512))
         for h in range(2):
+            o, i = A(out, 16 * h, 16 * h + 16), A("gt", at + 16 * h, at + 512, 32)
             if out[0] == "f":
-                cp(A(out, 16 * h, 16 * h + 16), A("gt", 16 * h, 512, 32))
+                cp(o, i)
             else:
-                ts(A(out, 16 * h, 16 * h + 16), A("gt", 16 * h, 512, 32), 1.0 / LOW, Op.mult, M - (SH + RK * (r + 1)) / LOW, Op.add)
+                ts(o, i, 1.0 / LOW, Op.mult, M - (SH + RK * (r + 1)) / LOW, Op.add)
 
-    def gathered(k, name, wlen, lists, dn, d0, dw, slot, pause=None):
+    def forward_lists(out, at, t, wlen):
+        for h in range(2):
+            cp(A("u2", at // 16 + h, at // 16 + 32, 2), t)
+        act(A("gx", at, at + 512), A("uw", 0, wlen), off=A("u2", at // 16, at // 16 + 32))
+        pair_lists(out, at)
+
+    def backward_lists(out, at, level):
+        for k in range(2):
+            act(A("gx", at + 256 * k, at + 256 * k + 256), A("w2", SU0), off=A("pd", 48 * k + 16 * level, 48 * k + 16 * level + 16))
+        pair_lists(out, at)
+
+    def gathered(k, name, wlen, lists, dn, d0, dw, slot):
         pq, pp = "pk%d" % k, "ps%d" % k
         for a, b in ((0, 8), (8, 16), (16, 32)):
             pick(pq, pp, 16 * a, name + "q", name + "s", wlen, A(lists, a, b))
         for h in range(2):
             for b in range(4):
                 mm(bank("PA", b, M), "eeq", "ees", 128 * b, pq, pp, 128 * h, M, h == 0, False)
-        if pause:
-            pause()
         for b in range(4):
             mm(bank("PA", b, M), "eoq", "eos", 128 * b, pq, pp, 256, M, False, False)
             mm(bank("PA", b, M), "eoq", "eos", 128 * b, pq, pp, 384, M, False, True)
             tt(A("xs", 512 * slot + b, 512 * slot + 512, 4), bank("PA", b, M), A(dn, dw * b + d0, dw * b + d0 + M), Op.add)
         quant("xq", "xp", 128 * slot, M, A("xs", 512 * slot, 512 * slot + 512))
 
-    def layer(wn, wsn, slot, out, engines="vsvs"):
+    def layer(wn, wsn, slot, out):
         for b in range(4):
             mm(bank("PB", b, M), wn, wsn, 128 * b, "xq", "xp", 128 * slot, M)
-        return [lambda b=b: scaled(engines[b], out(b), bank("PB", b, M)) for b in range(4)]
+            if b % 2:
+                act(out(b), bank("PB", b, M), scale=0.03125)
+            else:
+                ts(out(b), bank("PB", b, M), 0.03125, Op.mult)
 
-    def send(k, evac, win, lists):
+    def send(k, win, lists):
         at = 4 * SL * (k - 3)
-        for f in evac:
-            f()
         for piece, (a, z) in enumerate(((0, 12), (12, 21))):
             for b in range(4):
                 plain("vs"[b % 2], A("st", at + 64 * a + b, at + 64 * z, 4), win(b), A(lists, a, z))
@@ -462,359 +488,278 @@ def rank_program(g, core, T, topo):
     def decode(qn, sn, a, n, out, engines="ssss"):
         for b in range(4):
             mm(bank("PA", b, n), "e1q", "e1s", 128 * b, qn, sn, a, n)
-        for b in range(4):
             plain(engines[b], out(b), bank("PA", b, n))
 
-    def constant(qn, i, b):
-        quant(qn + "q", qn + "s", 128 * b, 128, A("et", EW * i + 3 - b, EW * i + 515 - b))
+    def line(i, x, even, odd):
+        o = A("et", EW * i, EW * i + 512)
+        run("g", [A("zt")], [o], lambda: g.affine_select(ap(o), ap(A("zt")), [[-128, 4], [odd - even - 64, 2], [-1, 64]], Op.not_equal,
+                                                         x, 3 + even, 4), 1024, 0.18, [(c, CALL) for c in calls[-1:]])
+
+    def constants(qn, i):
+        for b in range(4):
+            quant(qn + "q", qn + "s", 128 * b, 128, A("et", EW * i + 3 - b, EW * i + 515 - b))
 
     def tile(name, i):
         return lambda b: A(name, 512 * i + b, 512 * i + 512, 4)
 
-    def level(l):
-        a = 2 - l
-        return (A("es", 256 * a, 256 * a + 256), A("si", SEG * a, SEG * a + 16), A("ci", SEG * a, SEG * a + 16),
-                A("pm", 8 * SEG * a + 7, 8 * SEG * a + 128, 8))
+    def flat(name, a, step):
+        return lambda b: A(name, a + step * b, a + step * b + M)
 
-    def numbered(l):
-        for k in range(2):
-            a = 16 * (2 - l) + 8 * k
-            ts(A("pn", a, a + 8), A("m2", M * l + 15, M * l + M, 16), EXTRA, Op.subtract, float(C * k - RK), Op.add)
-
-    def sort_entries(l, k):
-        a = 2 - l
-        act(A("es", 256 * a + M * k, 256 * a + M * k + M), A("eexp"), Act.Identity, off=A("pn", 16 * a + 8 * k, 16 * a + 8 * k + 8),
-            bias=float(C * k + 1))
-
-    def listed(l):
-        a = 2 - l
-        t = to_table(level(l)[0], 256, C * a)
-        return lambda: ts(A("vi", SEG * a, SEG * a + 16), t, EXTRA, Op.subtract, float(-C), Op.add)
-
-    def twice(k, h):
-        ts(A("pd", 48 * k + h, 48 * k + 48, 2), A("permu"), float(C * k), Op.add)
-
-    def slots():
-        W = 2 * SEG
-
-        def w(n):
-            return A(n, 0, W - 1)
-        one = listed(1)
-        quant("wfq", "wfs", FY, M, A("ti", 0, 512))
-        one()
-        ones_where(A("rp"), [[0, W - 1], [1, 8]], Op.is_gt, 0, 0)
-        iota(A("pl", 0, 256), [[0, 2], [LOW, M]], LOW * M)
-        iota(A("w2", NE, NE + SL), [[0, SL]], SH)
-        iota(A("zt"), [[0, 512]], 0)
-        iota(A("uw", UM), [[1, SL]], FL2)
-        constant("eo", 2, 0)
-        ts(w("si"), w("vi"), 1.0 / RK, Op.mult, RND, Op.add)
-        constant("eo", 2, 1)
-        for i in range(NP):
-            ts(A("oh", W * i + 1, W * i + W), w("si"), RND + ps[i] + 1, Op.is_equal)
-        ts(w("pv"), w("si"), RND, Op.subtract, float(-RK), Op.mult)
-        ts(w("on"), w("si"), RND + r + 1, Op.is_equal)
-        named(0)
-        scan(A("c1"), A("rs"), A("oh"))
-        tt(w("ci"), w("vi"), w("pv"), Op.add)
-        twice(0, 0)
-        cp(A("tot", 0, 2 * NP), A("c1", SEG - 1, None, SEG))
-        named(1)
-        ts(w("pv"), w("ci"), float(SU0 + C - 1), Op.add)
-        trn(A("tt"), A("tot"))
-        tt(A("kt", 0, 2 * NP), A("kc", 0, 2 * NP), A("tot", 0, 2 * NP), Op.subtract)
-        named(2)
-        scan(A("ts"), A("rt"), A("tt"))
-        tt(w("pv"), w("pv"), w("on"), Op.mult)
-        named(3)
-        trn(A("tb"), A("ts"))
-        named(4)
-        act(A("gx"), A("uw", 0, UM), off=A("u2"))
-        tt(A("prod", 7, None, 8), w("pv"), w("pu"), Op.max)
-        tt(A("oh", 0, None, SEG), A("tb", 0, 2 * NP), A("kt", 0, 2 * NP), Op.add)
-        ts(A("et", EW, 2 * EW), A("et", 0, EW), A("pe", 0, 1), Op.mult)
-        scan(A("c2"), A("rs"), A("oh"))
-        constant("ee", 1, 3)
-        for i in range(NP):
-            tt(A("prod", i, None, 8), A("oh", W * i + 1, W * i + W), A("c2", W * i + 1, W * i + W), Op.mult)
-        constant("ee", 1, 0)
-        scan(A("pm"), A("rp"), A("prod"), Op.max)
-        placed(2)
-        cp(A("ou", 0, 16), level(2)[3])
-        constant("ee", 1, 1)
-
-    def placed(l):
-        a = 256 * (2 - l)
-        scan(A("val", a, a + 256), A("pl", a, a + 256), level(l)[0], Op.add, Op.max)
-
-    def named(step):
-        if step == 0:
-            ts(A("a1", 0, 16), level(1)[1], RND, Op.subtract, float(C), Op.mult)
-        elif step == 1:
-            tt(A("a2", 0, 16), A("a1", 0, 16), level(1)[2], Op.add)
-        elif step == 2:
-            ts(A("a2", 8, 16), A("a2", 8, 16), float(-C), Op.add)
-        else:
-            cp(A("u2", step - 3, 32, 2), A("a2", 0, 16))
-
-    def fill_slots(l):
-        scat(A("w2"), A("ou", 16 * (2 - l), 16 * (3 - l)), A("val", 256 * (2 - l), 256 * (3 - l)))
-
-    def tables(l, meanwhile):
-        a, b, at = "req%d" % l, "rin%d" % l, NE + SL * (2 - l)
-        t = to_table(A("w2", at, at + SL), SL)
-        meanwhile()
-        ts(A(a, 0, 21), t, EXTRA, Op.subtract)
-        before("g", [A(a)], [])
+    def tables(l):
+        a, b, j = "req%d" % l, "rin%d" % l, 2 - l
+        val = A("val", 256 * j, 256 * j + 256)
+        scan(val, A("pl", 256 * j, 256 * j + 256), A("es", 256 * j, 256 * j + 256), Op.add, Op.max)
+        cp(A("ou", 16 * j, 16 * j + 16), A("pm", 8 * SEG * j + 7, 8 * SEG * j + 128, 8))
+        scat(A("w2"), A("ou", 16 * j, 16 * j + 16), val)
+        ts(A(a, 0, 21), to_table(A("w2", NE + SL * j, NE + SL * j + SL), SL, 896 + SL * j), EXTRA, Op.subtract)
         soon = list(enumerate(parts(off_chip, 2))) + [(NP - 1, rest)]
         late = [(2 + i, es) for i, es in enumerate(parts(off_chip, 4))]
-        for part, sem in ((soon, "ar_r%d" % l), (late, "ar_t%d" % l)):
-            call([(T.cores[ps[i]], es, sem, ap(A(a, 3 * i, 3 * i + 3)), ap(A(b, 3 * back(i), 3 * back(i) + 3))) for i, es in part])
-            for i in range(NP):
-                if direct[i][0] in dict(part):
-                    note("x", [], [A(b, 3 * i, 3 * i + 3)], sem, sum(len(es) for j, es in part))
-
-    def sent_from(l):
-        ts(A("hi", 0, 21), A("req%d" % l, 0, 21), 13, Op.arith_shift_right)
-        ts(A("h%d" % l, 0, 21), A("hi", 0, 21), float(M - M * l), Op.add, 0.0, Op.max)
+        for part, sem in ((soon, "ar_r"), (late, "ar_t")):
+            call([(T.cores[ps[i]], es, sem + str(l), ap(A(a, 3 * i, 3 * i + 3)), ap(A(b, 3 * back(i), 3 * back(i) + 3))) for i, es in part], [A(a)])
+            lands([A(b, 3 * i, 3 * i + 3) for i in range(NP) if back(i) in dict(part)], sem + str(l), sum(len(es) for i, es in part), WAY[sem])
+        ts(A("hi", 24 * j, 24 * j + 21), A(a, 0, 21), 13, Op.arith_shift_right)
+        ts(A("h%d" % l, 0, 21), A("hi", 24 * j, 24 * j + 21), float(M - M * l), Op.add, 0.0, Op.max)
 
     def asked(l, a, z):
         ts(A("lo", 24 * (2 - l) + a, 24 * (2 - l) + z), A("rin%d" % l, a, z), LOW - 1, Op.bitwise_and)
-        return A("lo", 24 * (2 - l), 24 * (2 - l) + 21)
 
-    def successors(l, low):
-        ts(A("xb3", 0, 21), low, float(SL - 1 - RK * (r + 1)), Op.add)
-        tt(A("xb3", 0, 21), A("xb3", 0, 21), A("nt", 0, 21), Op.max)
-        cp(A("suu", 0, 21), A("xb3", 0, 21))
-        scat(A("w2", NE + NS), A("suu", 0, 21), A("sud", SL * (2 - l), SL * (3 - l)))
+    def successors(l):
+        x, j = A("x%d" % l, 0, 21), 24 * (2 - l)
+        ts(x, A("lo", j, j + 21), float(SL - 1 - RK * (r + 1)), Op.add)
+        tt(x, x, A("nt", 0, 21), Op.max)
+        cp(A("suu", j, j + 21), x)
+        scat(A("w2", NE + NS), A("suu", j, j + 21), A("sud", SL * (2 - l), SL * (3 - l)))
 
     def coded(place):
         return LOW * (place - M) + SH + RK * (r + 1) + C
 
-    dmas("ld_l", [("ys"[i % 2], T.lvt[16 * i:16 * i + 16, :], T.lv[:], [], [A("lvt")]) for i in range(8)])
-    dmas("ld_e", [("y", T.e[:, 0:24], T.pr0[:], [], [A("e", 0, 24)]), ("y", T.e[:, 24:48], T.pr1[:], [], [A("e", 24, 48)])])
-    dmas("ld_x", [("y", T.xt[:], T.x[:], [], [A("xt")])])
-    dmas("ld_w", [("y", u8(A("wq")), T.wc[:], [], [A("wq")]), ("y", T.wp[:], T.ws[:], [], [A("wp")])])
-    dmas("ld_v", [("y", u8(A("vq")), T.vc[:], [], [A("vq")]), ("y", T.vp[:], T.vs[:], [], [A("vp")])])
-    dmas("ld_u", [("y", T.ut[:], T.u[:], [], [A("ut")])])
+    dmas("ld_l", [("ys"[i % 2], T.lvt[16 * i:16 * i + 16, :], T.lv[:], [], [A("lvt")]) for i in range(8)], 1.75, now=True)
+    dmas("ld_e", [("y", T.e[:, 0:24], T.pr0[:], [], [A("e", 0, 24)]), ("y", T.e[:, 24:48], T.pr1[:], [], [A("e", 24, 48)])], 2.4, now=True)
+    dmas("ld_x", [("y", T.xt[:], T.x[:], [], [A("xt")])], 3.8, now=True)
+    dmas("ld_w", [("y", u8(A("wq")), T.wc[:], [], [A("wq")]), ("y", T.wp[:], T.ws[:], [], [A("wp")])], 5.0, now=True)
 
+    fill(A("zt"), 0.0)
     fill(A("ones"), 1.0)
     iota(A("pc", 0, 1), [[0, 1]], 0, 1)
-    ones_where(A("et", 0, EW), [[-1, EW]], Op.is_equal, 3, 4)
-    iota(A("kc", 14, 17), [[M, 3]], -1)
-    iota(A("nt0"), [[16, 24]], 0)
-    iota(A("nm"), [[0, C // 16], [1, 16]], 0)
-    iota(A("io2"), [[FL1, 3], [1, M]], 0)
-    fill(A("lrs"), 1.0)
-    scan(A("iot"), A("ones", 0, C), A("ones", 0, C), first=-1.0)
-    for k in range(2):
-        act(A("w2", SU0 + C * k, SU0 + C * k + C), A("ones", 0, C), scale=float(coded(BZ)))
-    fill(A("rt"), 1.0)
-    fill(A("tot"), 0.0)
-    fill(A("loh", 0, None, LSEG), 0.0)
+    for i in range(3):
+        fill(A("et", EW * i + 512, EW * i + EW), 0.0)
+    line(0, 1.0, 0, 0)
+    iota(A("nm"), [[0, SL // 16], [1, 16]], 0)
+    scan(A("iot"), A("ones"), A("ones"), first=-1.0)
+    act(A("w2", SU0, SU0 + C), A("ones"), scale=float(coded(BZ)))
+    dmas("ld_s", [("y", ap(A("w2", SU0 + C)), ap(A("w2", SU0, SU0 + C)), [A("w2", SU0, SU0 + C)], [A("w2", SU0 + C)])], 4.5)
+    for name, n, step in (("lrs", 152, 0), ("rt", 32, 16), ("rs", 2 * NP * SEG, SEG), ("rp", 264, 8)):
+        fill(A(name), 1.0)
+        if step:
+            fill(A(name, 0, n, step), 0.0)
+    runs, threes = A("lrs", 0, 3 * LSEG), A("lrs", 80, 152)
+    fill(A("lrs", 0, 3 * LSEG, LSEG), 0.0)
+    fill(A("lrs", 80, 152, 3), 0.0)
+    for v in (A("tot"), A("kc"), A("loh", 0, None, LSEG), A("oh", 0, 2 * NP * SEG, SEG), A("vi", 16, 17), A("vn", 16, 17)):
+        fill(v, 0.0)
+    fill(A("si", 16, 17), 0)
     fill(A("ew", 0, 1), float(RK * (N + 1) + SH))
-    for name, step in (("lrs", LSEG), ("rt", 16)):
-        fill(A(name, 0, None, step), 0.0)
+    fill(A("uw", 0, UM, UM - 1), float(FZ))
     ts(A("pc", 1, 2), A("pc", 0, 1), 15, Op.bitwise_and)
-    ts(A("pc", 2, 3), A("pc", 0, 1), 16, Op.bitwise_and)
+    cp(OWN, A("pc", 1, 2))
     ts(A("pf", 1, 2), A("pc", 1, 2), -1.0, Op.mult, -0.5, Op.add)
-    cp(A("pf", 0, 1), A("pc", 1, 2))
-    ts(EXTRA, A("pc", 1, 2), float(-BIG), Op.mult, float(15 * BIG + SH), Op.add)
-    ts(A("pe", 0, 1), A("pc", 2, 3), 0.03125, Op.mult, -0.5, Op.add)
-    ts(A("pe", 1, 2), A("pc", 2, 3), -0.03125, Op.mult)
-    fill(A("vi"), 0.0)
-    fill(A("oh", 0, None, SEG), 0.0)
+    for b in range(4):
+        ts(A("pf", 3 + b, 4 + b), A("pc", 1, 2), float(-BIG), Op.mult, float(15 * BIG + SH - b), Op.add)
+    ts(A("pf", 7, 8), A("pc", 1, 2), float(-BIG), Op.mult, float(15 * BIG + SH + C), Op.add)
+    ts(A("kc", 14, 17), A("iot", 0, 3), float(M), Op.mult, -1.0, Op.add)
+    for h in range(2):
+        ts(A("kc", h, 2 * NP, 2), A("iot", 0, NP), float(CAP), Op.mult, float(NE - 1 + SL * h), Op.add)
+    trn(A("s2"), A("kc"))
+    ts(A("nt"), A("iot", 0, 24), 16.0, Op.mult, OWN, Op.add)
+    ts(A("pu", 0, SEG), A("iot", 0, SEG), 16.0, Op.mult, OWN, Op.add)
+    ts(A("pu", SEG, 33), A("iot", 0, 16), 16.0, Op.mult, OWN, Op.add)
     for s in range(N):
-        act(A("ew", 1 + C * s, 1 + C * s + C), A("iot"), Act.Identity, bias=float(RK * (s + 1) + SH))
-        if s == 5:
-            act(A("ma"), A("nm"), Act.Sign, bias=A("pf", 1, 2))
-            act(A("keep"), A("ma"), Act.Identity, bias=-15.5 * BIG, scale=16.5 * BIG)
+        if s < N - 2:
+            act(A("ew", 1 + C * s, 1 + C * s + C), A("iot"), Act.Identity, bias=float(RK * (s + 1) + SH))
+        else:
+            iota(A("ew", 1 + C * s, 1 + C * s + C), [[1, C]], RK * (s + 1) + SH)
+    act(A("ma"), A("nm"), Act.Sign, bias=A("pf", 1, 2))
+    act(A("keep"), A("ma"), Act.Identity, bias=-15.5 * BIG, scale=16.5 * BIG)
+    constants("e1", 0)
 
     for l in range(3):
         ts(A("loh", LSEG * l + 1, LSEG * l + LSEG), A("lvt"), float(l), Op.is_equal)
-    constant("e1", 0, 0)
-    for l in range(3):
         summed(A("tot", l, l + 1), A("loh", LSEG * l + 1, LSEG * l + LSEG))
-    constant("e1", 0, 1)
     trn(A("tt"), A("tot"))
-    tt(A("kt", 0, 3), A("kc", 14, 17), A("tot", 0, 3), Op.subtract)
     scan(A("ts"), A("rt"), A("tt"))
-    constant("e1", 0, 2)
     trn(A("tb"), A("ts"))
-    ts(A("u1"), A("e"), 1.0, Op.add)
-    ts(A("nt"), A("nt0"), A("pf", 0, 1), Op.add)
-    tt(A("loh", 0, None, LSEG), A("tb", 0, 3), A("kt", 0, 3), Op.add)
-    constant("e1", 0, 3)
-    scan(A("lc2"), A("lrs"), A("loh"))
-    ts(A("pu", 0, SEG), A("nt0", 0, SEG), A("pf", 0, 1), Op.add)
-    tt(A("lc1"), A("loh"), A("lc2"), Op.mult)
-    cp(A("pu", SEG, 2 * SEG - 1), A("nt", 0, 16))
-    tt(A("pos"), A("lc1", 1, LSEG), A("lc1", LSEG + 1, 2 * LSEG), Op.add)
-    ts(A("pf", 4, 5), EXTRA, -1.0, Op.add)
-    tt(A("pos"), A("pos"), A("lc1", 2 * LSEG + 1, 3 * LSEG), Op.add)
-    ts(A("pf", 5, 6), EXTRA, -2.0, Op.add)
-    cp(A("posu"), A("pos"))
-    before("g", [A("posu")], [])
+    scan(A("lc2"), runs, A("loh"))
+    ts(A("lc1"), A("loh"), -1.0, Op.add, 1024.0, Op.mult)
+    tt(A("lc1"), A("lc1"), A("lc2"), Op.add)
+    tt(A("kt", 0, 3), A("kc", 14, 17), A("tot", 0, 3), Op.subtract)
+    for l in range(3):
+        ts(A("lc3", l, 72, 3), A("lc1", LSEG * l + 1, LSEG * l + LSEG), A("tb", l, l + 1), Op.add, A("kt", l, l + 1), Op.add)
+    scan(A("lc3", 72), threes, A("lc3", 0, 72), Op.max)
+    cp(A("posu"), A("lc3", 74, 144, 3))
     halves = parts(off_chip, 2)
     same = [i for i in range(4) if topo.die(T.cores[ps[i]]) == topo.die(core)]
     plan = [[(same[0], halves[0], "ar_pa"), (same[1], halves[1], "ar_pa")],
             [(4, halves[0], "ar_pb"), (5, halves[1], "ar_pb"), (NP - 1, rest, "ar_pc")]]
     for j, part in enumerate(plan):
         call([(T.cores[ps[i]], es, sem, ap(A("posu")), ap(A("pin", 24 * back(i), 24 * back(i) + 24))) for i, es, sem in part] +
-             [(hs[h], helper_engines(T, topo, r, 1)[h], "ar_hp", ap(A("posu")), ap(A("hp"))) for h in range(2 - 2 * j)])
-    PSEM = [("ar_pa" if topo.die(T.cores[ps[i]]) == topo.die(core) else "ar_pd") if j < 4 else "ar_pb" if j < 6 else "ar_pc"
-            for i, (j, n) in enumerate(direct)]
-    for i in range(NP):
-        note("x", [], [A("pin", 24 * i, 24 * i + 24)], PSEM[i], len(off_chip) * (2 if PSEM[i] == "ar_pd" else 1))
-    iota(A("kc", 0, 14), [[CAP, NP], [SL, 2]], NE - 1)
-    ones_where(A("rs"), [[0, 2 * NP], [1, SEG]], Op.is_gt, 0, 0)
-    fill(A("uw", 0, UM, UM - 1), float(FZ))
-    scat(A("pw"), A("posu"), A("ew", 1, 1 + C))
-    act(A("eexp", 0, C), A("ew"), off=A("u1", 0, 24))
-    act(A("eexp", C, NE), A("ew"), off=A("u1", 24, 48))
-    quant("sq", "ss", 0, C, A("xt"))
-    first = to_table(A("pw", 0, M), M)
-    to_table(A("pw", M, C), C - M, M)
-    ts(A("permu", 0, 8), first, EXTRA, Op.subtract, float(-RK), Op.add)
+             [(hs[h], parts(rest, 2)[h], "ar_hp", ap(A("posu")), ap(A("hp"))) for h in range(2 - 2 * j)], [A("posu")])
+    PSEM = [("ar_pa" if topo.die(T.cores[ps[i]]) == topo.die(core) else "ar_pd") if back(i) < 4 else "ar_pb" if back(i) < 6 else "ar_pc"
+            for i in range(NP)]
+    turn = sorted(range(NP), key=lambda i: ("cabd".index(PSEM[i][-1]), i))
+    for i in turn:
+        lands([A("pin", 24 * i, 24 * i + 24)], PSEM[i], len(off_chip) * (2 if PSEM[i] == "ar_pd" else 1), WAY[PSEM[i]])
+    iota(A("io2"), [[FL1, 3], [1, M]], 0)
+    iota(A("pl", 0, 256), [[0, 2], [LOW, M]], LOW * M)
+    scat(A("pw", 0, C), A("posu"), A("ew", 1, 1 + C))
+    ts(A("permu", 0, 8), to_table(A("pw", 0, M), M, 0), EXTRA, Op.subtract, float(-RK), Op.add)
+    ts(A("permu", 8, 24), to_table(A("pw", M, C), C - M, M), EXTRA, Op.subtract, float(-RK), Op.add)
 
-    numbered(2)
+    quant("sq", "ss", 0, C, A("xt"))
     pick("spq", "sps", 0, "sq", "ss", C, A("permu", 0, 8))
-    sort_entries(2, 0)
-    numbered(1)
-    ts(A("permu", 8, 24), A("m2", M + 15, C, 16), EXTRA, Op.subtract, float(-RK), Op.add)
-    ts(A("pf", 6, 7), EXTRA, -3.0, Op.add)
     decode("spq", "sps", 0, M, tile("xs", 6), "vsvs")
-    sort_entries(2, 1)
-    sort_entries(1, 0)
     quant("xq", "xp", 128 * 6, M, A("xs", 512 * 6, 512 * 7))
-    ev = layer("wq", "wp", 6, tile("ti", 0))
-    ts(A("et", 2 * EW, 3 * EW), A("et", 0, EW), A("pe", 1, 2), Op.mult)
-    for f in ev:
-        f()
-    sort_entries(1, 1)
-    two = listed(2)
+    layer("wq", "wp", 6, tile("ti", 0))
     quant("swq1", "sws1", 0, M, A("ti", 0, 512))
     exchange(1)
-    two()
+    quant("wfq", "wfs", FY, M, A("ti", 0, 512))
+    iota(A("w2", NE, NE + SL), [[0, SL]], SH)
+    line(1, -0.5, 0, 1024)
+    line(2, -0.5, 1024, 0)
+    constants("ee", 1)
+    constants("eo", 2)
+    quant("wfq", "wfs", FZ, M, A("zt"))
 
-    def place(i):
+    ts(A("u1"), A("e"), 1.0, Op.add)
+    for a in range(0, 48, 12):
+        act(A("eexp", 16 * a, 16 * a + 192), A("ew"), off=A("u1", a, a + 12))
+    for j in range(2):
+        l = 2 - j
+        for k in range(2):
+            a = 16 * j + 8 * k
+            ts(A("pn", a, a + 8), A("m2", M * l + 15, M * l + M, 16), EXTRA, Op.subtract, float(-RK), Op.add)
+            act(A("es", 16 * a, 16 * a + M), A("eexp", C * k, C * k + C), Act.Identity, off=A("pn", a, a + 8), bias=float(C * k + 1))
+        t = to_table(A("es", 256 * j, 256 * j + 256), 256, C + 256 * j)
+        ts(A("si", SEG * j, SEG * j + 16), t, A("pf", 7, 8), Op.subtract, 1.0 / RK, Op.mult)
+        ts(A("vi", SEG * j, SEG * j + 16), t, EXTRA, Op.subtract, float(SU0 - 1 - RK * (r + 1)), Op.add)
+        for k in range(2):
+            a = C + 256 * j + M * k
+            ts(A("vn", SEG * j + 8 * k, SEG * j + 8 * k + 8), A("m2", a + 15, a + M, 16), EXTRA, Op.subtract, float(-C - C * k), Op.add)
+    ts(A("pv"), A("si"), float(C - RK), Op.mult)
+    tt(A("n1"), A("vn"), A("pv"), Op.add)
+
+    for i in [NP] + turn:
         s, off = (r, A("posu")) if i == NP else (ps[i], A("pin", 24 * i, 24 * i + 24))
         act(A("uw", 1 + C * s, 1 + C * s + C), A("iot" if i == NP else "io2"), Act.Identity, off=off, bias=float(M * i))
-    place(NP)
-    for i in sorted(range(NP), key=lambda i: ("cabd".index(PSEM[i][-1]), i)):
-        place(i)
-    slots()
-    fill_slots(2)
-    constant("ee", 1, 2)
-    tables(2, lambda: pick("spq", "sps", M, "sq", "ss", C, A("permu", 8, 16)))
-    iota(A("sud", 0, SL), [[LOW, SL]], coded(BL3))
-    iota(A("pl", 256, 512), [[0, 2], [LOW, M]], 0)
-    decode("spq", "sps", M, M, lambda b: A("ds", 256 * b, 256 * b + M))
-    trn(A("gt"), A("gx"))
-    quant("wfq", "wfs", FZ, M, A("zt"))
-    cp(A("f1", 0, 16), A("gt", 0, 512, 32))
-    cp(A("f1", 16, 32), A("gt", 16, 512, 32))
-    twice(0, 1)
+    forward_lists("f1", 0, A("n1", SEG, 33), UM)
 
-    def own():
-        constant("eo", 2, 2)
-        constant("eo", 2, 3)
-        for k in range(2):
-            act(A("pp", C * k, C * k + C), A("uw", 1 + C * r, 1 + C * r + C), Act.Identity, bias=float(SH - 4 * M * NP), scale=4.0)
-    gathered(1, "wf", FL2, "f1", "ds", 0, 256, 0, own)
-    ev = layer("wq", "wp", 0, tile("ti", 1), "vsvv")
-    low = asked(2, 12, 21)
-    ts(A("a2", 0, 16), level(2)[3], float(UM - NE), Op.add)
-    ts(A("c2u", 12, 21), A("lo", 12, 21), float(-1 - RK * (r + 1)), Op.add, 0.0, Op.max)
-    act(A("pw", 0, 144), A("pp"), off=A("c2u", 12, 21))
-    for f in ev:
-        f()
-    t = to_table(A("pw", 0, 144), 144)
+    W = 2 * SEG
+    for i in range(NP):
+        ts(A("oh", W * i + 1, W * i + W), A("si"), float(ps[i] + 1), Op.is_equal)
+    counted = scan(A("ct", 0, NP * W), A("rs"), A("oh", 0, NP * W))
+    trn(A("t2"), A("ct", SEG - 1, 32 * SEG, SEG))
+    for h in (0, 16):
+        scan(A("s2", h + 1, h + 16), A("ones", 0, 15), A("t2", h, h + 15), first=A("s2", h, h + 1))
+    trn(A("oh", 0, None, SEG), A("s2"))
+    scan(A("c2"), A("rs"), A("oh", 0, NP * W))
+    for i in range(NP):
+        tt(A("prod", i, None, 8), A("oh", W * i + 1, W * i + W), A("c2", W * i + 1, W * i + W), Op.mult)
+    ts(A("on"), A("si"), float(r + 1), Op.is_equal)
+    tt(A("vi"), A("vi"), A("on"), Op.mult)
+    tt(A("prod", 7, None, 8), A("vi"), A("pu"), Op.max)
+    scan(A("pm"), A("rp"), A("prod"), Op.max)
+    tables(2)
+    dmas("ld_v", [("y", u8(A("vq")), T.vc[:], [], [A("vq")]), ("y", T.vp[:], T.vs[:], [], [A("vp")])], 4.0, [(counted, 0.0)])
+    dmas("ld_u", [("y", T.ut[:], T.u[:], [], [A("ut")])], 4.0, [(counted, 0.0)])
+
+    pick("spq", "sps", M, "sq", "ss", C, A("permu", 8, 16))
+    decode("spq", "sps", M, M, flat("ds", 0, 256))
+    gathered(1, "wf", FL2, "f1", "ds", 0, 256, 0)
+    layer("wq", "wp", 0, tile("ti", 1))
     quant("swq2", "sws2", 0, M, A("ti", 512, 1024))
     exchange(2, 0)
-    for b in (1, 0, 3, 2):
-        ts(A("g2", 10 * b, 10 * b + 9), t, A("pf", 3 + b, 4 + b), Op.subtract, float(8 * M - 4 + b), Op.min)
+    for k in range(2):
+        act(A("pp", C * k, C * k + C), A("uw", 1 + C * r, 1 + C * r + C), Act.Identity, bias=float(SH - 4 * M * NP), scale=4.0)
+    asked(2, 12, 21)
+    ts(A("c2u", 12, 21), A("lo", 12, 21), float(-1 - RK * (r + 1)), Op.add, 0.0, Op.max)
+    act(A("pw", C), A("pp"), off=A("c2u", 12, 21))
+    t = to_table(A("pw", C), 144, 1568)
+    act(A("st", 8 * SL + 576), A("zt", 0, 192))
     for b in range(4):
+        ts(A("g2", 10 * b, 10 * b + 9), t, A("pf", 3 + b, 4 + b), Op.subtract, float(8 * M - 4 + b), Op.min)
         plain("vs"[b % 2], A("st", 8 * SL + b, 8 * SL + 576, 4), A("ti", 0, 1024), A("g2", 10 * b, 10 * b + 9))
-    ts(A("a3", 0, 16), level(2)[3], float(NE), Op.is_ge)
-    quant("sdq2", "sds2", 0, 144, A("st", 8 * SL, 8 * SL + 576))
+    quant("sdq2", "sds2", 0, 4 * CAP, A("st", 8 * SL))
     exchange(2, 1)
+    quant("wfq", "wfs", FY + M, M, A("ti", 512, 1024))
     iota(A("w2", NE + SL, NE + NS), [[0, SL]], SH)
     iota(A("sud", SL, NS), [[LOW, SL]], coded(BL4))
 
-    def places():
-        es, si, ci, O = level(2)
-        whole = [A("oh", 2 * SEG * i + 1, 2 * SEG * i + SEG) for i in range(NP) if direct[i][0] < WHOLE]
-        a1, a2, a3, a4, a5 = [A("a%d" % i, 0, 16) for i in range(1, 6)]
-        ts(a1, si, RND, Op.subtract, float(C), Op.mult)
-        tt(a4, whole[0], whole[1], Op.add)
-        tt(a5, whole[2], whole[3], Op.add)
-        tt(a1, a1, ci, Op.add)
-        tt(a4, a4, A("on", 0, 16), Op.add)
-        ts(A("a1", 8, 16), A("a1", 8, 16), float(-C), Op.add)
-        tt(a4, a4, a5, Op.add)
-        tt(a2, a2, a3, Op.mult)
-        tt(a1, a1, a2, Op.subtract)
-        tt(a1, a1, a4, Op.mult)
-        tt(a5, a1, a2, Op.add)
+    act(A("uw", UM), A("iot", 0, SL), Act.Identity, bias=float(FL2))
+    a1, a2, a3, a4 = [A("a%d" % i, 0, 16) for i in range(1, 5)]
+    by_slot = [A("oh", W * i + 1, W * i + SEG) for i in range(NP) if back(i) >= WHOLE]
+    tt(a1, by_slot[0], by_slot[1], Op.add)
+    tt(a1, a1, by_slot[2], Op.add)
+    ts(a2, A("n1", 0, 16), -1.0, Op.mult, float(UM - NE), Op.add)
+    tt(a3, a2, A("pm", 7, 128, 8), Op.add)
+    tt(a3, a3, a1, Op.mult)
+    tt(a4, a3, A("n1", 0, 16), Op.add)
+    forward_lists("f2", 512, a4, UM + SL)
+    for k in range(2):
         for h in range(2):
-            cp(A("u2", h, 32, 2), a5)
-        act(A("gx"), A("uw"), off=A("u2"))
-    weave(places, lambda: (twice(1, 0), twice(1, 1), sent_from(2), cp(A("ou", 16, 32), level(1)[3])))
+            ts(A("pd", 48 * k + h, 48 * k + 48, 2), A("permu"), float(C * k), Op.add)
+        act(A("pl", 256 + M * k, 256 + M * k + M), A("iot", 0, M), scale=float(LOW))
+    act(A("sud", 0, SL), A("iot", 0, SL), Act.Identity, bias=float(coded(BL3)), scale=float(LOW))
     asked(2, 0, 12)
-    pick("spq", "sps", 2 * M, "sq", "ss", C, A("permu", 16, 24))
-    decode("spq", "sps", 2 * M, M, lambda b: A("ds", 256 * b + M, 256 * b + 256))
-    weave(lambda: successors(2, low), lambda: (quant("wfq", "wfs", FY + M, M, A("ti", 512, 1024)), placed(1)))
-    pair_lists("f2")
+    successors(2)
+    backward_lists("b1", 0, 1)
 
+    pick("spq", "sps", 2 * M, "sq", "ss", C, A("permu", 16, 24))
+    decode("spq", "sps", 2 * M, M, flat("ds", M, 256))
     gathered(2, "wf", FW, "f2", "ds", 128, 256, 1)
-    for f in layer("wq", "wp", 1, tile("xs", 2)):
-        f()
+    layer("wq", "wp", 1, tile("xs", 2))
     quant("xq", "xp", 256, M, A("xs", 1024, 1536))
     decode("xq", "xp", 256, M, tile("xs", 3), "vsvs")
     quant("xq", "xp", 384, M, A("xs", 1536, 2048))
-    ev = layer("vq", "vp", 3, lambda b: A("zp", 128 * b, 128 * b + M))
-    send(3, ev, lambda b: A("zp", 128 * b, 128 * b + M), "h2")
-
-    SU = A("w2", SU0)
+    layer("vq", "vp", 3, flat("zp", 0, M))
+    send(3, flat("zp", 0, M), "h2")
     for b in range(4):
-        act(tile("ti", 2)(b), A("zp", 128 * b, 128 * b + M))
-    spread_lists(SU, 1)
+        act(tile("ti", 2)(b), flat("zp", 0, M)(b))
     decode("wfq", "wfs", FY, 256, lambda b: A("dy", 256 * b, 256 * b + 256))
     quant("wbq", "wbs", BZ, M, A("zt"))
     quant("wbq", "wbs", 2 * M, M, A("ti", 1024, 1536))
-    pair_lists("b1")
-    fill_slots(1)
-    quant("uq", "us", 0, 128, A("ut"))
-    tables(1, lambda: None)
-    sent_from(1)
+    tables(1)
 
     gathered(3, "wb", BL4, "b1", "dy", M, 256, 4)
-    ev = layer("vq", "vp", 4, lambda b: A("zp", 512 + 128 * b, 512 + 128 * b + M))
-    send(4, ev, lambda b: A("zp", 512 + 128 * b, 512 + 128 * b + M), "h1")
-
-    successors(1, asked(1, 0, 21))
-    spread_lists(SU, 0)
+    layer("vq", "vp", 4, flat("zp", 512, M))
+    send(4, flat("zp", 512, M), "h1")
+    asked(1, 0, 21)
+    successors(1)
+    backward_lists("b0", 512, 0)
     for b in range(4):
-        act(tile("ti", 3)(b), A("zp", 512 + 128 * b, 512 + 128 * b + M))
-    pair_lists("b0")
+        act(tile("ti", 3)(b), flat("zp", 512, M)(b))
     quant("wbq", "wbs", M, M, A("ti", 1536, 2048))
+    quant("uq", "us", 0, 128, A("ut"))
     mm(bank("PB", 0, 256), "uq", "us", 0, "wbq", "wbs", M, 256)
     act(A("ys", M, C), bank("PB", 0, 256))
 
     gathered(4, "wb", BW, "b0", "dy", 0, 256, 5)
-    for f in layer("vq", "vp", 5, tile("ti", 4)):
-        f()
+    layer("vq", "vp", 5, tile("ti", 4))
     quant("wbq", "wbs", 0, M, A("ti", 2048, 2560))
     mm(bank("PA", 0, M), "uq", "us", 0, "wbq", "wbs", 0, M)
     pick("oq", "opl", 0, "wbq", "wbs", C, A("posu"))
     act(A("ys", 0, M), bank("PA", 0, M))
-    dmas("st_c", [("y", T.oc[:], u8(A("oq")), [A("oq")], [])])
-    dmas("st_s", [("y", T.osc[4 * k:4 * k + 4, :], T.opl[32 * k:32 * k + 4, :], [A("opl")], []) for k in range(4)])
+    dmas("st_c", [("y", T.oc[:], u8(A("oq")), [A("oq")], [])], 2.4)
+    dmas("st_s", [("y", T.osc[4 * k:4 * k + 4, :], T.opl[32 * k:32 * k + 4, :], [A("opl")], []) for k in range(4)], 2.2)
     for h in range(2):
         plain("vs"[h], A("yo", 192 * h, 192 * h + 192), A("ys"), A("posu", 12 * h, 12 * h + 12))
-    dmas("st_y", [("s", T.y[:], T.yo[:], [A("yo")], [])])
+    dmas("st_y", [("y", T.y[:], T.yo[:], [A("yo")], [])], 2.4)
 
+    pre = needs(ops)
+    if not ORDER:
+        ORDER.extend(arrange(ops, pre))
+    at = {j: i for i, j in enumerate(ORDER)}
+    assert len(at) == len(ops) and all(at[i] < at[j] for j in range(len(ops)) for i in pre[j])
+    for j in ORDER:
+        ops[j][3]()
     g.wait_ge(T.sem.sent, sent[0])
     for sem, val in total.items():
         g.wait_ge(T.sem[sem], val)

@@ -11,7 +11,7 @@ BZ, BL3, BL4, BW = 384, 512, 512 + SL, 512 + 2 * SL
 NE, NS = 2 * C, 2 * SL
 SEG, LSEG = 17, 25
 UM = 2 + N * C
-EW = 528
+EW = 512
 RK = 800
 LOW = 8192
 BIG = 256 * LOW
@@ -19,22 +19,40 @@ SH = 128 - 8 * BIG
 SU0 = NE + NS + SL
 IOT = 240
 LAND = {1: ("wf", 0, FY), 2: ("wf", FL2, FW), 3: ("wb", BL3, BL4), 4: ("wb", BL4, BW)}
-CYC, WAKE, CALL, FIRST, GATHER, SCATTER = 0.00096, 0.18, 0.2, 1.4, 1.65, 4.0
+CYC, WAKE, CALL, FIRST, GATHER, SCATTER = 0.00091, 0.23, 0.2, 1.6, 1.8, 4.5
 WAY = {"ar_pa": 2.0, "ar_pb": 2.6, "ar_pc": 2.0, "ar_pd": 4.6, "ar_r": 1.8, "ar_t": 5.0,
-       1: (4.0, 4.6), 2: (3.6, 4.6), 3: (3.6, 4.2), 4: (3.6, 4.2)}
-ORDER = []
+       1: (3.8, 4.4), 2: (3.2, 4.2), 3: (3.2, 3.8), 4: (3.2, 3.8)}
+ORDER = [int(_n) for _n in """
+5 22 27 6 46 9 0 16 10 24 29 14 1 13 4 2 3 11 12 40 44 15 23 8 32 37 20 34 7 26 31 42 41 54 56 58 35 55 57 59 63 64 47 48 28 45 60 21 43
+65 61 66 50 49 62 17 304 36 130 132 67 69 68 52 70 25 30 33 133 71 51 82 39 131 157 89 134 83 90 88 84 72 260 53 92 259 86 73 81 91 135
+136 85 93 18 137 95 87 96 97 99 100 138 147 145 94 146 98 139 129 101 301 74 75 143 76 148 140 300 102 149 103 104 106 150 108 77 107 141
+78 105 109 151 158 38 110 174 172 176 111 177 171 173 175 154 153 142 152 178 112 113 117 191 116 179 160 162 159 192 119 144 155 79 180
+181 161 80 164 193 195 182 156 196 183 166 165 19 185 190 184 186 187 188 118 189 121 290 194 288 122 120 197 289 302 291 163 198 211 199
+201 200 212 123 202 124 292 126 167 168 114 115 127 293 169 265 203 125 170 213 214 221 223 215 216 205 217 219 218 220 209 225 222 224
+295 128 294 210 227 228 226 229 230 204 261 231 232 287 233 234 235 306 334 236 262 238 239 237 241 242 244 263 245 240 243 246 296 264
+247 207 267 248 266 250 252 254 303 268 249 253 333 251 255 256 269 271 335 273 337 339 272 257 270 341 276 208 277 258 206 278 279 321
+336 338 340 308 274 307 342 305 275 280 281 285 322 297 282 286 309 299 323 430 310 324 312 311 313 325 314 315 298 317 283 284 344 346
+319 343 345 347 349 348 350 351 352 326 353 354 355 356 357 358 359 360 316 361 362 363 364 365 366 367 368 369 327 370 372 374 376 371
+373 320 375 377 328 378 379 381 383 385 380 382 384 386 318 387 490 388 329 491 390 392 394 389 422 492 391 393 395 396 424 398 397 403
+399 400 405 411 426 428 404 406 407 410 412 401 418 402 419 420 409 413 421 330 493 423 408 414 425 431 415 427 331 332 429 494 495 496
+416 417 433 435 432 434 489 438 436 437 439 497 440 441 442 443 498 444 445 446 447 449 450 452 448 453 455 451 456 454 457 458 499 459
+461 463 465 460 462 464 466 468 467 469 470 474 475 471 477 476 481 483 482 472 502 500 473 503 478 504 480 484 505 507 479 501 485 506
+486 508 509 487 488 511 513 510 512 516 514 515 517 518 519 520 521 522 523 524 525 527 528 530 526 531 533 529 534 532 535 536 537 539
+541 543 538 540 542 544 545 547 546 549 553 552 550 548 554 551""".split()]
 
 
 def lot(k, i):
     if k == 1 or k == 2 and i < WHOLE:
         return "sw%%s%d" % k, 0, M, FL1 * (k - 1)
-    return "sd%%s%d" % k, CAP * (i - WHOLE * (k == 2)), CAP, LAND[k][1]
+    return "sd%%s%d" % k, CAP * i + (0, 0, 32, 112)[i // 2], CAP, LAND[k][1]
 
 
 def wide(k, h):
     if lot(k, 2 * h)[2] == M:
         return 0, M
-    return (0 if h < 2 or k == 2 else SL - 4 * CAP), 4 * CAP
+    if h < 2:
+        return 2 * CAP * h, 2 * CAP
+    return M, 4 * CAP
 
 
 def _sb(n, d):
@@ -42,9 +60,9 @@ def _sb(n, d):
 
 
 SMALL = {}
-for _n in ("tot", "tt", "ts", "tb", "rt", "kc", "kt", "t2", "s2", "nt", "a1", "a2", "a3", "a4", "x1", "x2",
+for _n in ("tot", "kc", "tt", "ts", "tb", "rt", "kt", "t2", "s2", "a1", "a2", "a3", "a4", "x1", "x2",
            "vi", "vn", "pv", "n1", "on", "pu"):
-    SMALL[_n] = (40 * len(SMALL), 32 if len(SMALL) < 9 else 24 if len(SMALL) < 16 else 33)
+    SMALL[_n] = (40 * len(SMALL), 32 if len(SMALL) < 9 else 24 if len(SMALL) < 15 else 33)
 
 SCRATCH = {
     "sm": _sb(40 * len(SMALL), F32), "e": _sb(48, I32), "lvt": _sb(24, I32), "ct": _sb(IOT + C, F32), "io2": _sb(C, F32),
@@ -53,35 +71,34 @@ SCRATCH = {
     "prod": _sb(264, F32), "rp": _sb(264, BF), "pm": _sb(264, F32),
     "loh": _sb(3 * LSEG, F32), "lrs": _sb(152, BF), "lc1": _sb(3 * LSEG, F32), "lc2": _sb(3 * LSEG, F32), "lc3": _sb(144, F32),
     "ou": _sb(32, U16), "pp": _sb(NE, F32), "posu": _sb(24, U16), "pin": _sb(24 * NP, U16), "pc": _sb(4, I32), "pf": _sb(8, F32),
-    "nm": _sb(SL, BF), "ma": _sb(SL, BF), "keep": _sb(SL, BF), "m2": _sb(1712, F32),
+    "nm": _sb(144, BF), "ma": _sb(144, BF), "keep": _sb(144, BF), "m2": _sb(1712, F32),
     "req1": _sb(24, I32), "req2": _sb(24, I32), "rin1": _sb(24, I32), "rin2": _sb(24, I32), "hi": _sb(48, I32), "hp": _sb(24, U16),
     "c2u": _sb(22, U16), "g2": _sb(40, U16), "h1": _sb(22, U16), "h2": _sb(22, U16),
     "pw": _sb(C + 144, F32), "permu": _sb(24, U16), "pd": _sb(96, U16), "pn": _sb(32, U16),
     "u1": _sb(48, U16), "u2": _sb(64, U16), "uw": _sb(UM + SL, F32),
     "gx": _sb(1024, F32), "gt": _sb(1024, F32), "f1": _sb(32, U16), "f2": _sb(32, U16), "b1": _sb(32, U16), "b0": _sb(32, U16),
-    "pl": _sb(512, F32), "w2": _sb(SU0 + NE, F32), "sud": _sb(NS, F32), "suu": _sb(48, U16),
-    "ones": _sb(C, BF), "et": _sb(3 * EW, BF), "zt": _sb(512, BF),
+    "pl": _sb(2 * M, F32), "w2": _sb(SU0 + NE, F32), "sud": _sb(NS, F32), "suu": _sb(48, U16),
+    "ones": _sb(C, BF), "et": _sb(3 * EW + 16, BF), "zt": _sb(512, BF),
     "e1q": _sb(512, Q4), "e1s": _sb(512, U8), "eeq": _sb(512, Q4), "ees": _sb(512, U8), "eoq": _sb(512, Q4), "eos": _sb(512, U8),
     "xt": _sb(4 * C, BF), "ut": _sb(512, BF), "sq": _sb(C, Q4), "ss": _sb(C, U8), "uq": _sb(128, Q4), "us": _sb(128, U8),
     "wq": _sb(512, Q4), "wp": _sb(512, U8), "vq": _sb(512, Q4), "vp": _sb(512, U8),
     "wfq": _sb(FW, Q4), "wfs": _sb(FW, U8), "wbq": _sb(BW, Q4), "wbs": _sb(BW, U8),
     "spq": _sb(C, Q4), "sps": _sb(C, U8), "ds": _sb(1024, BF), "dy": _sb(1024, BF),
     "xs": _sb(7 * 512, BF), "xq": _sb(7 * 128, Q4), "xp": _sb(7 * 128, U8), "ti": _sb(5 * 512, BF), "zp": _sb(1024, BF),
-    "st": _sb(8 * SL + 16 * CAP, BF), "oq": _sb(C, Q4), "opl": _sb(C, U8), "ys": _sb(C, F32), "yo": _sb(C, F32),
+    "st": _sb(8 * SL + 20 * CAP, BF), "oq": _sb(C, Q4), "opl": _sb(C, U8), "ys": _sb(C, F32), "yo": _sb(C, F32),
     "PA": ("psum", [128, 2048], F32), "PB": ("psum", [128, 2048], F32),
 }
 for _k in range(1, 5):
     SCRATCH["pk%d" % _k] = _sb(512, Q4)
     SCRATCH["ps%d" % _k] = _sb(512, U8)
-    for _n, _w in [("sw", M)] * (_k < 3) + [("sd", SL)] * (_k > 1):
+    for _n, _w in [("sw", M)] * (_k < 3) + [("sd", 448)] * (_k > 1):
         SCRATCH["%sq%d" % (_n, _k)] = _sb(_w, Q4)
         SCRATCH["%ss%d" % (_n, _k)] = _sb(_w, U8)
     SCRATCH["hs%d" % _k] = _sb(4 * CAP, U8)
-for _k in (1, 2):
     SCRATCH["hc%d" % _k] = _sb(M, Q4)
-SEMAPHORES = ["q_v", "q_s", "q_t", "q_g", "sent", "ld_l", "ld_s", "ld_e", "ld_x", "ld_w", "ld_v", "ld_u", "st_c", "st_s", "st_y",
-              "ar_pa", "ar_pb", "ar_pc", "ar_pd", "ar_hp", "ar_r1", "ar_r2", "ar_t1", "ar_t2", "ar_g1", "ar_g2"] + \
-    ["ar_%s%d" % (_n, _k) for _k in range(1, 5) for _n in "csh"]
+SEMAPHORES = ["q_v", "q_s", "q_t", "q_g", "sent", "ld_l", "ld_e", "ld_x", "ld_w", "ld_v", "ld_u", "st_c", "st_s", "st_y",
+              "ar_pa", "ar_pb", "ar_pc", "ar_pd", "ar_hp", "ar_r1", "ar_r2", "ar_t1", "ar_t2"] + \
+    ["ar_%s%d" % (_n, _k) for _k in range(1, 5) for _n in "cshg"]
 
 
 def peers_of(T, topo, r):
@@ -151,43 +168,6 @@ def needs(ops):
     return out
 
 
-def placed(ops, pre, turn):
-    start, busy = [0.0] * len(ops), {}
-    for j in turn:
-        t, dur = max([0.0] + [start[i] + x for i, x in pre[j].items()]), ops[j][4]
-        if ops[j][0]:
-            line = busy.setdefault(ops[j][0], [])
-            at = 0
-            for a, z in line:
-                if t + dur <= a + 1e-9:
-                    break
-                t, at = max(t, z), at + 1
-            line.insert(at, (t, t + dur))
-        start[j] = t
-    return start
-
-
-def arrange(ops, pre):
-    n = len(ops)
-    post = [{n: o[5]} for o in ops] + [{}]
-    for j in range(n):
-        for i, t in pre[j].items():
-            post[i][j] = t + ops[j][4] - ops[i][4]
-    way = [o[4] + o[5] for o in ops]
-    for j in range(n - 1, -1, -1):
-        for i, t in pre[j].items():
-            way[i] = max(way[i], t + way[j])
-    turn, best = sorted(range(n), key=lambda j: (-way[j], j)), None
-    for rounds in range(4):
-        start = placed(ops, pre, turn)
-        end = max(start[j] + ops[j][4] + ops[j][5] for j in range(n))
-        if best is None or end < best[0] - 1e-6:
-            best = (end, sorted(range(n), key=lambda j: (start[j], j)))
-        late = placed(ops + [(None, 0, 0, 0, 0.0)], post, [n] + sorted(range(n), key=lambda j: (-start[j] - ops[j][4], -j)))
-        turn = sorted(range(n), key=lambda j: (-late[j] - ops[j][4], j))
-    return best[1]
-
-
 def helper_program(g, core, T, topo, r, h):
     ps = peers_of(T, topo, r)
     off, rest = engine_sets(T, topo, r)
@@ -209,14 +189,16 @@ def helper_program(g, core, T, topo, r, h):
         call([(d, off, "ar_pd", T.hp[:], T.pin[:, at:at + 24])])
     for k in range(1, 5):
         g.wait_ge(T.sem["ar_h%d" % k], len(rest) // (1 if h == 2 else 2))
-        call([plane(k, 2 * h + j, es) for j, es in enumerate(parts(off, 2))] + ([plane(k, NP - 1, rest)] if h == 2 else []))
-        if k < 3 and h < 2:
+        call([plane(k, 2 * h + j, es) for j, es in enumerate(parts(off, 2))] + ([plane(k, NP - 1, rest)] if h == 2 and k == 1 else []))
+        if h < 2 or k == 1:
             s = [s for s in ps[:NP - 1] if far_helper(T, topo, s, h) == core][0]
-            g.wait_ge(T.sem["ar_g%d" % k], len(off) // 2)
+            g.wait_ge(T.sem["ar_g%d" % k], len(off) // (1 if h == 2 else 2))
             items = []
+            w, base = lot(k, 0)[2:]
             for d, es in zip((r, ps[-1]), parts(off + rest, 2)):
-                at = lot(k, 0)[3] + M * peers_of(T, topo, d).index(s)
-                items.append((d, es, "ar_c%d" % k, T["hc%d" % k][:].bitcast(dt.uint8), T.wfq[:, at:at + M].bitcast(dt.uint8)))
+                a, at = 0 if w == M else w * (peers_of(T, topo, s).index(d) % 2), base + w * peers_of(T, topo, d).index(s)
+                items.append((d, es, "ar_c%d" % k, T["hc%d" % k][:, a:a + w].bitcast(dt.uint8),
+                              T[LAND[k][0] + "q"][:, at:at + w].bitcast(dt.uint8)))
             call(items)
     g.wait_ge(T.sem.sent, sent[0])
 
@@ -299,8 +281,11 @@ def rank_program(g, core, T, topo):
             return run("v", [i, off], [o], lambda: g.vector.tensor_copy(ap(o), src(i, off)), GATHER * size(o), 0.055)
         return run("v", [i], [o], lambda: g.vector.tensor_copy(ap(o), ap(i)), cycles(o, i))
 
-    def scat(o, off, i):
-        run("v", [i, off], [o], lambda: g.vector.tensor_copy(ap(o).indirect(ap(off)), ap(i)), SCATTER * size(i), 0.055)
+    def scat(o, off, i, step):
+        for a in range(0, size(off), step):
+            z = min(a + step, size(off))
+            x, y = (off[0], off[1] + a, off[1] + z, 1), (i[0], i[1] + 16 * a, i[1] + 16 * z, 1)
+            run("v", [y, x], [o], lambda x=x, y=y: g.vector.tensor_copy(ap(o).indirect(ap(x)), ap(y)), SCATTER * size(y), 0.055)
 
     def tt(o, a, b, op):
         run("v", [a, b], [o], lambda: g.vector.tensor_tensor(ap(o), ap(a), ap(b), op), size(o) * (1 if a[0][0] == "P" else 2))
@@ -314,7 +299,7 @@ def rank_program(g, core, T, topo):
 
     def scan(o, reset, d, op1=Op.add, op0=Op.mult, first=0.0):
         r1, x1 = col(first)
-        return run("v", [reset, d] + r1, [o], lambda: g.vector.tensor_tensor_scan(ap(o), ap(reset), ap(d), x1, op0, op1), size(o))
+        run("v", [reset, d] + r1, [o], lambda: g.vector.tensor_tensor_scan(ap(o), ap(reset), ap(d), x1, op0, op1), size(o))
 
     def summed(o, i):
         run("v", [i], [o], lambda: g.vector.tensor_reduce(ap(o), ap(i), AxisListType.X, Op.add), size(i))
@@ -353,17 +338,17 @@ def rank_program(g, core, T, topo):
             GATHER * n, 0.055)
         act(A(so, a, a + n), A(si, 0, wlen), off=off)
 
-    def dmas(sem, items, lag, after=(), now=False):
+    def dmas(sem, items, lag, behind=(), now=False):
         def issue():
             for q, o, i, rd, wr in items:
-                before(q, rd, wr)
+                before(q, rd + list(behind), wr)
                 Q[q].dma_start(o, i).then_inc(T.sem[sem], 16)
             for q, o, i, rd, wr in items:
                 note(q, rd, wr, sem, 16 * len(items))
         if now:
             issue()
-        put(None if now else items[0][0], sum([p[3] for p in items], []), sum([p[4] for p in items], []),
-            (lambda: None) if now else issue, 0.0 if now else 0.05 * len(items), lag, after)
+        put(None if now else items[0][0], sum([p[3] for p in items], list(behind)), sum([p[4] for p in items], []),
+            (lambda: None) if now else issue, 0.0 if now else 0.05 * len(items), lag)
 
     def u8(v):
         return ap(v).bitcast(dt.uint8)
@@ -392,7 +377,9 @@ def rank_program(g, core, T, topo):
             return A(n % kind, a, a + w), A(name + kind, base + w * back(i), base + w * back(i) + w)
 
         def far(h, es):
-            return far_helper(T, topo, r, h), es, "ar_g%d" % k, u8(ends(2 * h, "q")[0]), u8(A("hc%d" % k))
+            n, a, w, base = lot(k, 2 * h)
+            w = w if w == M else 2 * w
+            return far_helper(T, topo, r, h), es, "ar_g%d" % k, u8(A(n % "q", a, a + w)), u8(A("hc%d" % k, 0, w))
 
         def plane(h):
             a, w = wide(k, h)
@@ -403,21 +390,23 @@ def rank_program(g, core, T, topo):
 
         def codes(i, es):
             return (T.cores[ps[i]], es, "ar_c%d" % k) + tuple(u8(v) for v in ends(i, "q"))
-        rd = [ends(i, "q")[0] for i in {None: range(NP), 0: range(4), 1: range(4, NP)}[piece]] + \
-            [plane(h) for h in {None: range(3), 0: range(2), 1: [2]}[piece]]
+        rd = [ends(i, "q")[0] for i in {None: range(NP), 0: range(4), 1: (4, 5), 2: [6]}[piece]] + \
+            [plane(h) for h in {None: range(3), 0: range(2), 1: [2], 2: []}[piece]]
         o2, r2, n, m = parts(off_chip, 2), parts(rest, 2), len(off_chip), len(rest)
-        if k < 3 and piece != 1:
+        if piece in (None, 0):
             call([relay(0, r2[0]), relay(1, r2[1])] + ([relay(2, off_chip)] if k == 1 else []), rd)
             call([far(0, o2[0]), far(1, o2[1])] + ([codes(6, rest)] if k == 1 else []), rd)
-        elif piece == 0:
-            call([codes(i, es) for i, es in enumerate(parts(off_chip, 4))] + [relay(0, r2[0]), relay(1, r2[1])], rd)
         if piece == 0:
             return
-        call([codes(4, o2[0]), codes(5, o2[1])] + ([relay(2, rest)] if k > 1 else []), rd)
-        ways = ((0.0,) if k > 1 else ()) + WAY[k]
+        if piece != 2:
+            call([codes(4, o2[0]), codes(5, o2[1]), relay(2, rest)] if k > 1 else [far(2, off_chip)], rd)
+        if piece == 1:
+            return
+        ways = ((1.6, 0.0) if k > 1 else ()) + WAY[k]
         if k > 1:
             call([codes(6, rest)], rd)
-        lands([A(name + "q", a0, z0)], "ar_c%d" % k, (2 * (n + m) if k < 3 else n) + n + m, *ways)
+            call([(T.cores[ps[6]], rest, "ar_s%d" % k) + tuple(ap(v) for v in ends(6, "s"))], [ends(6, "s")[0]])
+        lands([A(name + "q", a0, z0)], "ar_c%d" % k, 2 * (n + m) + (n if k > 1 else n + m) + m, *ways)
         lands([A(name + "s", a0, z0)], "ar_s%d" % k, 3 * n + m, *ways)
 
     def bank(p, b, n):
@@ -433,7 +422,9 @@ def rank_program(g, core, T, topo):
     EXTRA = A("pf", 3, 4)
 
     def to_table(w, n, a):
-        scan(A("m2", a, a + n), A("keep", 0, n), w, Op.max, Op.add)
+        step = M if n % M == 0 else n // 3 if n > 2 * M else n
+        for b in range(0, n, step):
+            scan(A("m2", a + b, a + b + step), A("keep", 0, step), (w[0], w[1] + b, w[1] + b + step, 1), Op.max, Op.add)
         return A("m2", a + 15, a + n, 16)
 
     def pair_lists(out, at):
@@ -479,10 +470,10 @@ def rank_program(g, core, T, topo):
 
     def send(k, win, lists):
         at = 4 * SL * (k - 3)
-        for piece, (a, z) in enumerate(((0, 12), (12, 21))):
+        for piece, (a, z, to, n) in enumerate(((0, 12, 0, 192), (12, 18, 192, M), (18, 21, 320, M))):
             for b in range(4):
                 plain("vs"[b % 2], A("st", at + 64 * a + b, at + 64 * z, 4), win(b), A(lists, a, z))
-            quant("sdq%d" % k, "sds%d" % k, 16 * a, 16 * (z - a), A("st", at + 64 * a, at + 64 * z))
+            quant("sdq%d" % k, "sds%d" % k, to, n, A("st", at + 64 * z - 4 * n, at + 64 * z))
             exchange(k, piece)
 
     def decode(qn, sn, a, n, out, engines="ssss"):
@@ -491,9 +482,9 @@ def rank_program(g, core, T, topo):
             plain(engines[b], out(b), bank("PA", b, n))
 
     def line(i, x, even, odd):
-        o = A("et", EW * i, EW * i + 512)
+        o = A("et", EW * i, EW * i + EW)
         run("g", [A("zt")], [o], lambda: g.affine_select(ap(o), ap(A("zt")), [[-128, 4], [odd - even - 64, 2], [-1, 64]], Op.not_equal,
-                                                         x, 3 + even, 4), 1024, 0.18, [(c, CALL) for c in calls[-1:]])
+                                                         x, 3 + even, 4), 2 * EW, 0.18, [(c, CALL) for c in calls[-1:]])
 
     def constants(qn, i):
         for b in range(4):
@@ -508,9 +499,10 @@ def rank_program(g, core, T, topo):
     def tables(l):
         a, b, j = "req%d" % l, "rin%d" % l, 2 - l
         val = A("val", 256 * j, 256 * j + 256)
-        scan(val, A("pl", 256 * j, 256 * j + 256), A("es", 256 * j, 256 * j + 256), Op.add, Op.max)
+        for x in (256 * j, 256 * j + M):
+            scan(A("val", x, x + M), A("pl", M * j, M * j + M), A("es", x, x + M), Op.add, Op.max)
         cp(A("ou", 16 * j, 16 * j + 16), A("pm", 8 * SEG * j + 7, 8 * SEG * j + 128, 8))
-        scat(A("w2"), A("ou", 16 * j, 16 * j + 16), val)
+        scat(A("w2"), A("ou", 16 * j, 16 * j + 16), val, 8 * l)
         ts(A(a, 0, 21), to_table(A("w2", NE + SL * j, NE + SL * j + SL), SL, 896 + SL * j), EXTRA, Op.subtract)
         soon = list(enumerate(parts(off_chip, 2))) + [(NP - 1, rest)]
         late = [(2 + i, es) for i, es in enumerate(parts(off_chip, 4))]
@@ -526,28 +518,27 @@ def rank_program(g, core, T, topo):
     def successors(l):
         x, j = A("x%d" % l, 0, 21), 24 * (2 - l)
         ts(x, A("lo", j, j + 21), float(SL - 1 - RK * (r + 1)), Op.add)
-        tt(x, x, A("nt", 0, 21), Op.max)
+        tt(x, x, A("pu", 0, 21), Op.max)
         cp(A("suu", j, j + 21), x)
-        scat(A("w2", NE + NS), A("suu", j, j + 21), A("sud", SL * (2 - l), SL * (3 - l)))
+        scat(A("w2", NE + NS), A("suu", j, j + 21), A("sud", SL * (2 - l), SL * (3 - l)), 8)
 
     def coded(place):
         return LOW * (place - M) + SH + RK * (r + 1) + C
 
     dmas("ld_l", [("ys"[i % 2], T.lvt[16 * i:16 * i + 16, :], T.lv[:], [], [A("lvt")]) for i in range(8)], 1.75, now=True)
     dmas("ld_e", [("y", T.e[:, 0:24], T.pr0[:], [], [A("e", 0, 24)]), ("y", T.e[:, 24:48], T.pr1[:], [], [A("e", 24, 48)])], 2.4, now=True)
-    dmas("ld_x", [("y", T.xt[:], T.x[:], [], [A("xt")])], 3.8, now=True)
-    dmas("ld_w", [("y", u8(A("wq")), T.wc[:], [], [A("wq")]), ("y", T.wp[:], T.ws[:], [], [A("wp")])], 5.0, now=True)
+    dmas("ld_x", [("y", T.xt[:], T.x[:], [], [A("xt")])], 4.7, now=True)
+    dmas("ld_w", [("y", u8(A("wq")), T.wc[:], [], [A("wq")]), ("y", T.wp[:], T.ws[:], [], [A("wp")])], 6.0, now=True)
 
     fill(A("zt"), 0.0)
     fill(A("ones"), 1.0)
     iota(A("pc", 0, 1), [[0, 1]], 0, 1)
-    for i in range(3):
-        fill(A("et", EW * i + 512, EW * i + EW), 0.0)
-    line(0, 1.0, 0, 0)
-    iota(A("nm"), [[0, SL // 16], [1, 16]], 0)
+    fill(A("et", 3 * EW), 0.0)
+    line(2, 1.0, 0, 0)
+    iota(A("nm"), [[0, 9], [1, 16]], 0)
     scan(A("iot"), A("ones"), A("ones"), first=-1.0)
-    act(A("w2", SU0, SU0 + C), A("ones"), scale=float(coded(BZ)))
-    dmas("ld_s", [("y", ap(A("w2", SU0 + C)), ap(A("w2", SU0, SU0 + C)), [A("w2", SU0, SU0 + C)], [A("w2", SU0 + C)])], 4.5)
+    for k in range(2):
+        act(A("w2", SU0 + C * k, SU0 + C * k + C), A("ones"), scale=float(coded(BZ)))
     for name, n, step in (("lrs", 152, 0), ("rt", 32, 16), ("rs", 2 * NP * SEG, SEG), ("rp", 264, 8)):
         fill(A(name), 1.0)
         if step:
@@ -555,7 +546,7 @@ def rank_program(g, core, T, topo):
     runs, threes = A("lrs", 0, 3 * LSEG), A("lrs", 80, 152)
     fill(A("lrs", 0, 3 * LSEG, LSEG), 0.0)
     fill(A("lrs", 80, 152, 3), 0.0)
-    for v in (A("tot"), A("kc"), A("loh", 0, None, LSEG), A("oh", 0, 2 * NP * SEG, SEG), A("vi", 16, 17), A("vn", 16, 17)):
+    for v in (A("tot", 0, 72), A("loh", 0, None, LSEG), A("oh", 0, 2 * NP * SEG, SEG), A("vi", 16, 57, 40)):
         fill(v, 0.0)
     fill(A("si", 16, 17), 0)
     fill(A("ew", 0, 1), float(RK * (N + 1) + SH))
@@ -563,16 +554,14 @@ def rank_program(g, core, T, topo):
     ts(A("pc", 1, 2), A("pc", 0, 1), 15, Op.bitwise_and)
     cp(OWN, A("pc", 1, 2))
     ts(A("pf", 1, 2), A("pc", 1, 2), -1.0, Op.mult, -0.5, Op.add)
-    for b in range(4):
-        ts(A("pf", 3 + b, 4 + b), A("pc", 1, 2), float(-BIG), Op.mult, float(15 * BIG + SH - b), Op.add)
+    ts(EXTRA, A("pc", 1, 2), float(-BIG), Op.mult, float(15 * BIG + SH), Op.add)
+    ts(A("pf", 4, 7), A("iot", 1, 4), -1.0, Op.mult, EXTRA, Op.add)
     ts(A("pf", 7, 8), A("pc", 1, 2), float(-BIG), Op.mult, float(15 * BIG + SH + C), Op.add)
     ts(A("kc", 14, 17), A("iot", 0, 3), float(M), Op.mult, -1.0, Op.add)
     for h in range(2):
         ts(A("kc", h, 2 * NP, 2), A("iot", 0, NP), float(CAP), Op.mult, float(NE - 1 + SL * h), Op.add)
     trn(A("s2"), A("kc"))
-    ts(A("nt"), A("iot", 0, 24), 16.0, Op.mult, OWN, Op.add)
-    ts(A("pu", 0, SEG), A("iot", 0, SEG), 16.0, Op.mult, OWN, Op.add)
-    ts(A("pu", SEG, 33), A("iot", 0, 16), 16.0, Op.mult, OWN, Op.add)
+    ts(A("pu"), A("iot", 0, 33), 16.0, Op.mult, OWN, Op.add)
     for s in range(N):
         if s < N - 2:
             act(A("ew", 1 + C * s, 1 + C * s + C), A("iot"), Act.Identity, bias=float(RK * (s + 1) + SH))
@@ -580,7 +569,7 @@ def rank_program(g, core, T, topo):
             iota(A("ew", 1 + C * s, 1 + C * s + C), [[1, C]], RK * (s + 1) + SH)
     act(A("ma"), A("nm"), Act.Sign, bias=A("pf", 1, 2))
     act(A("keep"), A("ma"), Act.Identity, bias=-15.5 * BIG, scale=16.5 * BIG)
-    constants("e1", 0)
+    constants("e1", 2)
 
     for l in range(3):
         ts(A("loh", LSEG * l + 1, LSEG * l + LSEG), A("lvt"), float(l), Op.is_equal)
@@ -609,12 +598,12 @@ def rank_program(g, core, T, topo):
     for i in turn:
         lands([A("pin", 24 * i, 24 * i + 24)], PSEM[i], len(off_chip) * (2 if PSEM[i] == "ar_pd" else 1), WAY[PSEM[i]])
     iota(A("io2"), [[FL1, 3], [1, M]], 0)
-    iota(A("pl", 0, 256), [[0, 2], [LOW, M]], LOW * M)
-    scat(A("pw", 0, C), A("posu"), A("ew", 1, 1 + C))
+    scat(A("pw", 0, C), A("posu"), A("ew", 1, 1 + C), 24)
     ts(A("permu", 0, 8), to_table(A("pw", 0, M), M, 0), EXTRA, Op.subtract, float(-RK), Op.add)
     ts(A("permu", 8, 24), to_table(A("pw", M, C), C - M, M), EXTRA, Op.subtract, float(-RK), Op.add)
 
-    quant("sq", "ss", 0, C, A("xt"))
+    for a in range(0, C, M):
+        quant("sq", "ss", a, M, A("xt", 4 * a, 4 * a + 4 * M))
     pick("spq", "sps", 0, "sq", "ss", C, A("permu", 0, 8))
     decode("spq", "sps", 0, M, tile("xs", 6), "vsvs")
     quant("xq", "xp", 128 * 6, M, A("xs", 512 * 6, 512 * 7))
@@ -622,11 +611,12 @@ def rank_program(g, core, T, topo):
     quant("swq1", "sws1", 0, M, A("ti", 0, 512))
     exchange(1)
     quant("wfq", "wfs", FY, M, A("ti", 0, 512))
+    iota(A("pl", 0, M), [[LOW, M]], LOW * M)
     iota(A("w2", NE, NE + SL), [[0, SL]], SH)
     line(1, -0.5, 0, 1024)
-    line(2, -0.5, 1024, 0)
+    line(0, -0.5, 1024, 0)
     constants("ee", 1)
-    constants("eo", 2)
+    constants("eo", 0)
     quant("wfq", "wfs", FZ, M, A("zt"))
 
     ts(A("u1"), A("e"), 1.0, Op.add)
@@ -655,7 +645,7 @@ def rank_program(g, core, T, topo):
     W = 2 * SEG
     for i in range(NP):
         ts(A("oh", W * i + 1, W * i + W), A("si"), float(ps[i] + 1), Op.is_equal)
-    counted = scan(A("ct", 0, NP * W), A("rs"), A("oh", 0, NP * W))
+    scan(A("ct", 0, NP * W), A("rs"), A("oh", 0, NP * W))
     trn(A("t2"), A("ct", SEG - 1, 32 * SEG, SEG))
     for h in (0, 16):
         scan(A("s2", h + 1, h + 16), A("ones", 0, 15), A("t2", h, h + 15), first=A("s2", h, h + 1))
@@ -668,8 +658,8 @@ def rank_program(g, core, T, topo):
     tt(A("prod", 7, None, 8), A("vi"), A("pu"), Op.max)
     scan(A("pm"), A("rp"), A("prod"), Op.max)
     tables(2)
-    dmas("ld_v", [("y", u8(A("vq")), T.vc[:], [], [A("vq")]), ("y", T.vp[:], T.vs[:], [], [A("vp")])], 4.0, [(counted, 0.0)])
-    dmas("ld_u", [("y", T.ut[:], T.u[:], [], [A("ut")])], 4.0, [(counted, 0.0)])
+    iota(A("w2", NE + SL, NE + NS), [[0, SL]], SH)
+    dmas("ld_v", [("y", u8(A("vq")), T.vc[:], [], [A("vq")]), ("y", T.vp[:], T.vs[:], [], [A("vp")])], 4.0, [A("f1")])
 
     pick("spq", "sps", M, "sq", "ss", C, A("permu", 8, 16))
     decode("spq", "sps", M, M, flat("ds", 0, 256))
@@ -683,14 +673,16 @@ def rank_program(g, core, T, topo):
     ts(A("c2u", 12, 21), A("lo", 12, 21), float(-1 - RK * (r + 1)), Op.add, 0.0, Op.max)
     act(A("pw", C), A("pp"), off=A("c2u", 12, 21))
     t = to_table(A("pw", C), 144, 1568)
-    act(A("st", 8 * SL + 576), A("zt", 0, 192))
+    act(A("st", 8 * SL, 8 * SL + 384), A("zt", 0, 384))
     for b in range(4):
         ts(A("g2", 10 * b, 10 * b + 9), t, A("pf", 3 + b, 4 + b), Op.subtract, float(8 * M - 4 + b), Op.min)
-        plain("vs"[b % 2], A("st", 8 * SL + b, 8 * SL + 576, 4), A("ti", 0, 1024), A("g2", 10 * b, 10 * b + 9))
-    quant("sdq2", "sds2", 0, 4 * CAP, A("st", 8 * SL))
-    exchange(2, 1)
+    for piece, a, z, to, n in ((1, 0, 6, M, 192), (2, 6, 9, 320, M)):
+        at = 8 * SL + 384
+        for b in range(4):
+            plain("vs"[b % 2], A("st", at + 64 * a + b, at + 64 * z, 4), A("ti", 0, 1024), A("g2", 10 * b + a, 10 * b + z))
+        quant("sdq2", "sds2", to, n, A("st", at + 64 * z - 4 * n, at + 64 * z))
+        exchange(2, piece)
     quant("wfq", "wfs", FY + M, M, A("ti", 512, 1024))
-    iota(A("w2", NE + SL, NE + NS), [[0, SL]], SH)
     iota(A("sud", SL, NS), [[LOW, SL]], coded(BL4))
 
     act(A("uw", UM), A("iot", 0, SL), Act.Identity, bias=float(FL2))
@@ -706,8 +698,9 @@ def rank_program(g, core, T, topo):
     for k in range(2):
         for h in range(2):
             ts(A("pd", 48 * k + h, 48 * k + 48, 2), A("permu"), float(C * k), Op.add)
-        act(A("pl", 256 + M * k, 256 + M * k + M), A("iot", 0, M), scale=float(LOW))
+    act(A("pl", M), A("iot", 0, M), scale=float(LOW))
     act(A("sud", 0, SL), A("iot", 0, SL), Act.Identity, bias=float(coded(BL3)), scale=float(LOW))
+    tables(1)
     asked(2, 0, 12)
     successors(2)
     backward_lists("b1", 0, 1)
@@ -726,11 +719,11 @@ def rank_program(g, core, T, topo):
     decode("wfq", "wfs", FY, 256, lambda b: A("dy", 256 * b, 256 * b + 256))
     quant("wbq", "wbs", BZ, M, A("zt"))
     quant("wbq", "wbs", 2 * M, M, A("ti", 1024, 1536))
-    tables(1)
 
     gathered(3, "wb", BL4, "b1", "dy", M, 256, 4)
     layer("vq", "vp", 4, flat("zp", 512, M))
     send(4, flat("zp", 512, M), "h1")
+    dmas("ld_u", [("y", T.ut[:], T.u[:], [], [A("ut")])], 3.0, [A("pk3", 0, M)])
     asked(1, 0, 21)
     successors(1)
     backward_lists("b0", 512, 0)
@@ -748,14 +741,12 @@ def rank_program(g, core, T, topo):
     pick("oq", "opl", 0, "wbq", "wbs", C, A("posu"))
     act(A("ys", 0, M), bank("PA", 0, M))
     dmas("st_c", [("y", T.oc[:], u8(A("oq")), [A("oq")], [])], 2.4)
-    dmas("st_s", [("y", T.osc[4 * k:4 * k + 4, :], T.opl[32 * k:32 * k + 4, :], [A("opl")], []) for k in range(4)], 2.2)
+    dmas("st_s", [("sy"[k % 2], T.osc[4 * k:4 * k + 4, :], T.opl[32 * k:32 * k + 4, :], [A("opl")], []) for k in range(4)], 1.5)
     for h in range(2):
         plain("vs"[h], A("yo", 192 * h, 192 * h + 192), A("ys"), A("posu", 12 * h, 12 * h + 12))
     dmas("st_y", [("y", T.y[:], T.yo[:], [A("yo")], [])], 2.4)
 
     pre = needs(ops)
-    if not ORDER:
-        ORDER.extend(arrange(ops, pre))
     at = {j: i for i, j in enumerate(ORDER)}
     assert len(at) == len(ops) and all(at[i] < at[j] for j in range(len(ops)) for i in pre[j])
     for j in ORDER:

from concourse.bass import DstId, RemoteDMATransfer
from concourse.mybir import dt, AluOpType as Op, ActivationFunctionType as Act, AxisListType

N, C, M, CAP, NP = 8, 384, 128, 48, 7
SL = CAP * NP
F32, BF, I32, U16, Q4, U8 = "float32", "bfloat16", "int32", "uint16", "float8_e4m3fn_x4", "uint8"
FY, FZ, FL2, FL1 = NP * M, NP * M + 2 * M, NP * M + 3 * M, NP * M + 3 * M + SL
FW = FL1 + NP * M
WHOLE = 4
BZ, BL3, BL4, BW = 384, 512, 512 + SL, 512 + 2 * SL
NE, NS = 2 * C, 2 * SL
SEG, LSEG = 17, 25
UM = 2 + N * C
EW = 512
RK = 800
LOW = 8192
BIG = 256 * LOW
SH = 128 - 8 * BIG
SU0 = NE + NS + SL
IOT = 240
LAND = {1: ("wf", 0, FY), 2: ("wf", FL2, FW), 3: ("wb", BL3, BL4), 4: ("wb", BL4, BW)}
CYC, WAKE, CALL, FIRST, GATHER, SCATTER = 0.00091, 0.23, 0.2, 1.6, 1.8, 4.5
WAY = {"ar_pa": 2.0, "ar_pb": 2.6, "ar_pc": 2.0, "ar_pd": 4.6, "ar_r": 1.8, "ar_t": 5.0,
       1: (3.8, 4.4), 2: (3.2, 4.2), 3: (3.2, 3.8), 4: (3.2, 3.8)}
ORDER = [int(_n) for _n in """
5 22 27 6 46 9 0 16 10 24 29 14 1 13 4 2 3 11 12 40 44 15 23 8 32 37 20 34 7 26 31 42 41 54 56 58 35 55 57 59 63 64 47 48 28 45 60 21 43
65 61 66 50 49 62 17 304 36 130 132 67 69 68 52 70 25 30 33 133 71 51 82 39 131 157 89 134 83 90 88 84 72 260 53 92 259 86 73 81 91 135
136 85 93 18 137 95 87 96 97 99 100 138 147 145 94 146 98 139 129 101 301 74 75 143 76 148 140 300 102 149 103 104 106 150 108 77 107 141
78 105 109 151 158 38 110 174 172 176 111 177 171 173 175 154 153 142 152 178 112 113 117 191 116 179 160 162 159 192 119 144 155 79 180
181 161 80 164 193 195 182 156 196 183 166 165 19 185 190 184 186 187 188 118 189 121 290 194 288 122 120 197 289 302 291 163 198 211 199
201 200 212 123 202 124 292 126 167 168 114 115 127 293 169 265 203 125 170 213 214 221 223 215 216 205 217 219 218 220 209 225 222 224
295 128 294 210 227 228 226 229 230 204 261 231 232 287 233 234 235 306 334 236 262 238 239 237 241 242 244 263 245 240 243 246 296 264
247 207 267 248 266 250 252 254 303 268 249 253 333 251 255 256 269 271 335 273 337 339 272 257 270 341 276 208 277 258 206 278 279 321
336 338 340 308 274 307 342 305 275 280 281 285 322 297 282 286 309 299 323 430 310 324 312 311 313 325 314 315 298 317 283 284 344 346
319 343 345 347 349 348 350 351 352 326 353 354 355 356 357 358 359 360 316 361 362 363 364 365 366 367 368 369 327 370 372 374 376 371
373 320 375 377 328 378 379 381 383 385 380 382 384 386 318 387 490 388 329 491 390 392 394 389 422 492 391 393 395 396 424 398 397 403
399 400 405 411 426 428 404 406 407 410 412 401 418 402 419 420 409 413 421 330 493 423 408 414 425 431 415 427 331 332 429 494 495 496
416 417 433 435 432 434 489 438 436 437 439 497 440 441 442 443 498 444 445 446 447 449 450 452 448 453 455 451 456 454 457 458 499 459
461 463 465 460 462 464 466 468 467 469 470 474 475 471 477 476 481 483 482 472 502 500 473 503 478 504 480 484 505 507 479 501 485 506
486 508 509 487 488 511 513 510 512 516 514 515 517 518 519 520 521 522 523 524 525 527 528 530 526 531 533 529 534 532 535 536 537 539
541 543 538 540 542 544 545 547 546 549 553 552 550 548 554 551""".split()]


def lot(k, i):
    if k == 1 or k == 2 and i < WHOLE:
        return "sw%%s%d" % k, 0, M, FL1 * (k - 1)
    return "sd%%s%d" % k, CAP * i + (0, 0, 32, 112)[i // 2], CAP, LAND[k][1]


def wide(k, h):
    if lot(k, 2 * h)[2] == M:
        return 0, M
    if h < 2:
        return 2 * CAP * h, 2 * CAP
    return M, 4 * CAP


def _sb(n, d):
    return ("sbuf", [128, n], d)


SMALL = {}
for _n in ("tot", "kc", "tt", "ts", "tb", "rt", "kt", "t2", "s2", "a1", "a2", "a3", "a4", "x1", "x2",
           "vi", "vn", "pv", "n1", "on", "pu"):
    SMALL[_n] = (40 * len(SMALL), 32 if len(SMALL) < 9 else 24 if len(SMALL) < 15 else 33)

SCRATCH = {
    "sm": _sb(40 * len(SMALL), F32), "e": _sb(48, I32), "lvt": _sb(24, I32), "ct": _sb(IOT + C, F32), "io2": _sb(C, F32),
    "ew": _sb(UM - 1, F32), "eexp": _sb(NE, F32), "es": _sb(512, F32), "si": _sb(33, I32), "val": _sb(512, F32), "lo": _sb(48, I32),
    "oh": _sb(32 * SEG, F32), "rs": _sb(2 * NP * SEG, BF), "c2": _sb(2 * NP * SEG, F32),
    "prod": _sb(264, F32), "rp": _sb(264, BF), "pm": _sb(264, F32),
    "loh": _sb(3 * LSEG, F32), "lrs": _sb(152, BF), "lc1": _sb(3 * LSEG, F32), "lc2": _sb(3 * LSEG, F32), "lc3": _sb(144, F32),
    "ou": _sb(32, U16), "pp": _sb(NE, F32), "posu": _sb(24, U16), "pin": _sb(24 * NP, U16), "pc": _sb(4, I32), "pf": _sb(8, F32),
    "nm": _sb(144, BF), "ma": _sb(144, BF), "keep": _sb(144, BF), "m2": _sb(1712, F32),
    "req1": _sb(24, I32), "req2": _sb(24, I32), "rin1": _sb(24, I32), "rin2": _sb(24, I32), "hi": _sb(48, I32), "hp": _sb(24, U16),
    "c2u": _sb(22, U16), "g2": _sb(40, U16), "h1": _sb(22, U16), "h2": _sb(22, U16),
    "pw": _sb(C + 144, F32), "permu": _sb(24, U16), "pd": _sb(96, U16), "pn": _sb(32, U16),
    "u1": _sb(48, U16), "u2": _sb(64, U16), "uw": _sb(UM + SL, F32),
    "gx": _sb(1024, F32), "gt": _sb(1024, F32), "f1": _sb(32, U16), "f2": _sb(32, U16), "b1": _sb(32, U16), "b0": _sb(32, U16),
    "pl": _sb(2 * M, F32), "w2": _sb(SU0 + NE, F32), "sud": _sb(NS, F32), "suu": _sb(48, U16),
    "ones": _sb(C, BF), "et": _sb(3 * EW + 16, BF), "zt": _sb(512, BF),
    "e1q": _sb(512, Q4), "e1s": _sb(512, U8), "eeq": _sb(512, Q4), "ees": _sb(512, U8), "eoq": _sb(512, Q4), "eos": _sb(512, U8),
    "xt": _sb(4 * C, BF), "ut": _sb(512, BF), "sq": _sb(C, Q4), "ss": _sb(C, U8), "uq": _sb(128, Q4), "us": _sb(128, U8),
    "wq": _sb(512, Q4), "wp": _sb(512, U8), "vq": _sb(512, Q4), "vp": _sb(512, U8),
    "wfq": _sb(FW, Q4), "wfs": _sb(FW, U8), "wbq": _sb(BW, Q4), "wbs": _sb(BW, U8),
    "spq": _sb(C, Q4), "sps": _sb(C, U8), "ds": _sb(1024, BF), "dy": _sb(1024, BF),
    "xs": _sb(7 * 512, BF), "xq": _sb(7 * 128, Q4), "xp": _sb(7 * 128, U8), "ti": _sb(5 * 512, BF), "zp": _sb(1024, BF),
    "st": _sb(8 * SL + 20 * CAP, BF), "oq": _sb(C, Q4), "opl": _sb(C, U8), "ys": _sb(C, F32), "yo": _sb(C, F32),
    "PA": ("psum", [128, 2048], F32), "PB": ("psum", [128, 2048], F32),
}
for _k in range(1, 5):
    SCRATCH["pk%d" % _k] = _sb(512, Q4)
    SCRATCH["ps%d" % _k] = _sb(512, U8)
    for _n, _w in [("sw", M)] * (_k < 3) + [("sd", 448)] * (_k > 1):
        SCRATCH["%sq%d" % (_n, _k)] = _sb(_w, Q4)
        SCRATCH["%ss%d" % (_n, _k)] = _sb(_w, U8)
    SCRATCH["hs%d" % _k] = _sb(4 * CAP, U8)
    SCRATCH["hc%d" % _k] = _sb(M, Q4)
SEMAPHORES = ["q_v", "q_s", "q_t", "q_g", "sent", "ld_l", "ld_e", "ld_x", "ld_w", "ld_v", "ld_u", "st_c", "st_s", "st_y",
              "ar_pa", "ar_pb", "ar_pc", "ar_pd", "ar_hp", "ar_r1", "ar_r2", "ar_t1", "ar_t2"] + \
    ["ar_%s%d" % (_n, _k) for _k in range(1, 5) for _n in "cshg"]


def peers_of(T, topo, r):
    n = len(T.cores)
    mine = topo.chip(T.cores[r])
    far = [(r + i) % n for i in range(1, n) if topo.chip(T.cores[(r + i) % n]) != mine]
    chips = []
    for s in far:
        if topo.chip(T.cores[s]) not in chips:
            chips.append(topo.chip(T.cores[s]))
    out = [s for ch in chips for s in sorted(far) if topo.chip(T.cores[s]) == ch]
    return out + [s for s in range(n) if s != r and topo.chip(T.cores[s]) == mine]


def helpers_of(T, topo, r):
    core = T.cores[r]
    return [c for c in topo.cores_of(core) if topo.die(c) == topo.die(core) and T.rank_of(c) is None][:3]


def bits(es):
    return sum(1 << e for e in es)


def parts(es, n):
    k = len(es) // n
    return [es[k * i:k * i + k] for i in range(n)]


def engine_sets(T, topo, r):
    ps = peers_of(T, topo, r)
    core = T.cores[r]
    off = topo.engines(core, T.cores[ps[0]])
    return off, [e for e in topo.engines(core, T.cores[ps[-1]]) if e not in off]


def far_helper(T, topo, s, h):
    d = [d for d in peers_of(T, topo, s)[2 * h:2 * h + 2] if topo.die(T.cores[d]) == topo.die(T.cores[s])][0]
    return helpers_of(T, topo, d)[h]


def dst(topo, c):
    a = topo.addr(c)
    return DstId(rid=a[0], pnc=a[1])


def meet(u, v):
    if u[0][0] == "P":
        return u[1] // 512 <= (v[2] - 1) // 512 and v[1] // 512 <= (u[2] - 1) // 512
    if u[1] >= v[2] or v[1] >= u[2]:
        return False
    return not (u[3] == v[3] and u[3] > 1 and (u[1] - v[1]) % u[3])


def needs(ops):
    out, log = [], {}
    for j, (q, rd, wr, f, dur, lag, after) in enumerate(ops):
        p = dict(after)
        views = [(v, False) for v in rd] + [(v, True) for v in wr]
        for v, w in views:
            for u, uw, i in log.get(v[0], []):
                psum = v[0][0] == "P"
                if (uw or w or psum) and meet(u, v):
                    p[i] = max(p.get(i, 0), ops[i][4] + ops[i][5] + (0 if psum and ops[i][0] == q else WAKE))
        for v, w in views:
            log.setdefault(v[0], []).append((v, w, j))
        out.append(p)
    return out


def helper_program(g, core, T, topo, r, h):
    ps = peers_of(T, topo, r)
    off, rest = engine_sets(T, topo, r)
    sent = [0]

    def call(items):
        g.remote_dma_fused([RemoteDMATransfer(dst_ids=[dst(topo, T.cores[d])], dma_engine_mask=bits(es), remote_sem=T.sem[sem], src=a, dst=b)
                            for d, es, sem, a, b in items], local_sem=T.sem.sent)
        sent[0] += sum(len(p[1]) for p in items)

    def plane(k, i, es):
        n, a, w, base = lot(k, i)
        a, at = a - wide(k, h)[0], base + w * peers_of(T, topo, ps[i]).index(r)
        return ps[i], es, "ar_s%d" % k, T["hs%d" % k][:, a:a + w], T[LAND[k][0] + "s"][:, at:at + w]
    if h < 2:
        d = [d for d in ps[2 * h:2 * h + 2] if topo.die(T.cores[d]) != topo.die(core)][0]
        at = 24 * peers_of(T, topo, d).index(r)
        g.wait_ge(T.sem.ar_hp, len(rest) // 2)
        call([(d, off, "ar_pd", T.hp[:], T.pin[:, at:at + 24])])
    for k in range(1, 5):
        g.wait_ge(T.sem["ar_h%d" % k], len(rest) // (1 if h == 2 else 2))
        call([plane(k, 2 * h + j, es) for j, es in enumerate(parts(off, 2))] + ([plane(k, NP - 1, rest)] if h == 2 and k == 1 else []))
        if h < 2 or k == 1:
            s = [s for s in ps[:NP - 1] if far_helper(T, topo, s, h) == core][0]
            g.wait_ge(T.sem["ar_g%d" % k], len(off) // (1 if h == 2 else 2))
            items = []
            w, base = lot(k, 0)[2:]
            for d, es in zip((r, ps[-1]), parts(off + rest, 2)):
                a, at = 0 if w == M else w * (peers_of(T, topo, s).index(d) % 2), base + w * peers_of(T, topo, d).index(s)
                items.append((d, es, "ar_c%d" % k, T["hc%d" % k][:, a:a + w].bitcast(dt.uint8),
                              T[LAND[k][0] + "q"][:, at:at + w].bitcast(dt.uint8)))
            call(items)
    g.wait_ge(T.sem.sent, sent[0])


def rank_program(g, core, T, topo):
    r = T.rank_of(core)
    if r is None:
        for s in range(len(T.cores)):
            hs = helpers_of(T, topo, s)
            if core in hs:
                helper_program(g, core, T, topo, s, hs.index(core))
        return
    ps = peers_of(T, topo, r)
    hs = helpers_of(T, topo, r)
    Q = {"v": g.vector, "s": g.scalar, "t": g.tensor, "g": g, "y": g.sync}
    cnt = {"v": 0, "s": 0, "t": 0, "g": 0}
    seen = {k: {} for k in Q}
    log = {}
    total = {}
    sent = [0]
    ops = []
    calls = []

    def A(name, a=0, b=None, step=1):
        if name in SMALL:
            at, n = SMALL[name]
            return ("sm", at + a, at + (n if b is None else b), step)
        if name == "iot":
            return ("ct", IOT + a, IOT + (C if b is None else b), step)
        return (name, a, SCRATCH[name][1][1] if b is None else b, step)

    def ap(v):
        return T[v[0]][:, v[1]:v[2]] if v[3] == 1 else T[v[0]][:, v[1]:v[2]:v[3]]

    def size(v):
        return len(range(v[1], v[2], v[3]))

    def before(q, reads, writes):
        w = {}
        for v, wr in [(v, False) for v in reads] + [(v, True) for v in writes]:
            for u, uw, uq, sem, val in log.get(v[0], []):
                psum = v[0][0] == "P"
                if psum and uq == q:
                    continue
                if (uw or wr or psum) and meet(u, v):
                    w[sem] = max(w.get(sem, 0), val)
        for sem, val in w.items():
            if seen[q].get(sem, 0) < val:
                Q[q].wait_ge(T.sem[sem], val)
                seen[q][sem] = val

    def note(q, reads, writes, sem, val):
        for v, wr in [(v, False) for v in reads] + [(v, True) for v in writes]:
            log.setdefault(v[0], []).append((v, wr, q, sem, val))
        total[sem] = max(total.get(sem, 0), val)

    def put(q, reads, writes, issue, dur, lag=0.0, after=()):
        ops.append((q, list(reads), list(writes), issue, dur, lag, dict(after)))
        return len(ops) - 1

    def run(q, reads, writes, call, cycles, more=0.0, after=()):
        def issue():
            before(q, reads, writes)
            cnt[q] += 1
            call().then_inc(T.sem["q_" + q], 1)
            note(q, reads, writes, "q_" + q, cnt[q])
        return put(q, reads, writes, issue, more + CYC * max(64, cycles), after=after)

    def cycles(o, *ins):
        return size(o) * (0.5 if all(SCRATCH[v[0]][2] in (BF, U16) for v in (o,) + ins) else 1)

    def col(x):
        return ([x], ap(x)) if isinstance(x, tuple) else ([], x)

    def src(v, off):
        return ap(v) if off is None else ap(v).indirect(ap(off))

    def cp(o, i, off=None):
        if off:
            return run("v", [i, off], [o], lambda: g.vector.tensor_copy(ap(o), src(i, off)), GATHER * size(o), 0.055)
        return run("v", [i], [o], lambda: g.vector.tensor_copy(ap(o), ap(i)), cycles(o, i))

    def scat(o, off, i, step):
        for a in range(0, size(off), step):
            z = min(a + step, size(off))
            x, y = (off[0], off[1] + a, off[1] + z, 1), (i[0], i[1] + 16 * a, i[1] + 16 * z, 1)
            run("v", [y, x], [o], lambda x=x, y=y: g.vector.tensor_copy(ap(o).indirect(ap(x)), ap(y)), SCATTER * size(y), 0.055)

    def tt(o, a, b, op):
        run("v", [a, b], [o], lambda: g.vector.tensor_tensor(ap(o), ap(a), ap(b), op), size(o) * (1 if a[0][0] == "P" else 2))

    def ts(o, a, s1, op0, s2=None, op1=None):
        (r1, x1), (r2, x2) = col(s1), col(s2)
        if op1 is None:
            run("v", [a] + r1, [o], lambda: g.vector.tensor_scalar(ap(o), ap(a), x1, None, op0), cycles(o, a))
        else:
            run("v", [a] + r1 + r2, [o], lambda: g.vector.tensor_scalar(ap(o), ap(a), x1, x2, op0, op1), cycles(o, a))

    def scan(o, reset, d, op1=Op.add, op0=Op.mult, first=0.0):
        r1, x1 = col(first)
        run("v", [reset, d] + r1, [o], lambda: g.vector.tensor_tensor_scan(ap(o), ap(reset), ap(d), x1, op0, op1), size(o))

    def summed(o, i):
        run("v", [i], [o], lambda: g.vector.tensor_reduce(ap(o), ap(i), AxisListType.X, Op.add), size(i))

    def trn(o, i):
        run("v", [i], [o], lambda: g.vector.transpose(ap(o), ap(i)), size(o))

    def fill(o, x):
        run("v", [], [o], lambda: g.vector.memset(ap(o), x), cycles(o))

    def act(o, i, f=Act.Copy, off=None, bias=None, scale=None):
        kw, rd = {}, [i] + ([off] if off else [])
        for k, x in (("bias", bias), ("scale", scale)):
            if x is not None:
                rr, kw[k] = col(x)
                rd = rd + rr
        run("s", rd, [o], lambda: g.scalar.activation(ap(o), src(i, off), f, **kw), size(o) * (GATHER if off else 1), 0.07 if off else 0.0)

    def iota(o, pat, base, cm=0):
        kw = {} if SCRATCH[o[0]][2] == I32 else {"allow_small_or_imprecise_dtypes": True}
        run("g", [], [o], lambda: g.iota(ap(o), pat, base, cm, **kw), 2 * size(o), 0.14, [(c, CALL) for c in calls[-1:]])

    def quant(qn, sn, a, n, i):
        o, s = A(qn, a, a + n), A(sn, a, a + n)
        run("v", [i], [o, s], lambda: g.vector.quantize_mx(ap(o), ap(s), ap(i)), 1.06 * n, 0.013)

    def mm(o, wn, wsn, a, xn, xsn, b, n, start=True, stop=True):
        w, ws, x, xs = A(wn, a, a + 128), A(wsn, a, a + 128), A(xn, b, b + n), A(xsn, b, b + n)
        run("t", [w, ws, x, xs], [o], lambda: g.tensor.matmul_mx(ap(o), ap(w), ap(ws), ap(x), ap(xs), start, stop), 0.7 * (n + 16),
            after=[(j, ops[j][4]) for j in range(len(ops)) if ops[j][0] == "t"][-1:])

    def pick(qo, so, a, qi, si, wlen, off):
        n = 16 * (off[2] - off[1])
        o, i = A(qo, a, a + n), A(qi, 0, wlen)
        run("v", [i, off], [o], lambda: g.vector.tensor_copy(ap(o).bitcast(dt.uint32), ap(i).bitcast(dt.uint32).indirect(ap(off))),
            GATHER * n, 0.055)
        act(A(so, a, a + n), A(si, 0, wlen), off=off)

    def dmas(sem, items, lag, behind=(), now=False):
        def issue():
            for q, o, i, rd, wr in items:
                before(q, rd + list(behind), wr)
                Q[q].dma_start(o, i).then_inc(T.sem[sem], 16)
            for q, o, i, rd, wr in items:
                note(q, rd, wr, sem, 16 * len(items))
        if now:
            issue()
        put(None if now else items[0][0], sum([p[3] for p in items], list(behind)), sum([p[4] for p in items], []),
            (lambda: None) if now else issue, 0.0 if now else 0.05 * len(items), lag)

    def u8(v):
        return ap(v).bitcast(dt.uint8)

    def call(items, reads):
        def issue():
            before("g", reads, [])
            g.remote_dma_fused([RemoteDMATransfer(dst_ids=[dst(topo, c)], dma_engine_mask=bits(es), remote_sem=T.sem[sem], src=s, dst=d)
                                for c, es, sem, s, d in items], local_sem=T.sem.sent)
            sent[0] += sum(len(p[1]) for p in items)
        calls.append(put("g", reads, [], issue, CALL if calls else CALL + FIRST, after=[(c, ops[c][4]) for c in calls[-1:]]))

    def lands(views, sem, val, *ways):
        put(None, [], views, lambda: note("x", [], views, sem, val), 0.0, after=[(c, ops[c][4] + t) for c, t in zip(calls[::-1], ways)])

    def back(i):
        return peers_of(T, topo, ps[i]).index(r)

    off_chip, rest = engine_sets(T, topo, r)

    def exchange(k, piece=None):
        name, a0, z0 = LAND[k]

        def ends(i, kind):
            n, a, w, base = lot(k, i)
            return A(n % kind, a, a + w), A(name + kind, base + w * back(i), base + w * back(i) + w)

        def far(h, es):
            n, a, w, base = lot(k, 2 * h)
            w = w if w == M else 2 * w
            return far_helper(T, topo, r, h), es, "ar_g%d" % k, u8(A(n % "q", a, a + w)), u8(A("hc%d" % k, 0, w))

        def plane(h):
            a, w = wide(k, h)
            return A(lot(k, 2 * h)[0] % "s", a, a + w)

        def relay(h, es):
            return hs[h], es, "ar_h%d" % k, ap(plane(h)), ap(A("hs%d" % k, 0, wide(k, h)[1]))

        def codes(i, es):
            return (T.cores[ps[i]], es, "ar_c%d" % k) + tuple(u8(v) for v in ends(i, "q"))
        rd = [ends(i, "q")[0] for i in {None: range(NP), 0: range(4), 1: (4, 5), 2: [6]}[piece]] + \
            [plane(h) for h in {None: range(3), 0: range(2), 1: [2], 2: []}[piece]]
        o2, r2, n, m = parts(off_chip, 2), parts(rest, 2), len(off_chip), len(rest)
        if piece in (None, 0):
            call([relay(0, r2[0]), relay(1, r2[1])] + ([relay(2, off_chip)] if k == 1 else []), rd)
            call([far(0, o2[0]), far(1, o2[1])] + ([codes(6, rest)] if k == 1 else []), rd)
        if piece == 0:
            return
        if piece != 2:
            call([codes(4, o2[0]), codes(5, o2[1]), relay(2, rest)] if k > 1 else [far(2, off_chip)], rd)
        if piece == 1:
            return
        ways = ((1.6, 0.0) if k > 1 else ()) + WAY[k]
        if k > 1:
            call([codes(6, rest)], rd)
            call([(T.cores[ps[6]], rest, "ar_s%d" % k) + tuple(ap(v) for v in ends(6, "s"))], [ends(6, "s")[0]])
        lands([A(name + "q", a0, z0)], "ar_c%d" % k, 2 * (n + m) + (n if k > 1 else n + m) + m, *ways)
        lands([A(name + "s", a0, z0)], "ar_s%d" % k, 3 * n + m, *ways)

    def bank(p, b, n):
        return A(p, 512 * b, 512 * b + n)

    def plain(q, o, i, off=None):
        if q == "v":
            cp(o, i, off)
        else:
            act(o, i, off=off)

    OWN = A("pf", 0, 1)
    EXTRA = A("pf", 3, 4)

    def to_table(w, n, a):
        step = M if n % M == 0 else n // 3 if n > 2 * M else n
        for b in range(0, n, step):
            scan(A("m2", a + b, a + b + step), A("keep", 0, step), (w[0], w[1] + b, w[1] + b + step, 1), Op.max, Op.add)
        return A("m2", a + 15, a + n, 16)

    def pair_lists(out, at):
        trn(A("gt", at, at + 512), A("gx", at, at + 512))
        for h in range(2):
            o, i = A(out, 16 * h, 16 * h + 16), A("gt", at + 16 * h, at + 512, 32)
            if out[0] == "f":
                cp(o, i)
            else:
                ts(o, i, 1.0 / LOW, Op.mult, M - (SH + RK * (r + 1)) / LOW, Op.add)

    def forward_lists(out, at, t, wlen):
        for h in range(2):
            cp(A("u2", at // 16 + h, at // 16 + 32, 2), t)
        act(A("gx", at, at + 512), A("uw", 0, wlen), off=A("u2", at // 16, at // 16 + 32))
        pair_lists(out, at)

    def backward_lists(out, at, level):
        for k in range(2):
            act(A("gx", at + 256 * k, at + 256 * k + 256), A("w2", SU0), off=A("pd", 48 * k + 16 * level, 48 * k + 16 * level + 16))
        pair_lists(out, at)

    def gathered(k, name, wlen, lists, dn, d0, dw, slot):
        pq, pp = "pk%d" % k, "ps%d" % k
        for a, b in ((0, 8), (8, 16), (16, 32)):
            pick(pq, pp, 16 * a, name + "q", name + "s", wlen, A(lists, a, b))
        for h in range(2):
            for b in range(4):
                mm(bank("PA", b, M), "eeq", "ees", 128 * b, pq, pp, 128 * h, M, h == 0, False)
        for b in range(4):
            mm(bank("PA", b, M), "eoq", "eos", 128 * b, pq, pp, 256, M, False, False)
            mm(bank("PA", b, M), "eoq", "eos", 128 * b, pq, pp, 384, M, False, True)
            tt(A("xs", 512 * slot + b, 512 * slot + 512, 4), bank("PA", b, M), A(dn, dw * b + d0, dw * b + d0 + M), Op.add)
        quant("xq", "xp", 128 * slot, M, A("xs", 512 * slot, 512 * slot + 512))

    def layer(wn, wsn, slot, out):
        for b in range(4):
            mm(bank("PB", b, M), wn, wsn, 128 * b, "xq", "xp", 128 * slot, M)
            if b % 2:
                act(out(b), bank("PB", b, M), scale=0.03125)
            else:
                ts(out(b), bank("PB", b, M), 0.03125, Op.mult)

    def send(k, win, lists):
        at = 4 * SL * (k - 3)
        for piece, (a, z, to, n) in enumerate(((0, 12, 0, 192), (12, 18, 192, M), (18, 21, 320, M))):
            for b in range(4):
                plain("vs"[b % 2], A("st", at + 64 * a + b, at + 64 * z, 4), win(b), A(lists, a, z))
            quant("sdq%d" % k, "sds%d" % k, to, n, A("st", at + 64 * z - 4 * n, at + 64 * z))
            exchange(k, piece)

    def decode(qn, sn, a, n, out, engines="ssss"):
        for b in range(4):
            mm(bank("PA", b, n), "e1q", "e1s", 128 * b, qn, sn, a, n)
            plain(engines[b], out(b), bank("PA", b, n))

    def line(i, x, even, odd):
        o = A("et", EW * i, EW * i + EW)
        run("g", [A("zt")], [o], lambda: g.affine_select(ap(o), ap(A("zt")), [[-128, 4], [odd - even - 64, 2], [-1, 64]], Op.not_equal,
                                                         x, 3 + even, 4), 2 * EW, 0.18, [(c, CALL) for c in calls[-1:]])

    def constants(qn, i):
        for b in range(4):
            quant(qn + "q", qn + "s", 128 * b, 128, A("et", EW * i + 3 - b, EW * i + 515 - b))

    def tile(name, i):
        return lambda b: A(name, 512 * i + b, 512 * i + 512, 4)

    def flat(name, a, step):
        return lambda b: A(name, a + step * b, a + step * b + M)

    def tables(l):
        a, b, j = "req%d" % l, "rin%d" % l, 2 - l
        val = A("val", 256 * j, 256 * j + 256)
        for x in (256 * j, 256 * j + M):
            scan(A("val", x, x + M), A("pl", M * j, M * j + M), A("es", x, x + M), Op.add, Op.max)
        cp(A("ou", 16 * j, 16 * j + 16), A("pm", 8 * SEG * j + 7, 8 * SEG * j + 128, 8))
        scat(A("w2"), A("ou", 16 * j, 16 * j + 16), val, 8 * l)
        ts(A(a, 0, 21), to_table(A("w2", NE + SL * j, NE + SL * j + SL), SL, 896 + SL * j), EXTRA, Op.subtract)
        soon = list(enumerate(parts(off_chip, 2))) + [(NP - 1, rest)]
        late = [(2 + i, es) for i, es in enumerate(parts(off_chip, 4))]
        for part, sem in ((soon, "ar_r"), (late, "ar_t")):
            call([(T.cores[ps[i]], es, sem + str(l), ap(A(a, 3 * i, 3 * i + 3)), ap(A(b, 3 * back(i), 3 * back(i) + 3))) for i, es in part], [A(a)])
            lands([A(b, 3 * i, 3 * i + 3) for i in range(NP) if back(i) in dict(part)], sem + str(l), sum(len(es) for i, es in part), WAY[sem])
        ts(A("hi", 24 * j, 24 * j + 21), A(a, 0, 21), 13, Op.arith_shift_right)
        ts(A("h%d" % l, 0, 21), A("hi", 24 * j, 24 * j + 21), float(M - M * l), Op.add, 0.0, Op.max)

    def asked(l, a, z):
        ts(A("lo", 24 * (2 - l) + a, 24 * (2 - l) + z), A("rin%d" % l, a, z), LOW - 1, Op.bitwise_and)

    def successors(l):
        x, j = A("x%d" % l, 0, 21), 24 * (2 - l)
        ts(x, A("lo", j, j + 21), float(SL - 1 - RK * (r + 1)), Op.add)
        tt(x, x, A("pu", 0, 21), Op.max)
        cp(A("suu", j, j + 21), x)
        scat(A("w2", NE + NS), A("suu", j, j + 21), A("sud", SL * (2 - l), SL * (3 - l)), 8)

    def coded(place):
        return LOW * (place - M) + SH + RK * (r + 1) + C

    dmas("ld_l", [("ys"[i % 2], T.lvt[16 * i:16 * i + 16, :], T.lv[:], [], [A("lvt")]) for i in range(8)], 1.75, now=True)
    dmas("ld_e", [("y", T.e[:, 0:24], T.pr0[:], [], [A("e", 0, 24)]), ("y", T.e[:, 24:48], T.pr1[:], [], [A("e", 24, 48)])], 2.4, now=True)
    dmas("ld_x", [("y", T.xt[:], T.x[:], [], [A("xt")])], 4.7, now=True)
    dmas("ld_w", [("y", u8(A("wq")), T.wc[:], [], [A("wq")]), ("y", T.wp[:], T.ws[:], [], [A("wp")])], 6.0, now=True)

    fill(A("zt"), 0.0)
    fill(A("ones"), 1.0)
    iota(A("pc", 0, 1), [[0, 1]], 0, 1)
    fill(A("et", 3 * EW), 0.0)
    line(2, 1.0, 0, 0)
    iota(A("nm"), [[0, 9], [1, 16]], 0)
    scan(A("iot"), A("ones"), A("ones"), first=-1.0)
    for k in range(2):
        act(A("w2", SU0 + C * k, SU0 + C * k + C), A("ones"), scale=float(coded(BZ)))
    for name, n, step in (("lrs", 152, 0), ("rt", 32, 16), ("rs", 2 * NP * SEG, SEG), ("rp", 264, 8)):
        fill(A(name), 1.0)
        if step:
            fill(A(name, 0, n, step), 0.0)
    runs, threes = A("lrs", 0, 3 * LSEG), A("lrs", 80, 152)
    fill(A("lrs", 0, 3 * LSEG, LSEG), 0.0)
    fill(A("lrs", 80, 152, 3), 0.0)
    for v in (A("tot", 0, 72), A("loh", 0, None, LSEG), A("oh", 0, 2 * NP * SEG, SEG), A("vi", 16, 57, 40)):
        fill(v, 0.0)
    fill(A("si", 16, 17), 0)
    fill(A("ew", 0, 1), float(RK * (N + 1) + SH))
    fill(A("uw", 0, UM, UM - 1), float(FZ))
    ts(A("pc", 1, 2), A("pc", 0, 1), 15, Op.bitwise_and)
    cp(OWN, A("pc", 1, 2))
    ts(A("pf", 1, 2), A("pc", 1, 2), -1.0, Op.mult, -0.5, Op.add)
    ts(EXTRA, A("pc", 1, 2), float(-BIG), Op.mult, float(15 * BIG + SH), Op.add)
    ts(A("pf", 4, 7), A("iot", 1, 4), -1.0, Op.mult, EXTRA, Op.add)
    ts(A("pf", 7, 8), A("pc", 1, 2), float(-BIG), Op.mult, float(15 * BIG + SH + C), Op.add)
    ts(A("kc", 14, 17), A("iot", 0, 3), float(M), Op.mult, -1.0, Op.add)
    for h in range(2):
        ts(A("kc", h, 2 * NP, 2), A("iot", 0, NP), float(CAP), Op.mult, float(NE - 1 + SL * h), Op.add)
    trn(A("s2"), A("kc"))
    ts(A("pu"), A("iot", 0, 33), 16.0, Op.mult, OWN, Op.add)
    for s in range(N):
        if s < N - 2:
            act(A("ew", 1 + C * s, 1 + C * s + C), A("iot"), Act.Identity, bias=float(RK * (s + 1) + SH))
        else:
            iota(A("ew", 1 + C * s, 1 + C * s + C), [[1, C]], RK * (s + 1) + SH)
    act(A("ma"), A("nm"), Act.Sign, bias=A("pf", 1, 2))
    act(A("keep"), A("ma"), Act.Identity, bias=-15.5 * BIG, scale=16.5 * BIG)
    constants("e1", 2)

    for l in range(3):
        ts(A("loh", LSEG * l + 1, LSEG * l + LSEG), A("lvt"), float(l), Op.is_equal)
        summed(A("tot", l, l + 1), A("loh", LSEG * l + 1, LSEG * l + LSEG))
    trn(A("tt"), A("tot"))
    scan(A("ts"), A("rt"), A("tt"))
    trn(A("tb"), A("ts"))
    scan(A("lc2"), runs, A("loh"))
    ts(A("lc1"), A("loh"), -1.0, Op.add, 1024.0, Op.mult)
    tt(A("lc1"), A("lc1"), A("lc2"), Op.add)
    tt(A("kt", 0, 3), A("kc", 14, 17), A("tot", 0, 3), Op.subtract)
    for l in range(3):
        ts(A("lc3", l, 72, 3), A("lc1", LSEG * l + 1, LSEG * l + LSEG), A("tb", l, l + 1), Op.add, A("kt", l, l + 1), Op.add)
    scan(A("lc3", 72), threes, A("lc3", 0, 72), Op.max)
    cp(A("posu"), A("lc3", 74, 144, 3))
    halves = parts(off_chip, 2)
    same = [i for i in range(4) if topo.die(T.cores[ps[i]]) == topo.die(core)]
    plan = [[(same[0], halves[0], "ar_pa"), (same[1], halves[1], "ar_pa")],
            [(4, halves[0], "ar_pb"), (5, halves[1], "ar_pb"), (NP - 1, rest, "ar_pc")]]
    for j, part in enumerate(plan):
        call([(T.cores[ps[i]], es, sem, ap(A("posu")), ap(A("pin", 24 * back(i), 24 * back(i) + 24))) for i, es, sem in part] +
             [(hs[h], parts(rest, 2)[h], "ar_hp", ap(A("posu")), ap(A("hp"))) for h in range(2 - 2 * j)], [A("posu")])
    PSEM = [("ar_pa" if topo.die(T.cores[ps[i]]) == topo.die(core) else "ar_pd") if back(i) < 4 else "ar_pb" if back(i) < 6 else "ar_pc"
            for i in range(NP)]
    turn = sorted(range(NP), key=lambda i: ("cabd".index(PSEM[i][-1]), i))
    for i in turn:
        lands([A("pin", 24 * i, 24 * i + 24)], PSEM[i], len(off_chip) * (2 if PSEM[i] == "ar_pd" else 1), WAY[PSEM[i]])
    iota(A("io2"), [[FL1, 3], [1, M]], 0)
    scat(A("pw", 0, C), A("posu"), A("ew", 1, 1 + C), 24)
    ts(A("permu", 0, 8), to_table(A("pw", 0, M), M, 0), EXTRA, Op.subtract, float(-RK), Op.add)
    ts(A("permu", 8, 24), to_table(A("pw", M, C), C - M, M), EXTRA, Op.subtract, float(-RK), Op.add)

    for a in range(0, C, M):
        quant("sq", "ss", a, M, A("xt", 4 * a, 4 * a + 4 * M))
    pick("spq", "sps", 0, "sq", "ss", C, A("permu", 0, 8))
    decode("spq", "sps", 0, M, tile("xs", 6), "vsvs")
    quant("xq", "xp", 128 * 6, M, A("xs", 512 * 6, 512 * 7))
    layer("wq", "wp", 6, tile("ti", 0))
    quant("swq1", "sws1", 0, M, A("ti", 0, 512))
    exchange(1)
    quant("wfq", "wfs", FY, M, A("ti", 0, 512))
    iota(A("pl", 0, M), [[LOW, M]], LOW * M)
    iota(A("w2", NE, NE + SL), [[0, SL]], SH)
    line(1, -0.5, 0, 1024)
    line(0, -0.5, 1024, 0)
    constants("ee", 1)
    constants("eo", 0)
    quant("wfq", "wfs", FZ, M, A("zt"))

    ts(A("u1"), A("e"), 1.0, Op.add)
    for a in range(0, 48, 12):
        act(A("eexp", 16 * a, 16 * a + 192), A("ew"), off=A("u1", a, a + 12))
    for j in range(2):
        l = 2 - j
        for k in range(2):
            a = 16 * j + 8 * k
            ts(A("pn", a, a + 8), A("m2", M * l + 15, M * l + M, 16), EXTRA, Op.subtract, float(-RK), Op.add)
            act(A("es", 16 * a, 16 * a + M), A("eexp", C * k, C * k + C), Act.Identity, off=A("pn", a, a + 8), bias=float(C * k + 1))
        t = to_table(A("es", 256 * j, 256 * j + 256), 256, C + 256 * j)
        ts(A("si", SEG * j, SEG * j + 16), t, A("pf", 7, 8), Op.subtract, 1.0 / RK, Op.mult)
        ts(A("vi", SEG * j, SEG * j + 16), t, EXTRA, Op.subtract, float(SU0 - 1 - RK * (r + 1)), Op.add)
        for k in range(2):
            a = C + 256 * j + M * k
            ts(A("vn", SEG * j + 8 * k, SEG * j + 8 * k + 8), A("m2", a + 15, a + M, 16), EXTRA, Op.subtract, float(-C - C * k), Op.add)
    ts(A("pv"), A("si"), float(C - RK), Op.mult)
    tt(A("n1"), A("vn"), A("pv"), Op.add)

    for i in [NP] + turn:
        s, off = (r, A("posu")) if i == NP else (ps[i], A("pin", 24 * i, 24 * i + 24))
        act(A("uw", 1 + C * s, 1 + C * s + C), A("iot" if i == NP else "io2"), Act.Identity, off=off, bias=float(M * i))
    forward_lists("f1", 0, A("n1", SEG, 33), UM)

    W = 2 * SEG
    for i in range(NP):
        ts(A("oh", W * i + 1, W * i + W), A("si"), float(ps[i] + 1), Op.is_equal)
    scan(A("ct", 0, NP * W), A("rs"), A("oh", 0, NP * W))
    trn(A("t2"), A("ct", SEG - 1, 32 * SEG, SEG))
    for h in (0, 16):
        scan(A("s2", h + 1, h + 16), A("ones", 0, 15), A("t2", h, h + 15), first=A("s2", h, h + 1))
    trn(A("oh", 0, None, SEG), A("s2"))
    scan(A("c2"), A("rs"), A("oh", 0, NP * W))
    for i in range(NP):
        tt(A("prod", i, None, 8), A("oh", W * i + 1, W * i + W), A("c2", W * i + 1, W * i + W), Op.mult)
    ts(A("on"), A("si"), float(r + 1), Op.is_equal)
    tt(A("vi"), A("vi"), A("on"), Op.mult)
    tt(A("prod", 7, None, 8), A("vi"), A("pu"), Op.max)
    scan(A("pm"), A("rp"), A("prod"), Op.max)
    tables(2)
    iota(A("w2", NE + SL, NE + NS), [[0, SL]], SH)
    dmas("ld_v", [("y", u8(A("vq")), T.vc[:], [], [A("vq")]), ("y", T.vp[:], T.vs[:], [], [A("vp")])], 4.0, [A("f1")])

    pick("spq", "sps", M, "sq", "ss", C, A("permu", 8, 16))
    decode("spq", "sps", M, M, flat("ds", 0, 256))
    gathered(1, "wf", FL2, "f1", "ds", 0, 256, 0)
    layer("wq", "wp", 0, tile("ti", 1))
    quant("swq2", "sws2", 0, M, A("ti", 512, 1024))
    exchange(2, 0)
    for k in range(2):
        act(A("pp", C * k, C * k + C), A("uw", 1 + C * r, 1 + C * r + C), Act.Identity, bias=float(SH - 4 * M * NP), scale=4.0)
    asked(2, 12, 21)
    ts(A("c2u", 12, 21), A("lo", 12, 21), float(-1 - RK * (r + 1)), Op.add, 0.0, Op.max)
    act(A("pw", C), A("pp"), off=A("c2u", 12, 21))
    t = to_table(A("pw", C), 144, 1568)
    act(A("st", 8 * SL, 8 * SL + 384), A("zt", 0, 384))
    for b in range(4):
        ts(A("g2", 10 * b, 10 * b + 9), t, A("pf", 3 + b, 4 + b), Op.subtract, float(8 * M - 4 + b), Op.min)
    for piece, a, z, to, n in ((1, 0, 6, M, 192), (2, 6, 9, 320, M)):
        at = 8 * SL + 384
        for b in range(4):
            plain("vs"[b % 2], A("st", at + 64 * a + b, at + 64 * z, 4), A("ti", 0, 1024), A("g2", 10 * b + a, 10 * b + z))
        quant("sdq2", "sds2", to, n, A("st", at + 64 * z - 4 * n, at + 64 * z))
        exchange(2, piece)
    quant("wfq", "wfs", FY + M, M, A("ti", 512, 1024))
    iota(A("sud", SL, NS), [[LOW, SL]], coded(BL4))

    act(A("uw", UM), A("iot", 0, SL), Act.Identity, bias=float(FL2))
    a1, a2, a3, a4 = [A("a%d" % i, 0, 16) for i in range(1, 5)]
    by_slot = [A("oh", W * i + 1, W * i + SEG) for i in range(NP) if back(i) >= WHOLE]
    tt(a1, by_slot[0], by_slot[1], Op.add)
    tt(a1, a1, by_slot[2], Op.add)
    ts(a2, A("n1", 0, 16), -1.0, Op.mult, float(UM - NE), Op.add)
    tt(a3, a2, A("pm", 7, 128, 8), Op.add)
    tt(a3, a3, a1, Op.mult)
    tt(a4, a3, A("n1", 0, 16), Op.add)
    forward_lists("f2", 512, a4, UM + SL)
    for k in range(2):
        for h in range(2):
            ts(A("pd", 48 * k + h, 48 * k + 48, 2), A("permu"), float(C * k), Op.add)
    act(A("pl", M), A("iot", 0, M), scale=float(LOW))
    act(A("sud", 0, SL), A("iot", 0, SL), Act.Identity, bias=float(coded(BL3)), scale=float(LOW))
    tables(1)
    asked(2, 0, 12)
    successors(2)
    backward_lists("b1", 0, 1)

    pick("spq", "sps", 2 * M, "sq", "ss", C, A("permu", 16, 24))
    decode("spq", "sps", 2 * M, M, flat("ds", M, 256))
    gathered(2, "wf", FW, "f2", "ds", 128, 256, 1)
    layer("wq", "wp", 1, tile("xs", 2))
    quant("xq", "xp", 256, M, A("xs", 1024, 1536))
    decode("xq", "xp", 256, M, tile("xs", 3), "vsvs")
    quant("xq", "xp", 384, M, A("xs", 1536, 2048))
    layer("vq", "vp", 3, flat("zp", 0, M))
    send(3, flat("zp", 0, M), "h2")
    for b in range(4):
        act(tile("ti", 2)(b), flat("zp", 0, M)(b))
    decode("wfq", "wfs", FY, 256, lambda b: A("dy", 256 * b, 256 * b + 256))
    quant("wbq", "wbs", BZ, M, A("zt"))
    quant("wbq", "wbs", 2 * M, M, A("ti", 1024, 1536))

    gathered(3, "wb", BL4, "b1", "dy", M, 256, 4)
    layer("vq", "vp", 4, flat("zp", 512, M))
    send(4, flat("zp", 512, M), "h1")
    dmas("ld_u", [("y", T.ut[:], T.u[:], [], [A("ut")])], 3.0, [A("pk3", 0, M)])
    asked(1, 0, 21)
    successors(1)
    backward_lists("b0", 512, 0)
    for b in range(4):
        act(tile("ti", 3)(b), flat("zp", 512, M)(b))
    quant("wbq", "wbs", M, M, A("ti", 1536, 2048))
    quant("uq", "us", 0, 128, A("ut"))
    mm(bank("PB", 0, 256), "uq", "us", 0, "wbq", "wbs", M, 256)
    act(A("ys", M, C), bank("PB", 0, 256))

    gathered(4, "wb", BW, "b0", "dy", 0, 256, 5)
    layer("vq", "vp", 5, tile("ti", 4))
    quant("wbq", "wbs", 0, M, A("ti", 2048, 2560))
    mm(bank("PA", 0, M), "uq", "us", 0, "wbq", "wbs", 0, M)
    pick("oq", "opl", 0, "wbq", "wbs", C, A("posu"))
    act(A("ys", 0, M), bank("PA", 0, M))
    dmas("st_c", [("y", T.oc[:], u8(A("oq")), [A("oq")], [])], 2.4)
    dmas("st_s", [("sy"[k % 2], T.osc[4 * k:4 * k + 4, :], T.opl[32 * k:32 * k + 4, :], [A("opl")], []) for k in range(4)], 1.5)
    for h in range(2):
        plain("vs"[h], A("yo", 192 * h, 192 * h + 192), A("ys"), A("posu", 12 * h, 12 * h + 12))
    dmas("st_y", [("y", T.y[:], T.yo[:], [A("yo")], [])], 2.4)

    pre = needs(ops)
    at = {j: i for i, j in enumerate(ORDER)}
    assert len(at) == len(ops) and all(at[i] < at[j] for j in range(len(ops)) for i in pre[j])
    for j in ORDER:
        ops[j][3]()
    g.wait_ge(T.sem.sent, sent[0])
    for sem, val in total.items():
        g.wait_ge(T.sem[sem], val)
